import numpy as np
import ml_dtypes


def mxq(x, axis, fmt="e4m3"):
    dtype, down = {"e4m3": (ml_dtypes.float8_e4m3fn, 7), "e5m2": (ml_dtypes.float8_e5m2, 14)}[fmt]
    v = np.moveaxis(np.asarray(x, np.float32).astype(ml_dtypes.bfloat16).astype(np.float64), axis, -1)
    blocks = v.reshape(v.shape[:-1] + (-1, 32))
    amax = np.abs(blocks).max(-1, keepdims=True)
    byte = np.maximum(np.where(amax > 0, np.frexp(amax)[1] - 1 + 127, 0) - down, 1)
    scale = np.exp2(byte - 127.0)
    codes = (blocks / scale).astype(np.float32).astype(dtype).astype(np.float64)
    return np.moveaxis((codes * scale).reshape(v.shape), -1, axis)


WIDE = False


def mx_kscale(k):
    if not WIDE:
        return np.ones(k)
    levels = np.array([10, -10, 5, -5, 0])
    if k % 512:
        return np.exp2(np.random.permutation(np.resize(levels, k // 32))).repeat(32)
    a = np.empty((k // 512, 16))
    for p in range(k // 512):
        a[p, :8] = np.random.permutation(np.resize(levels, 8))
        for g in range(8):
            far = levels[np.abs(levels - a[p, g]) >= 10]
            a[p, g + 8] = far[np.random.randint(len(far))]
    return np.exp2(a.ravel()).repeat(32)


def f64(x):
    return np.asarray(x).astype(np.float64)


def striped(idx):
    return np.tile(idx.reshape(-1, 16).T, (8, 1)).astype(np.uint16)


def unstriped(offs):
    return offs[:16].T.reshape(-1).astype(np.int64)


E2M1 = np.array([0.0, 0.5, 1.0, 1.5, 2.0, 3.0, 4.0, 6.0, -0.0, -0.5, -1.0, -1.5, -2.0, -3.0, -4.0, -6.0])


def pack_weight(w, fmt):
    k, n = w.shape
    w = f64(np.asarray(w, np.float32).astype(ml_dtypes.bfloat16)).reshape(k // 32, 32, n)
    amax = np.abs(w).max(1)
    if fmt == "e4m3":
        byte = np.frexp(amax)[1] - 1 + 127 - 7
    else:
        mant, ex = np.frexp(amax / 6.0)
        byte = np.where(mant > 0.5, ex, ex - 1) + 127
    byte = np.clip(np.where(amax > 0, byte, 1), 1, 254)
    scaled = (w * np.exp2(127.0 - byte)[:, None, :]).reshape(k, n).astype(np.float32)
    by_word = np.ascontiguousarray(scaled.reshape(k // 512, 128, 4, n).transpose(0, 1, 3, 2))
    if fmt == "e4m3":
        words = by_word.astype(ml_dtypes.float8_e4m3fn).view(np.uint8)
    else:
        c = by_word.astype(ml_dtypes.float4_e2m1fn).view(np.uint8) & 0xF
        words = (c[..., 0::2] | (c[..., 1::2] << 4)).reshape(k // 512, 128, 2 * n)
    return np.ascontiguousarray(words), np.ascontiguousarray(byte.astype(np.uint8).reshape(k // 512, 16, n))


def unpack_weight(words, scales, fmt):
    g, _, n = scales.shape
    words = np.ascontiguousarray(words).reshape(g, 128, n, -1)
    if fmt == "e4m3":
        vals = words.view(ml_dtypes.float8_e4m3fn).astype(np.float64)
    else:
        nib = np.empty((g, 128, n, 4), np.uint8)
        nib[..., 0::2] = words & 0xF
        nib[..., 1::2] = words >> 4
        vals = E2M1[nib]
    vals = vals * np.repeat(np.exp2(scales.astype(np.float64) - 127.0), 8, axis=1)[..., None]
    return vals.transpose(0, 1, 3, 2).reshape(g * 512, n)


def gelu(v):
    return 0.5 * v * (1.0 + np.tanh(np.sqrt(2.0 / np.pi) * (v + 0.044715 * v**3)))


K, H, N, T, S = 1024, 1024, 512, 2048, 1024

def setup_inputs():
    n = np.random.standard_normal
    s = mx_kscale(K)[:, None]
    u = mx_kscale(H)[:, None]
    tab_words, tab_scales = pack_weight(n((K, T)) * s, "e4m3")
    wf_words, wf_scales = pack_weight(n((K, H)) / np.sqrt(K) / s, "e2m1")
    wg = (n((K, H)) / np.sqrt(K) / s).astype(np.float32)
    gain = (np.exp(0.3 * n(H)) * u[:, 0]).astype(np.float32)
    wo_words, wo_scales = pack_weight(2.0 * n((H, N)) / np.sqrt(H) / u, "e4m3")
    bo = (0.5 * n(N)).astype(np.float32)
    offs = striped(np.random.permutation(T)[:S])
    return {"tab_words": tab_words, "tab_scales": tab_scales, "offs": offs,
            "wf_words": wf_words, "wf_scales": wf_scales, "wg": wg, "gain": gain,
            "wo_words": wo_words, "wo_scales": wo_scales, "bo": bo}

def reference(tab_words, tab_scales, offs, wf_words, wf_scales, wg, gain, wo_words, wo_scales, bo):
    v = unpack_weight(tab_words, tab_scales, "e4m3")[:, unstriped(offs)]
    wf = unpack_weight(wf_words, wf_scales, "e2m1")
    wo = unpack_weight(wo_words, wo_scales, "e4m3")
    wgq = mxq(f64(wg), 0, "e4m3")
    f = wf.T @ v
    g = wgq.T @ v
    gate = 1.0 / (1.0 + np.exp(-g))
    h = f64(gain)[:, None] * (np.tanh(f) * gate)
    hq = mxq(h, 0, "e4m3")
    y = wo.T @ hq
    return y + f64(bo)[:, None]

@@ -1,0 +1,260 @@
+from contextlib import ExitStack
+
+import concourse.mybir as mybir
+
+K, H, N, T, S = 1024, 1024, 512, 2048, 1024
+FLOPS = 2 * S * (2 * K * H + H * N)
+
+F32 = mybir.dt.float32
+BF16 = mybir.dt.bfloat16
+I32 = mybir.dt.int32
+U32 = mybir.dt.uint32
+U16 = mybir.dt.uint16
+U8 = mybir.dt.uint8
+FP8X4 = mybir.dt.float8_e4m3fn_x4
+FP4X4 = mybir.dt.float4_e2m1fn_x4
+ACT = mybir.ActivationFunctionType
+MULT = mybir.AluOpType.mult
+ADD = mybir.AluOpType.add
+
+P = 128
+PACK = 4
+KP = P * PACK
+HALF = 512
+AL = 64
+
+
+def tile_list_unit_vocoder_gate_kernel(
+    tc, tab_words, tab_scales, offs, wf_words, wf_scales, wg, gain, wo_words, wo_scales, bo, out
+):
+    nc = tc.nc
+    with ExitStack() as ctx:
+        keep = ctx.enter_context(tc.tile_pool(name="keep", bufs=1))
+        work = ctx.enter_context(tc.tile_pool(name="work", bufs=2))
+        psum = ctx.enter_context(tc.psum_pool(name="psum", bufs=4))
+
+        def kept(shape, dtype, name):
+            return keep.tile(shape, dtype, name=name, align_bytes=AL)
+
+        offsets = keep.tile([P, S // 16], U16, name="offsets")
+        nc.sync.dma_start(offsets[:], offs)
+
+        tab_sc = kept([P, T // 4], I32, "tab_sc")
+        wf_sc_raw = kept([P, 2, H // 4], I32, "wf_sc_raw")
+        wo_sc = kept([P, 2, N // 4], I32, "wo_sc")
+        v_sc1 = kept([P, S // 4], I32, "v_sc1")
+        nc.vector.memset(tab_sc[:], 0)
+        nc.vector.memset(wf_sc_raw[:], 0)
+        nc.vector.memset(v_sc1[:], 0)
+        nc.vector.memset(wo_sc[:], 0)
+
+        tab = [kept([P, T], I32, f"tab{a}") for a in range(2)]
+        wf_raw = [kept([P, 2, KP // 2], I32, f"wf_raw{b}") for b in range(2)]
+        wg_raw = {(b, a): kept([P, PACK, KP], F32, f"wg_raw{b}{a}") for b in range(2) for a in range(2)}
+        wo_w = kept([P, 2, N], I32, "wo_w")
+        gain_sb = kept([P, 2, PACK], F32, "gain_sb")
+        bo_sb = kept([P, N // P], F32, "bo_sb")
+
+        def load_tab(a):
+            nc.sync.dma_start(tab[a][:], tab_words[a].rearrange("p n i -> p (n i)").bitcast(I32))
+
+        def load_wf(b):
+            src = wf_words.bitcast(I32).rearrange("a p c -> p a c")
+            nc.sync.dma_start(wf_raw[b][:], src[:, :, b * (KP // 2) : (b + 1) * (KP // 2)])
+
+        def load_wg(b, a):
+            src = wg[a * KP : (a + 1) * KP, b * KP : (b + 1) * KP]
+            nc.sync.dma_start(wg_raw[b, a][:], src.rearrange("(p j) c -> p j c", j=PACK))
+
+        def load_plane(plane, scales):
+            for q in range(4):
+                src = scales.bitcast(I32)[:, 4 * q : 4 * q + 4, :].rearrange("a r c -> r a c")
+                nc.gpsimd.dma_start(plane[32 * q : 32 * q + 4, :, :], src)
+
+        load_tab(0)
+        for q in range(4):
+            nc.scalar.dma_start(tab_sc[32 * q : 32 * q + 8, :], tab_scales.bitcast(I32)[:, 4 * q : 4 * q + 4, :])
+        load_wf(0)
+        load_tab(1)
+        load_plane(wf_sc_raw, wf_scales)
+        load_wg(0, 0)
+        load_wg(0, 1)
+
+        warm = kept([P, 1], F32, "warm")
+        warm_out = kept([P, 1], F32, "warm_out")
+        nc.vector.memset(warm[:], 0.0)
+        nc.scalar.activation(warm_out[:], warm[:], ACT.Sigmoid)
+
+        v_w = {(a, s): kept([P, HALF], U32, f"v_w{a}{s}") for a in range(2) for s in range(2)}
+        v_sc = kept([P, S], U8, "v_sc")
+        wf_w = [kept([P, 2, 2 * KP], U8, f"wf_w{b}") for b in range(2)]
+        wf_sc = [kept([P, 2, KP], U8, f"wf_sc{b}") for b in range(2)]
+        wg_w = {(b, a): kept([P, KP], U32, f"wg_w{b}{a}") for b in range(2) for a in range(2)}
+        wg_sc = {(b, a): kept([P, KP], U8, f"wg_sc{b}{a}") for b in range(2) for a in range(2)}
+        h_w = {(b, s): kept([P, HALF], U32, f"h_w{b}{s}") for b in range(2) for s in range(2)}
+        h_sc = {(b, s): kept([P, HALF], U8, f"h_sc{b}{s}") for b in range(2) for s in range(2)}
+
+        def gather_words(a, s):
+            cols = slice(s * HALF // 16, (s + 1) * HALF // 16)
+            nc.vector.tensor_copy(v_w[a, s][:], tab[a][:].bitcast(U32).indirect(offsets[:, cols]))
+
+        def gather_scales():
+            nc.vector.tensor_copy(v_sc[:], tab_sc[:].bitcast(U8).indirect(offsets[:]))
+            for q in range(4):
+                nc.scalar.dma_start(v_sc1[32 * q : 32 * q + 4, :], v_sc[:].bitcast(I32)[32 * q + 4 : 32 * q + 8, :])
+
+        def v_plane(a, cols):
+            return v_sc[:, cols] if a == 0 else v_sc1[:].bitcast(U8)[:, cols]
+
+        def permute_wf(b):
+            for a in range(2):
+                nc.vector.tensor_copy(
+                    wf_w[b][:, a, :].bitcast(U16).rearrange("p (t m i) -> p m t i", t=PACK, i=4),
+                    wf_raw[b][:, a, :].bitcast(U16).rearrange("p (m i t) -> p m t i", t=PACK, i=4),
+                )
+                src = wf_sc_raw[:, a, :].bitcast(U8)[:, b * KP : (b + 1) * KP]
+                nc.vector.tensor_copy(
+                    wf_sc[b][:, a, :].rearrange("p (t m i) -> p m t i", t=PACK, i=8),
+                    src.rearrange("p (m i t) -> p m t i", t=PACK, i=8),
+                )
+
+        wg_bf = {}
+
+        def cast_wg(b, a, on_scalar):
+            wg_bf[b, a] = work.tile([P, PACK * KP], BF16, name="wg_bf", align_bytes=AL)
+            dst = wg_bf[b, a][:].rearrange("p (t m j) -> p m t j", t=PACK, j=PACK)
+            src = wg_raw[b, a][:].rearrange("p j (m t) -> p m t j", t=PACK)
+            if on_scalar:
+                nc.scalar.copy(dst, src)
+            else:
+                nc.vector.tensor_copy(dst, src)
+
+        def quant_wg(b, a):
+            nc.vector.quantize_mx(out=wg_w[b, a][:].bitcast(FP8X4), scales=wg_sc[b, a][:], in_=wg_bf[b, a][:])
+
+        tanh_f = {}
+        sig_g = {}
+
+        def mm_f(bank, b, s, t, a):
+            nc.tensor.matmul_mx(
+                out=bank[:],
+                lhsT=wf_w[b][:, a, 2 * P * t : 2 * P * (t + 1)].bitcast(FP4X4),
+                lhsT_scale=wf_sc[b][:, a, P * t : P * (t + 1)],
+                rhs=v_w[a, s][:].bitcast(FP8X4),
+                rhs_scale=v_plane(a, slice(s * HALF, (s + 1) * HALF)),
+                start=(a == 0),
+                stop=(a == 1),
+            )
+
+        def filt(b, s, by_pass=False):
+            banks = [psum.tile([P, HALF], F32, name="fg") for t in range(PACK)]
+            order = [(t, a) for a in range(2) for t in range(PACK)] if by_pass else [(t, a) for t in range(PACK) for a in range(2)]
+            for t, a in order:
+                mm_f(banks[t], b, s, t, a)
+                if a == 1:
+                    tanh_f[b, s, t] = work.tile([P, HALF], F32, name="tanh_f", bufs=16)
+                    nc.scalar.activation(tanh_f[b, s, t][:], banks[t][:], ACT.Tanh)
+
+        h_planes = {}
+
+        def gate(b, s, c0, w):
+            planes = work.tile([P, PACK, w], BF16, name="h_planes", align_bytes=AL)
+            h_planes[b, s, c0] = planes
+            for t in range(PACK):
+                bank = psum.tile([P, w], F32, name="fg")
+                for a in range(2):
+                    nc.tensor.matmul_mx(
+                        out=bank[:],
+                        lhsT=wg_w[b, a][:, P * t : P * (t + 1)].bitcast(FP8X4),
+                        lhsT_scale=wg_sc[b, a][:, P * t : P * (t + 1)],
+                        rhs=v_w[a, s][:, c0 : c0 + w].bitcast(FP8X4),
+                        rhs_scale=v_plane(a, slice(s * HALF + c0, s * HALF + c0 + w)),
+                        start=(a == 0),
+                        stop=(a == 1),
+                    )
+                sig = work.tile([P, w], F32, name="sig", bufs=8)
+                nc.scalar.activation(sig[:], bank[:], ACT.Sigmoid)
+                nc.vector.scalar_tensor_tensor(
+                    planes[:, t, :], tanh_f[b, s, t][:, c0 : c0 + w], gain_sb[:, b, t : t + 1], sig[:], MULT, MULT
+                )
+
+        h_il = {}
+
+        def interleave_h(b, s, c0, w):
+            h_il[b, s, c0] = work.tile([P, PACK * w], BF16, name="h_il", align_bytes=AL)
+            nc.vector.tensor_copy(
+                h_il[b, s, c0][:].rearrange("p (c i t) -> p c t i", t=PACK, i=4),
+                h_planes[b, s, c0][:].rearrange("p t (c i) -> p c t i", i=4),
+            )
+
+        def quant_h(b, s, c0, w):
+            nc.vector.quantize_mx(
+                out=h_w[b, s][:, c0 : c0 + w].bitcast(FP8X4), scales=h_sc[b, s][:, c0 : c0 + w], in_=h_il[b, s, c0][:]
+            )
+
+        def project(s, c0, w, split):
+            for i in range(N // P):
+                bank = psum.tile([P, w], F32, name="y")
+                for b in range(2):
+                    nc.tensor.matmul_mx(
+                        out=bank[:],
+                        lhsT=wo_w[:, b, P * i : P * (i + 1)].bitcast(FP8X4),
+                        lhsT_scale=wo_sc[:, b, :].bitcast(U8)[:, P * i : P * (i + 1)],
+                        rhs=h_w[b, s][:, c0 : c0 + w].bitcast(FP8X4),
+                        rhs_scale=h_sc[b, s][:, c0 : c0 + w],
+                        start=(b == 0),
+                        stop=(b == 1),
+                    )
+                y = work.tile([P, w], F32, name="y_sb", bufs=8)
+                if split and i % 2 == 1:
+                    nc.vector.tensor_scalar(y[:], bank[:], bo_sb[:, i : i + 1], None, ADD)
+                else:
+                    nc.scalar.activation(y[:], bank[:], ACT.Identity, bias=bo_sb[:, i : i + 1])
+                nc.sync.dma_start(out[P * i : P * (i + 1), s * HALF + c0 : s * HALF + c0 + w], y[:])
+
+        gather_scales()
+        gather_words(0, 0)
+        load_wf(1)
+        load_wg(1, 0)
+        load_wg(1, 1)
+        nc.sync.dma_start(wo_w[:], wo_words.rearrange("a p n i -> p a (n i)").bitcast(I32))
+        nc.gpsimd.dma_start(gain_sb[:], gain.rearrange("(b p t) -> p b t", b=2, t=PACK))
+        load_plane(wo_sc, wo_scales)
+        with nc.allow_non_contiguous_dma(reason="one bias value a partition"):
+            nc.gpsimd.dma_start(bo_sb[:], bo.rearrange("(i p) -> p i", p=P))
+
+        permute_wf(0)
+        gather_words(1, 0)
+        filt(0, 0, by_pass=True)
+        gather_words(0, 1)
+        gather_words(1, 1)
+        cast_wg(0, 0, False)
+        filt(0, 1)
+        permute_wf(1)
+        quant_wg(0, 0)
+        cast_wg(0, 1, False)
+        filt(1, 0)
+        quant_wg(0, 1)
+        cast_wg(1, 0, False)
+        gate(0, 0, 0, HALF)
+        quant_wg(1, 0)
+        cast_wg(1, 1, True)
+        interleave_h(0, 0, 0, HALF)
+        gate(0, 1, 0, HALF)
+        quant_h(0, 0, 0, HALF)
+        quant_wg(1, 1)
+        interleave_h(0, 1, 0, HALF)
+        gate(1, 0, 0, HALF)
+        quant_h(0, 1, 0, HALF)
+        filt(1, 1)
+        interleave_h(1, 0, 0, HALF)
+        gate(1, 1, 0, HALF // 2)
+        quant_h(1, 0, 0, HALF)
+        project(0, 0, HALF, False)
+        interleave_h(1, 1, 0, HALF // 2)
+        gate(1, 1, HALF // 2, HALF // 2)
+        quant_h(1, 1, 0, HALF // 2)
+        interleave_h(1, 1, HALF // 2, HALF // 2)
+        project(1, 0, HALF // 2, False)
+        quant_h(1, 1, HALF // 2, HALF // 2)
+        project(1, HALF // 2, HALF // 2, True)

@@ -33,101 +33,101 @@ def tile_list_unit_vocoder_gate_kernel(
         work = ctx.enter_context(tc.tile_pool(name="work", bufs=2))
         psum = ctx.enter_context(tc.psum_pool(name="psum", bufs=4))
 
-        def kept(shape, dtype, name):
-            return keep.tile(shape, dtype, name=name, align_bytes=AL)
+        def kept(shape, dtype, name, tag=""):
+            return keep.tile(shape, dtype, name=name, tag=tag or name, align_bytes=AL)
 
         offsets = keep.tile([P, S // 16], U16, name="offsets")
         nc.sync.dma_start(offsets[:], offs)
 
-        tab_sc = kept([P, T // 4], I32, "tab_sc")
-        wf_sc_raw = kept([P, 2, H // 4], I32, "wf_sc_raw")
-        wo_sc = kept([P, 2, N // 4], I32, "wo_sc")
-        v_sc1 = kept([P, S // 4], I32, "v_sc1")
-        nc.vector.memset(tab_sc[:], 0)
-        nc.vector.memset(wf_sc_raw[:], 0)
-        nc.vector.memset(v_sc1[:], 0)
-        nc.vector.memset(wo_sc[:], 0)
+        tab_sc = kept([P, T // 4], I32, "tab_sc", "slot_a")
+        nc.sync.dma_start(tab_sc[0:32, :], tab_scales.bitcast(I32).rearrange("a q c -> q a c"))
+        nc.vector.memset(tab_sc[32:64, :], 0)
+        nc.vector.memset(tab_sc[64:128, :], 0)
+        wf_sc_raw = kept([P, 2, H // 4], I32, "wf_sc_raw", "slot_s")
+        v_pl = kept([P, 2, S // 4], I32, "v_pl")
+        nc.gpsimd.memset(wf_sc_raw[:], 0)
+        nc.gpsimd.memset(v_pl[:], 0)
+
+        warm = kept([P, 1], F32, "warm")
+        warm_out = kept([P, 1], F32, "warm_out")
+        nc.gpsimd.memset(warm[:], 0.0)
+        nc.scalar.activation(warm_out[:], warm[:], ACT.Sigmoid)
 
         tab = [kept([P, T], I32, f"tab{a}") for a in range(2)]
-        wf_raw = [kept([P, 2, KP // 2], I32, f"wf_raw{b}") for b in range(2)]
-        wg_raw = {(b, a): kept([P, PACK, KP], F32, f"wg_raw{b}{a}") for b in range(2) for a in range(2)}
-        wo_w = kept([P, 2, N], I32, "wo_w")
-        gain_sb = kept([P, 2, PACK], F32, "gain_sb")
-        bo_sb = kept([P, N // P], F32, "bo_sb")
+        wf_raw = {}
+        wg_raw = {}
 
         def load_tab(a):
             nc.sync.dma_start(tab[a][:], tab_words[a].rearrange("p n i -> p (n i)").bitcast(I32))
 
-        def load_wf(b):
+        def load_wf(b, dst):
+            wf_raw[b] = dst
             src = wf_words.bitcast(I32).rearrange("a p c -> p a c")
-            nc.sync.dma_start(wf_raw[b][:], src[:, :, b * (KP // 2) : (b + 1) * (KP // 2)])
+            nc.sync.dma_start(dst, src[:, :, b * (KP // 2) : (b + 1) * (KP // 2)])
 
-        def load_wg(b, a):
+        def load_wg(b, a, dst):
+            wg_raw[b, a] = dst
             src = wg[a * KP : (a + 1) * KP, b * KP : (b + 1) * KP]
-            nc.sync.dma_start(wg_raw[b, a][:], src.rearrange("(p j) c -> p j c", j=PACK))
+            nc.sync.dma_start(dst, src.rearrange("(p j) c -> p j c", j=PACK))
 
         def load_plane(plane, scales):
             for q in range(4):
                 src = scales.bitcast(I32)[:, 4 * q : 4 * q + 4, :].rearrange("a r c -> r a c")
-                nc.gpsimd.dma_start(plane[32 * q : 32 * q + 4, :, :], src)
+                nc.sync.dma_start(plane[32 * q : 32 * q + 4, :, :], src)
 
         load_tab(0)
-        for q in range(4):
-            nc.scalar.dma_start(tab_sc[32 * q : 32 * q + 8, :], tab_scales.bitcast(I32)[:, 4 * q : 4 * q + 4, :])
-        load_wf(0)
-        load_tab(1)
         load_plane(wf_sc_raw, wf_scales)
-        load_wg(0, 0)
-        load_wg(0, 1)
+        load_wf(0, kept([P, 2, KP // 2], I32, "wf_raw0", "slot_f")[:])
+        load_tab(1)
+        gain_sb = kept([P, 2, PACK], F32, "gain_sb")
+        nc.sync.dma_start(gain_sb[:], gain.rearrange("(b p t) -> p b t", b=2, t=PACK))
 
-        warm = kept([P, 1], F32, "warm")
-        warm_out = kept([P, 1], F32, "warm_out")
-        nc.vector.memset(warm[:], 0.0)
-        nc.scalar.activation(warm_out[:], warm[:], ACT.Sigmoid)
-
-        v_w = {(a, s): kept([P, HALF], U32, f"v_w{a}{s}") for a in range(2) for s in range(2)}
+        v_w = {}
         v_sc = kept([P, S], U8, "v_sc")
         wf_w = [kept([P, 2, 2 * KP], U8, f"wf_w{b}") for b in range(2)]
-        wf_sc = [kept([P, 2, KP], U8, f"wf_sc{b}") for b in range(2)]
+        wf_sc = {}
         wg_w = {(b, a): kept([P, KP], U32, f"wg_w{b}{a}") for b in range(2) for a in range(2)}
         wg_sc = {(b, a): kept([P, KP], U8, f"wg_sc{b}{a}") for b in range(2) for a in range(2)}
         h_w = {(b, s): kept([P, HALF], U32, f"h_w{b}{s}") for b in range(2) for s in range(2)}
         h_sc = {(b, s): kept([P, HALF], U8, f"h_sc{b}{s}") for b in range(2) for s in range(2)}
 
-        def gather_words(a, s):
+        def gather_words(a, s, tag=""):
+            v_w[a, s] = kept([P, HALF], U32, f"v_w{a}{s}", tag)
             cols = slice(s * HALF // 16, (s + 1) * HALF // 16)
             nc.vector.tensor_copy(v_w[a, s][:], tab[a][:].bitcast(U32).indirect(offsets[:, cols]))
 
         def gather_scales():
             nc.vector.tensor_copy(v_sc[:], tab_sc[:].bitcast(U8).indirect(offsets[:]))
             for q in range(4):
-                nc.scalar.dma_start(v_sc1[32 * q : 32 * q + 4, :], v_sc[:].bitcast(I32)[32 * q + 4 : 32 * q + 8, :])
+                nc.sync.dma_start(v_pl[32 * q : 32 * q + 4, :, :], v_sc[:].bitcast(I32)[8 * q : 8 * q + 8, :])
 
         def v_plane(a, cols):
-            return v_sc[:, cols] if a == 0 else v_sc1[:].bitcast(U8)[:, cols]
+            return v_pl[:, a, :].bitcast(U8)[:, cols]
 
         def permute_wf(b):
-            for a in range(2):
-                nc.vector.tensor_copy(
-                    wf_w[b][:, a, :].bitcast(U16).rearrange("p (t m i) -> p m t i", t=PACK, i=4),
-                    wf_raw[b][:, a, :].bitcast(U16).rearrange("p (m i t) -> p m t i", t=PACK, i=4),
-                )
-                src = wf_sc_raw[:, a, :].bitcast(U8)[:, b * KP : (b + 1) * KP]
-                nc.vector.tensor_copy(
-                    wf_sc[b][:, a, :].rearrange("p (t m i) -> p m t i", t=PACK, i=8),
-                    src.rearrange("p (m i t) -> p m t i", t=PACK, i=8),
-                )
+            nc.vector.tensor_copy(
+                wf_w[b][:].bitcast(U16).rearrange("p a (t m i) -> p a m t i", t=PACK, i=4),
+                wf_raw[b].bitcast(U16).rearrange("p a (m i t) -> p a m t i", t=PACK, i=4),
+            )
+
+        def permute_wf_scales(b, tag=""):
+            wf_sc[b] = kept([P, 2, KP], U8, f"wf_sc{b}", tag)
+            src = wf_sc_raw[:].bitcast(U8)[:, :, b * KP : (b + 1) * KP]
+            nc.gpsimd.tensor_copy(
+                wf_sc[b][:].rearrange("p a (t m) -> p a t m", t=PACK),
+                src.rearrange("p a (m t) -> p a t m", t=PACK),
+            )
 
         wg_bf = {}
 
-        def cast_wg(b, a, on_scalar):
-            wg_bf[b, a] = work.tile([P, PACK * KP], BF16, name="wg_bf", align_bytes=AL)
+        def cast_wg(b, a, on_vector, tag):
+            wg_bf[b, a] = kept([P, PACK * KP], BF16, f"wg_bf{b}{a}", tag)
             dst = wg_bf[b, a][:].rearrange("p (t m j) -> p m t j", t=PACK, j=PACK)
-            src = wg_raw[b, a][:].rearrange("p j (m t) -> p m t j", t=PACK)
-            if on_scalar:
-                nc.scalar.copy(dst, src)
-            else:
-                nc.vector.tensor_copy(dst, src)
+            src = wg_raw[b, a].rearrange("p j (m t) -> p m t j", t=PACK)
+            if on_vector > 0:
+                nc.vector.tensor_copy(dst[:, :on_vector], src[:, :on_vector])
+            if on_vector < P:
+                nc.scalar.copy(dst[:, on_vector:], src[:, on_vector:])
 
         def quant_wg(b, a):
             nc.vector.quantize_mx(out=wg_w[b, a][:].bitcast(FP8X4), scales=wg_sc[b, a][:], in_=wg_bf[b, a][:])
@@ -157,8 +157,8 @@ def tile_list_unit_vocoder_gate_kernel(
 
         h_planes = {}
 
-        def gate(b, s, c0, w):
-            planes = work.tile([P, PACK, w], BF16, name="h_planes", align_bytes=AL)
+        def gate(b, s, c0, w, tag):
+            planes = kept([P, PACK, w], BF16, f"h_planes{b}{s}{c0}", tag)
             h_planes[b, s, c0] = planes
             for t in range(PACK):
                 bank = psum.tile([P, w], F32, name="fg")
@@ -192,69 +192,88 @@ def tile_list_unit_vocoder_gate_kernel(
                 out=h_w[b, s][:, c0 : c0 + w].bitcast(FP8X4), scales=h_sc[b, s][:, c0 : c0 + w], in_=h_il[b, s, c0][:]
             )
 
-        def project(s, c0, w, split):
+        def mm_y(bank, s, c0, w, i, b):
+            nc.tensor.matmul_mx(
+                out=bank[:],
+                lhsT=wo_w[:, b, P * i : P * (i + 1)].bitcast(FP8X4),
+                lhsT_scale=wo_sc[:, b, :].bitcast(U8)[:, P * i : P * (i + 1)],
+                rhs=h_w[b, s][:, c0 : c0 + w].bitcast(FP8X4),
+                rhs_scale=h_sc[b, s][:, c0 : c0 + w],
+                start=(b == 0),
+                stop=(b == 1),
+            )
+
+        def store_y(bank, s, c0, w, i, on_vector):
+            y = work.tile([P, w], F32, name="y_sb", bufs=8)
+            if on_vector:
+                nc.vector.tensor_scalar(y[:], bank[:], bo_sb[:, i : i + 1], None, ADD)
+            else:
+                nc.scalar.activation(y[:], bank[:], ACT.Identity, bias=bo_sb[:, i : i + 1])
+            nc.sync.dma_start(out[P * i : P * (i + 1), s * HALF + c0 : s * HALF + c0 + w], y[:])
+
+        def project(s, c0, w):
             for i in range(N // P):
                 bank = psum.tile([P, w], F32, name="y")
                 for b in range(2):
-                    nc.tensor.matmul_mx(
-                        out=bank[:],
-                        lhsT=wo_w[:, b, P * i : P * (i + 1)].bitcast(FP8X4),
-                        lhsT_scale=wo_sc[:, b, :].bitcast(U8)[:, P * i : P * (i + 1)],
-                        rhs=h_w[b, s][:, c0 : c0 + w].bitcast(FP8X4),
-                        rhs_scale=h_sc[b, s][:, c0 : c0 + w],
-                        start=(b == 0),
-                        stop=(b == 1),
-                    )
-                y = work.tile([P, w], F32, name="y_sb", bufs=8)
-                if split and i % 2 == 1:
-                    nc.vector.tensor_scalar(y[:], bank[:], bo_sb[:, i : i + 1], None, ADD)
-                else:
-                    nc.scalar.activation(y[:], bank[:], ACT.Identity, bias=bo_sb[:, i : i + 1])
-                nc.sync.dma_start(out[P * i : P * (i + 1), s * HALF + c0 : s * HALF + c0 + w], y[:])
+                    mm_y(bank, s, c0, w, i, b)
+                store_y(bank, s, c0, w, i, False)
 
+        Q = HALF // 2
         gather_scales()
+        wg_b0 = kept([P, 2, PACK, KP], F32, "wg_b0", "slot_a")
+        for a in range(2):
+            load_wg(0, a, wg_b0[:, a, :, :])
+        load_wf(1, kept([P, 2, KP // 2], I32, "wf_raw1", "v_sc")[:])
+        permute_wf_scales(0)
         gather_words(0, 0)
-        load_wf(1)
-        load_wg(1, 0)
-        load_wg(1, 1)
-        nc.sync.dma_start(wo_w[:], wo_words.rearrange("a p n i -> p a (n i)").bitcast(I32))
-        nc.gpsimd.dma_start(gain_sb[:], gain.rearrange("(b p t) -> p b t", b=2, t=PACK))
-        load_plane(wo_sc, wo_scales)
-        with nc.allow_non_contiguous_dma(reason="one bias value a partition"):
-            nc.gpsimd.dma_start(bo_sb[:], bo.rearrange("(i p) -> p i", p=P))
-
         permute_wf(0)
+        permute_wf_scales(1, "slot_f")
         gather_words(1, 0)
         filt(0, 0, by_pass=True)
         gather_words(0, 1)
         gather_words(1, 1)
-        cast_wg(0, 0, False)
-        filt(0, 1)
-        permute_wf(1)
+        load_wg(1, 0, kept([P, PACK, KP], F32, "wg_b10", "tab1")[:])
+        wo_sc = kept([P, 2, N // 4], I32, "wo_sc", "slot_s")
+        nc.gpsimd.memset(wo_sc[:], 0)
+        load_plane(wo_sc, wo_scales)
+        cast_wg(0, 0, P, "bf0")
         quant_wg(0, 0)
-        cast_wg(0, 1, False)
-        filt(1, 0)
+        cast_wg(0, 1, P, "bf1")
+        load_wg(1, 1, kept([P, PACK, KP], F32, "wg_b11", "slot_a")[:])
+        permute_wf(1)
         quant_wg(0, 1)
-        cast_wg(1, 0, False)
-        gate(0, 0, 0, HALF)
+        filt(0, 1)
+        cast_wg(1, 0, P, "bf0")
+        wo_w = kept([P, 2, N], I32, "wo_w", "tab1")
+        nc.sync.dma_start(wo_w[:], wo_words.rearrange("a p n i -> p a (n i)").bitcast(I32))
+        bo_sb = kept([P, N // P], F32, "bo_sb", "v_sc")
+        with nc.allow_non_contiguous_dma(reason="one bias value a partition"):
+            nc.sync.dma_start(bo_sb[:], bo.rearrange("(i p) -> p i", p=P))
+        gate(0, 0, 0, HALF, "hp0")
         quant_wg(1, 0)
-        cast_wg(1, 1, True)
         interleave_h(0, 0, 0, HALF)
-        gate(0, 1, 0, HALF)
+        gate(0, 1, 0, HALF, "hp1")
+        cast_wg(1, 1, 0, "hp0")
         quant_h(0, 0, 0, HALF)
-        quant_wg(1, 1)
+        filt(1, 0)
         interleave_h(0, 1, 0, HALF)
-        gate(1, 0, 0, HALF)
+        quant_wg(1, 1)
         quant_h(0, 1, 0, HALF)
+        gate(1, 0, 0, HALF, "hp1")
         filt(1, 1)
         interleave_h(1, 0, 0, HALF)
-        gate(1, 1, 0, HALF // 2)
+        gate(1, 1, 0, Q, "hp0")
         quant_h(1, 0, 0, HALF)
-        project(0, 0, HALF, False)
-        interleave_h(1, 1, 0, HALF // 2)
-        gate(1, 1, HALF // 2, HALF // 2)
-        quant_h(1, 1, 0, HALF // 2)
-        interleave_h(1, 1, HALF // 2, HALF // 2)
-        project(1, 0, HALF // 2, False)
-        quant_h(1, 1, HALF // 2, HALF // 2)
-        project(1, HALF // 2, HALF // 2, True)
+        project(0, 0, HALF)
+        interleave_h(1, 1, 0, Q)
+        gate(1, 1, Q, Q, "hp1")
+        last = [psum.tile([P, Q], F32, name="fg") for i in range(N // P)]
+        for i in range(N // P):
+            mm_y(last[i], 1, Q, Q, i, 0)
+        quant_h(1, 1, 0, Q)
+        interleave_h(1, 1, Q, Q)
+        project(1, 0, Q)
+        quant_h(1, 1, Q, Q)
+        for i in range(N // P):
+            mm_y(last[i], 1, Q, Q, i, 1)
+            store_y(last[i], 1, Q, Q, i, i % 2 == 1)

@@ -31,7 +31,7 @@ def tile_list_unit_vocoder_gate_kernel(
     with ExitStack() as ctx:
         keep = ctx.enter_context(tc.tile_pool(name="keep", bufs=1))
         work = ctx.enter_context(tc.tile_pool(name="work", bufs=2))
-        psum = ctx.enter_context(tc.psum_pool(name="psum", bufs=4))
+        psum = ctx.enter_context(tc.psum_pool(name="psum", bufs=8))
 
         def kept(shape, dtype, name, tag=""):
             return keep.tile(shape, dtype, name=name, tag=tag or name, align_bytes=AL)
@@ -48,9 +48,11 @@ def tile_list_unit_vocoder_gate_kernel(
         nc.gpsimd.memset(wf_sc_raw[:], 0)
         nc.gpsimd.memset(v_pl[:], 0)
 
-        warm = kept([P, 1], F32, "warm")
+        wo_sc = kept([P, 2, N // 4], I32, "wo_sc")
+        warm = kept([P, 1], F32, "warm", "tab1")
         warm_out = kept([P, 1], F32, "warm_out")
         nc.gpsimd.memset(warm[:], 0.0)
+        nc.gpsimd.memset(wo_sc[:], 0)
         nc.scalar.activation(warm_out[:], warm[:], ACT.Sigmoid)
 
         tab = [kept([P, T], I32, f"tab{a}") for a in range(2)]
@@ -76,16 +78,16 @@ def tile_list_unit_vocoder_gate_kernel(
                 nc.sync.dma_start(plane[32 * q : 32 * q + 4, :, :], src)
 
         load_tab(0)
+        gain_sb = kept([P, 2, PACK], F32, "gain_sb")
+        nc.scalar.dma_start(gain_sb[:], gain.rearrange("(b p t) -> p b t", b=2, t=PACK))
         load_plane(wf_sc_raw, wf_scales)
         load_wf(0, kept([P, 2, KP // 2], I32, "wf_raw0", "slot_f")[:])
         load_tab(1)
-        gain_sb = kept([P, 2, PACK], F32, "gain_sb")
-        nc.sync.dma_start(gain_sb[:], gain.rearrange("(b p t) -> p b t", b=2, t=PACK))
 
         v_w = {}
         v_sc = kept([P, S], U8, "v_sc")
         wf_w = [kept([P, 2, 2 * KP], U8, f"wf_w{b}") for b in range(2)]
-        wf_sc = {}
+        wf_sc = kept([P, 2, H], U8, "wf_sc")
         wg_w = {(b, a): kept([P, KP], U32, f"wg_w{b}{a}") for b in range(2) for a in range(2)}
         wg_sc = {(b, a): kept([P, KP], U8, f"wg_sc{b}{a}") for b in range(2) for a in range(2)}
         h_w = {(b, s): kept([P, HALF], U32, f"h_w{b}{s}") for b in range(2) for s in range(2)}
@@ -110,24 +112,20 @@ def tile_list_unit_vocoder_gate_kernel(
                 wf_raw[b].bitcast(U16).rearrange("p a (m i t) -> p a m t i", t=PACK, i=4),
             )
 
-        def permute_wf_scales(b, tag=""):
-            wf_sc[b] = kept([P, 2, KP], U8, f"wf_sc{b}", tag)
-            src = wf_sc_raw[:].bitcast(U8)[:, :, b * KP : (b + 1) * KP]
-            nc.gpsimd.tensor_copy(
-                wf_sc[b][:].rearrange("p a (t m) -> p a t m", t=PACK),
-                src.rearrange("p a (m t) -> p a t m", t=PACK),
+        def permute_wf_scales():
+            nc.vector.tensor_copy(
+                wf_sc[:].rearrange("p a (b t m i) -> p (a b) m t i", b=2, t=PACK, i=8),
+                wf_sc_raw[:].bitcast(U8).rearrange("p a (b m i t) -> p (a b) m t i", b=2, t=PACK, i=8),
             )
 
         wg_bf = {}
 
-        def cast_wg(b, a, on_vector, tag):
-            wg_bf[b, a] = kept([P, PACK * KP], BF16, f"wg_bf{b}{a}", tag)
+        def cast_wg(b, a, copy, tag, m0=0, m1=P):
+            if m0 == 0:
+                wg_bf[b, a] = kept([P, PACK * KP], BF16, f"wg_bf{b}{a}", tag)
             dst = wg_bf[b, a][:].rearrange("p (t m j) -> p m t j", t=PACK, j=PACK)
             src = wg_raw[b, a].rearrange("p j (m t) -> p m t j", t=PACK)
-            if on_vector > 0:
-                nc.vector.tensor_copy(dst[:, :on_vector], src[:, :on_vector])
-            if on_vector < P:
-                nc.scalar.copy(dst[:, on_vector:], src[:, on_vector:])
+            copy(dst[:, m0:m1], src[:, m0:m1])
 
         def quant_wg(b, a):
             nc.vector.quantize_mx(out=wg_w[b, a][:].bitcast(FP8X4), scales=wg_sc[b, a][:], in_=wg_bf[b, a][:])
@@ -139,21 +137,20 @@ def tile_list_unit_vocoder_gate_kernel(
             nc.tensor.matmul_mx(
                 out=bank[:],
                 lhsT=wf_w[b][:, a, 2 * P * t : 2 * P * (t + 1)].bitcast(FP4X4),
-                lhsT_scale=wf_sc[b][:, a, P * t : P * (t + 1)],
+                lhsT_scale=wf_sc[:, a, KP * b + P * t : KP * b + P * (t + 1)],
                 rhs=v_w[a, s][:].bitcast(FP8X4),
                 rhs_scale=v_plane(a, slice(s * HALF, (s + 1) * HALF)),
                 start=(a == 0),
                 stop=(a == 1),
             )
 
-        def filt(b, s, by_pass=False):
-            banks = [psum.tile([P, HALF], F32, name="fg") for t in range(PACK)]
-            order = [(t, a) for a in range(2) for t in range(PACK)] if by_pass else [(t, a) for t in range(PACK) for a in range(2)]
-            for t, a in order:
-                mm_f(banks[t], b, s, t, a)
-                if a == 1:
-                    tanh_f[b, s, t] = work.tile([P, HALF], F32, name="tanh_f", bufs=16)
-                    nc.scalar.activation(tanh_f[b, s, t][:], banks[t][:], ACT.Tanh)
+        def filt(b, s, tiles=range(PACK)):
+            for t in tiles:
+                bank = psum.tile([P, HALF], F32, name="bank")
+                for a in range(2):
+                    mm_f(bank, b, s, t, a)
+                tanh_f[b, s, t] = work.tile([P, HALF], F32, name="tanh_f", bufs=16)
+                nc.scalar.activation(tanh_f[b, s, t][:], bank[:], ACT.Tanh)
 
         h_planes = {}
 
@@ -161,16 +158,16 @@ def tile_list_unit_vocoder_gate_kernel(
             planes = kept([P, PACK, w], BF16, f"h_planes{b}{s}{c0}", tag)
             h_planes[b, s, c0] = planes
             for t in range(PACK):
-                bank = psum.tile([P, w], F32, name="fg")
-                for a in range(2):
+                bank = psum.tile([P, w], F32, name="bank")
+                for a in (1, 0):
                     nc.tensor.matmul_mx(
                         out=bank[:],
                         lhsT=wg_w[b, a][:, P * t : P * (t + 1)].bitcast(FP8X4),
                         lhsT_scale=wg_sc[b, a][:, P * t : P * (t + 1)],
                         rhs=v_w[a, s][:, c0 : c0 + w].bitcast(FP8X4),
                         rhs_scale=v_plane(a, slice(s * HALF + c0, s * HALF + c0 + w)),
-                        start=(a == 0),
-                        stop=(a == 1),
+                        start=(a == 1),
+                        stop=(a == 0),
                     )
                 sig = work.tile([P, w], F32, name="sig", bufs=8)
                 nc.scalar.activation(sig[:], bank[:], ACT.Sigmoid)
@@ -204,76 +201,74 @@ def tile_list_unit_vocoder_gate_kernel(
             )
 
         def store_y(bank, s, c0, w, i, on_vector):
-            y = work.tile([P, w], F32, name="y_sb", bufs=8)
+            y = work.tile([P, w], F32, name="y_sb", bufs=12)
             if on_vector:
                 nc.vector.tensor_scalar(y[:], bank[:], bo_sb[:, i : i + 1], None, ADD)
             else:
                 nc.scalar.activation(y[:], bank[:], ACT.Identity, bias=bo_sb[:, i : i + 1])
             nc.sync.dma_start(out[P * i : P * (i + 1), s * HALF + c0 : s * HALF + c0 + w], y[:])
 
-        def project(s, c0, w):
-            for i in range(N // P):
-                bank = psum.tile([P, w], F32, name="y")
+        def project(s, c0, w, tiles=range(N // P), on_vector=()):
+            for i in tiles:
+                bank = psum.tile([P, w], F32, name="bank")
                 for b in range(2):
                     mm_y(bank, s, c0, w, i, b)
-                store_y(bank, s, c0, w, i, False)
+                store_y(bank, s, c0, w, i, i in on_vector)
 
         Q = HALF // 2
         gather_scales()
         wg_b0 = kept([P, 2, PACK, KP], F32, "wg_b0", "slot_a")
-        for a in range(2):
-            load_wg(0, a, wg_b0[:, a, :, :])
-        load_wf(1, kept([P, 2, KP // 2], I32, "wf_raw1", "v_sc")[:])
-        permute_wf_scales(0)
+        load_wg(0, 0, wg_b0[:, 0, :, :])
+        load_wf(1, kept([P, 2, KP // 2], I32, "wf_raw1")[:])
+        load_wg(0, 1, wg_b0[:, 1, :, :])
         gather_words(0, 0)
         permute_wf(0)
-        permute_wf_scales(1, "slot_f")
+        permute_wf_scales()
         gather_words(1, 0)
-        filt(0, 0, by_pass=True)
-        gather_words(0, 1)
+        filt(0, 0)
         gather_words(1, 1)
-        load_wg(1, 0, kept([P, PACK, KP], F32, "wg_b10", "tab1")[:])
-        wo_sc = kept([P, 2, N // 4], I32, "wo_sc", "slot_s")
-        nc.gpsimd.memset(wo_sc[:], 0)
-        load_plane(wo_sc, wo_scales)
-        cast_wg(0, 0, P, "bf0")
-        quant_wg(0, 0)
-        cast_wg(0, 1, P, "bf1")
-        load_wg(1, 1, kept([P, PACK, KP], F32, "wg_b11", "slot_a")[:])
-        permute_wf(1)
-        quant_wg(0, 1)
+        gather_words(0, 1, "tab1")
+        for a in range(2):
+            load_wg(1, a, kept([P, PACK, KP], F32, f"wg_b1{a}")[:])
         filt(0, 1)
-        cast_wg(1, 0, P, "bf0")
-        wo_w = kept([P, 2, N], I32, "wo_w", "tab1")
+        cast_wg(0, 0, nc.vector.tensor_copy, "bf0")
+        permute_wf(1)
+        cast_wg(0, 1, nc.vector.tensor_copy, "bf1")
+        wo_w = kept([P, 2, N], I32, "wo_w", "slot_a")
         nc.sync.dma_start(wo_w[:], wo_words.rearrange("a p n i -> p a (n i)").bitcast(I32))
-        bo_sb = kept([P, N // P], F32, "bo_sb", "v_sc")
+        load_plane(wo_sc, wo_scales)
+        quant_wg(0, 0)
+        quant_wg(0, 1)
+        bo_sb = kept([P, N // P], F32, "bo_sb", "wf_raw1")
         with nc.allow_non_contiguous_dma(reason="one bias value a partition"):
             nc.sync.dma_start(bo_sb[:], bo.rearrange("(i p) -> p i", p=P))
+        filt(1, 0, (0, 1))
+        cast_wg(1, 0, nc.vector.tensor_copy, "bf0")
         gate(0, 0, 0, HALF, "hp0")
+        cast_wg(1, 1, nc.scalar.copy, "bf1", 0, 128)
         quant_wg(1, 0)
         interleave_h(0, 0, 0, HALF)
         gate(0, 1, 0, HALF, "hp1")
-        cast_wg(1, 1, 0, "hp0")
         quant_h(0, 0, 0, HALF)
-        filt(1, 0)
-        interleave_h(0, 1, 0, HALF)
         quant_wg(1, 1)
+        filt(1, 0, (2, 3))
+        interleave_h(0, 1, 0, HALF)
+        gate(1, 0, 0, HALF, "hp0")
         quant_h(0, 1, 0, HALF)
-        gate(1, 0, 0, HALF, "hp1")
-        filt(1, 1)
+        filt(1, 1, range(PACK))
         interleave_h(1, 0, 0, HALF)
-        gate(1, 1, 0, Q, "hp0")
         quant_h(1, 0, 0, HALF)
-        project(0, 0, HALF)
+        gate(1, 1, 0, Q, "hp1")
         interleave_h(1, 1, 0, Q)
-        gate(1, 1, Q, Q, "hp1")
-        last = [psum.tile([P, Q], F32, name="fg") for i in range(N // P)]
-        for i in range(N // P):
-            mm_y(last[i], 1, Q, Q, i, 0)
+        gate(1, 1, Q, Q, "hp0")
+        project(0, 0, HALF)
         quant_h(1, 1, 0, Q)
         interleave_h(1, 1, Q, Q)
         project(1, 0, Q)
+        last = [psum.tile([P, Q], F32, name="bank") for i in range(N // P)]
+        for i in range(N // P):
+            mm_y(last[i], 1, Q, Q, i, 0)
         quant_h(1, 1, Q, Q)
         for i in range(N // P):
             mm_y(last[i], 1, Q, Q, i, 1)
-            store_y(last[i], 1, Q, Q, i, i % 2 == 1)
+            store_y(last[i], 1, Q, Q, i, i % 2 == 0)

@@ -31,10 +31,16 @@ def tile_list_unit_vocoder_gate_kernel(
     with ExitStack() as ctx:
         keep = ctx.enter_context(tc.tile_pool(name="keep", bufs=1))
         work = ctx.enter_context(tc.tile_pool(name="work", bufs=2))
-        psum = ctx.enter_context(tc.psum_pool(name="psum", bufs=8))
+        psum = ctx.enter_context(tc.psum_pool(name="psum", bufs=1))
 
         def kept(shape, dtype, name, tag=""):
             return keep.tile(shape, dtype, name=name, tag=tag or name, align_bytes=AL)
+
+        banks_taken = []
+
+        def take_bank(w):
+            banks_taken.append(psum.tile([P, w], F32, name=f"bank{len(banks_taken) % 8}"))
+            return banks_taken[-1]
 
         offsets = keep.tile([P, S // 16], U16, name="offsets")
         nc.sync.dma_start(offsets[:], offs)
@@ -87,7 +93,7 @@ def tile_list_unit_vocoder_gate_kernel(
         v_w = {}
         v_sc = kept([P, S], U8, "v_sc")
         wf_w = [kept([P, 2, 2 * KP], U8, f"wf_w{b}") for b in range(2)]
-        wf_sc = kept([P, 2, H], U8, "wf_sc")
+        wf_sc = {}
         wg_w = {(b, a): kept([P, KP], U32, f"wg_w{b}{a}") for b in range(2) for a in range(2)}
         wg_sc = {(b, a): kept([P, KP], U8, f"wg_sc{b}{a}") for b in range(2) for a in range(2)}
         h_w = {(b, s): kept([P, HALF], U32, f"h_w{b}{s}") for b in range(2) for s in range(2)}
@@ -108,24 +114,28 @@ def tile_list_unit_vocoder_gate_kernel(
 
         def permute_wf(b):
             nc.vector.tensor_copy(
-                wf_w[b][:].bitcast(U16).rearrange("p a (t m i) -> p a m t i", t=PACK, i=4),
-                wf_raw[b].bitcast(U16).rearrange("p a (m i t) -> p a m t i", t=PACK, i=4),
+                wf_w[b][:].bitcast(U16).rearrange("p a (t m i) -> p a m t i", t=PACK, i=8),
+                wf_raw[b].bitcast(U16).rearrange("p a (m i t) -> p a m t i", t=PACK, i=8),
             )
 
-        def permute_wf_scales():
-            nc.vector.tensor_copy(
-                wf_sc[:].rearrange("p a (b t m i) -> p (a b) m t i", b=2, t=PACK, i=8),
-                wf_sc_raw[:].bitcast(U8).rearrange("p a (b m i t) -> p (a b) m t i", b=2, t=PACK, i=8),
+        def permute_wf_scales(b, tag=""):
+            wf_sc[b] = kept([P, 2, KP], U8, f"wf_sc{b}", tag)
+            src = wf_sc_raw[:].bitcast(U8)[:, :, b * KP : (b + 1) * KP]
+            nc.gpsimd.tensor_copy(
+                wf_sc[b][:].rearrange("p a (t m) -> p a t m", t=PACK),
+                src.rearrange("p a (m t) -> p a t m", t=PACK),
             )
 
         wg_bf = {}
 
-        def cast_wg(b, a, copy, tag, m0=0, m1=P):
-            if m0 == 0:
-                wg_bf[b, a] = kept([P, PACK * KP], BF16, f"wg_bf{b}{a}", tag)
+        def cast_wg(b, a, tag, on_vector):
+            wg_bf[b, a] = kept([P, PACK * KP], BF16, f"wg_bf{b}{a}", tag)
             dst = wg_bf[b, a][:].rearrange("p (t m j) -> p m t j", t=PACK, j=PACK)
             src = wg_raw[b, a].rearrange("p j (m t) -> p m t j", t=PACK)
-            copy(dst[:, m0:m1], src[:, m0:m1])
+            if on_vector:
+                nc.vector.tensor_copy(dst, src)
+            else:
+                nc.scalar.copy(dst, src)
 
         def quant_wg(b, a):
             nc.vector.quantize_mx(out=wg_w[b, a][:].bitcast(FP8X4), scales=wg_sc[b, a][:], in_=wg_bf[b, a][:])
@@ -133,22 +143,22 @@ def tile_list_unit_vocoder_gate_kernel(
         tanh_f = {}
         sig_g = {}
 
-        def mm_f(bank, b, s, t, a):
+        def mm_f(bank, b, s, t, a, up):
             nc.tensor.matmul_mx(
                 out=bank[:],
                 lhsT=wf_w[b][:, a, 2 * P * t : 2 * P * (t + 1)].bitcast(FP4X4),
-                lhsT_scale=wf_sc[:, a, KP * b + P * t : KP * b + P * (t + 1)],
+                lhsT_scale=wf_sc[b][:, a, P * t : P * (t + 1)],
                 rhs=v_w[a, s][:].bitcast(FP8X4),
                 rhs_scale=v_plane(a, slice(s * HALF, (s + 1) * HALF)),
-                start=(a == 0),
-                stop=(a == 1),
+                start=(a == 0) == up,
+                stop=(a == 1) == up,
             )
 
         def filt(b, s, tiles=range(PACK)):
             for t in tiles:
-                bank = psum.tile([P, HALF], F32, name="bank")
-                for a in range(2):
-                    mm_f(bank, b, s, t, a)
+                bank = take_bank(HALF)
+                for a in ((0, 1) if (b, s) == (0, 0) else (1, 0)):
+                    mm_f(bank, b, s, t, a, (b, s) == (0, 0))
                 tanh_f[b, s, t] = work.tile([P, HALF], F32, name="tanh_f", bufs=16)
                 nc.scalar.activation(tanh_f[b, s, t][:], bank[:], ACT.Tanh)
 
@@ -158,7 +168,7 @@ def tile_list_unit_vocoder_gate_kernel(
             planes = kept([P, PACK, w], BF16, f"h_planes{b}{s}{c0}", tag)
             h_planes[b, s, c0] = planes
             for t in range(PACK):
-                bank = psum.tile([P, w], F32, name="bank")
+                bank = take_bank(w)
                 for a in (1, 0):
                     nc.tensor.matmul_mx(
                         out=bank[:],
@@ -210,7 +220,7 @@ def tile_list_unit_vocoder_gate_kernel(
 
         def project(s, c0, w, tiles=range(N // P), on_vector=()):
             for i in tiles:
-                bank = psum.tile([P, w], F32, name="bank")
+                bank = take_bank(w)
                 for b in range(2):
                     mm_y(bank, s, c0, w, i, b)
                 store_y(bank, s, c0, w, i, i in on_vector)
@@ -221,19 +231,20 @@ def tile_list_unit_vocoder_gate_kernel(
         load_wg(0, 0, wg_b0[:, 0, :, :])
         load_wf(1, kept([P, 2, KP // 2], I32, "wf_raw1")[:])
         load_wg(0, 1, wg_b0[:, 1, :, :])
+        permute_wf_scales(0)
         gather_words(0, 0)
         permute_wf(0)
-        permute_wf_scales()
+        permute_wf_scales(1, "slot_f")
         gather_words(1, 0)
         filt(0, 0)
         gather_words(1, 1)
-        gather_words(0, 1, "tab1")
+        gather_words(0, 1)
         for a in range(2):
             load_wg(1, a, kept([P, PACK, KP], F32, f"wg_b1{a}")[:])
         filt(0, 1)
-        cast_wg(0, 0, nc.vector.tensor_copy, "bf0")
+        cast_wg(0, 0, "bf0", True)
         permute_wf(1)
-        cast_wg(0, 1, nc.vector.tensor_copy, "bf1")
+        cast_wg(0, 1, "bf1", True)
         wo_w = kept([P, 2, N], I32, "wo_w", "slot_a")
         nc.sync.dma_start(wo_w[:], wo_words.rearrange("a p n i -> p a (n i)").bitcast(I32))
         load_plane(wo_sc, wo_scales)
@@ -242,16 +253,16 @@ def tile_list_unit_vocoder_gate_kernel(
         bo_sb = kept([P, N // P], F32, "bo_sb", "wf_raw1")
         with nc.allow_non_contiguous_dma(reason="one bias value a partition"):
             nc.sync.dma_start(bo_sb[:], bo.rearrange("(i p) -> p i", p=P))
-        filt(1, 0, (0, 1))
-        cast_wg(1, 0, nc.vector.tensor_copy, "bf0")
+        filt(1, 0, (0,))
+        cast_wg(1, 0, "bf0", True)
         gate(0, 0, 0, HALF, "hp0")
-        cast_wg(1, 1, nc.scalar.copy, "bf1", 0, 128)
+        cast_wg(1, 1, "bf1", False)
         quant_wg(1, 0)
         interleave_h(0, 0, 0, HALF)
         gate(0, 1, 0, HALF, "hp1")
         quant_h(0, 0, 0, HALF)
         quant_wg(1, 1)
-        filt(1, 0, (2, 3))
+        filt(1, 0, (1, 2, 3))
         interleave_h(0, 1, 0, HALF)
         gate(1, 0, 0, HALF, "hp0")
         quant_h(0, 1, 0, HALF)
@@ -265,7 +276,7 @@ def tile_list_unit_vocoder_gate_kernel(
         quant_h(1, 1, 0, Q)
         interleave_h(1, 1, Q, Q)
         project(1, 0, Q)
-        last = [psum.tile([P, Q], F32, name="bank") for i in range(N // P)]
+        last = [take_bank(Q) for i in range(N // P)]
         for i in range(N // P):
             mm_y(last[i], 1, Q, Q, i, 0)
         quant_h(1, 1, Q, Q)

@@ -22,6 +22,7 @@ PACK = 4
 KP = P * PACK
 HALF = 512
 AL = 64
+SIG_BUFS = 4
 
 
 def tile_list_unit_vocoder_gate_kernel(
@@ -45,21 +46,20 @@ def tile_list_unit_vocoder_gate_kernel(
         offsets = keep.tile([P, S // 16], U16, name="offsets")
         nc.sync.dma_start(offsets[:], offs)
 
-        tab_sc = kept([P, T // 4], I32, "tab_sc", "slot_a")
+        tab_sc = kept([P, T // 4], I32, "tab_sc")
         nc.sync.dma_start(tab_sc[0:32, :], tab_scales.bitcast(I32).rearrange("a q c -> q a c"))
+        wf_sc_raw = kept([P, 2, H // 4], I32, "wf_sc_raw", "slot_s")
+        nc.vector.memset(wf_sc_raw[:], 0)
         nc.vector.memset(tab_sc[32:64, :], 0)
         nc.vector.memset(tab_sc[64:128, :], 0)
-        wf_sc_raw = kept([P, 2, H // 4], I32, "wf_sc_raw", "slot_s")
         v_pl = kept([P, 2, S // 4], I32, "v_pl")
-        nc.gpsimd.memset(wf_sc_raw[:], 0)
         nc.gpsimd.memset(v_pl[:], 0)
 
         wo_sc = kept([P, 2, N // 4], I32, "wo_sc")
-        warm = kept([P, 1], F32, "warm", "tab1")
+        warm = kept([P, 1], F32, "warm")
         warm_out = kept([P, 1], F32, "warm_out")
         nc.gpsimd.memset(warm[:], 0.0)
         nc.gpsimd.memset(wo_sc[:], 0)
-        nc.scalar.activation(warm_out[:], warm[:], ACT.Sigmoid)
 
         tab = [kept([P, T], I32, f"tab{a}") for a in range(2)]
         wf_raw = {}
@@ -73,20 +73,19 @@ def tile_list_unit_vocoder_gate_kernel(
             src = wf_words.bitcast(I32).rearrange("a p c -> p a c")
             nc.sync.dma_start(dst, src[:, :, b * (KP // 2) : (b + 1) * (KP // 2)])
 
-        def load_wg(b, a, dst):
-            wg_raw[b, a] = dst
-            src = wg[a * KP : (a + 1) * KP, b * KP : (b + 1) * KP]
-            nc.sync.dma_start(dst, src.rearrange("(p j) c -> p j c", j=PACK))
+        def load_wg(b, a, c0=0, w=KP, tag=""):
+            wg_raw[b, a, c0] = kept([P, PACK, w], F32, f"wg_raw{b}{a}{c0}", tag)
+            src = wg[a * KP : (a + 1) * KP, b * KP + c0 : b * KP + c0 + w]
+            nc.sync.dma_start(wg_raw[b, a, c0][:], src.rearrange("(p j) c -> p j c", j=PACK))
 
-        def load_plane(plane, scales):
+        def load_plane(plane, scales, queue):
             for q in range(4):
                 src = scales.bitcast(I32)[:, 4 * q : 4 * q + 4, :].rearrange("a r c -> r a c")
-                nc.sync.dma_start(plane[32 * q : 32 * q + 4, :, :], src)
+                queue.dma_start(plane[32 * q : 32 * q + 4, :, :], src)
 
         load_tab(0)
-        gain_sb = kept([P, 2, PACK], F32, "gain_sb")
-        nc.scalar.dma_start(gain_sb[:], gain.rearrange("(b p t) -> p b t", b=2, t=PACK))
-        load_plane(wf_sc_raw, wf_scales)
+        load_plane(wf_sc_raw, wf_scales, nc.sync)
+        nc.scalar.activation(warm_out[:], warm[:], ACT.Sigmoid)
         load_wf(0, kept([P, 2, KP // 2], I32, "wf_raw0", "slot_f")[:])
         load_tab(1)
 
@@ -96,8 +95,8 @@ def tile_list_unit_vocoder_gate_kernel(
         wf_sc = {}
         wg_w = {(b, a): kept([P, KP], U32, f"wg_w{b}{a}") for b in range(2) for a in range(2)}
         wg_sc = {(b, a): kept([P, KP], U8, f"wg_sc{b}{a}") for b in range(2) for a in range(2)}
-        h_w = {(b, s): kept([P, HALF], U32, f"h_w{b}{s}") for b in range(2) for s in range(2)}
-        h_sc = {(b, s): kept([P, HALF], U8, f"h_sc{b}{s}") for b in range(2) for s in range(2)}
+        h_w = [kept([P, S], U32, f"h_w{b}") for b in range(2)]
+        h_sc = [kept([P, S], U8, f"h_sc{b}") for b in range(2)]
 
         def gather_words(a, s, tag=""):
             v_w[a, s] = kept([P, HALF], U32, f"v_w{a}{s}", tag)
@@ -128,20 +127,24 @@ def tile_list_unit_vocoder_gate_kernel(
 
         wg_bf = {}
 
-        def cast_wg(b, a, tag, on_vector):
-            wg_bf[b, a] = kept([P, PACK * KP], BF16, f"wg_bf{b}{a}", tag)
-            dst = wg_bf[b, a][:].rearrange("p (t m j) -> p m t j", t=PACK, j=PACK)
-            src = wg_raw[b, a].rearrange("p j (m t) -> p m t j", t=PACK)
+        def cast_wg(b, a, on_vector, c0=0, w=KP):
+            if (b, a) not in wg_bf:
+                wg_bf[b, a] = kept([P, PACK * KP], BF16, f"wg_bf{b}{a}")
+            dst = wg_bf[b, a][:].rearrange("p (t m j) -> p m t j", t=PACK, j=PACK)[:, c0 // PACK : (c0 + w) // PACK]
+            src = wg_raw[b, a, c0][:].rearrange("p j (m t) -> p m t j", t=PACK)
             if on_vector:
                 nc.vector.tensor_copy(dst, src)
             else:
                 nc.scalar.copy(dst, src)
 
-        def quant_wg(b, a):
-            nc.vector.quantize_mx(out=wg_w[b, a][:].bitcast(FP8X4), scales=wg_sc[b, a][:], in_=wg_bf[b, a][:])
+        def quant_wg(b, a, c0=0, w=KP):
+            nc.vector.quantize_mx(
+                out=wg_w[b, a][:, c0 : c0 + w].bitcast(FP8X4),
+                scales=wg_sc[b, a][:, c0 : c0 + w],
+                in_=wg_bf[b, a][:, PACK * c0 : PACK * (c0 + w)],
+            )
 
         tanh_f = {}
-        sig_g = {}
 
         def mm_f(bank, b, s, t, a, up):
             nc.tensor.matmul_mx(
@@ -163,123 +166,159 @@ def tile_list_unit_vocoder_gate_kernel(
                 nc.scalar.activation(tanh_f[b, s, t][:], bank[:], ACT.Tanh)
 
         h_planes = {}
+        sig_g = {}
 
-        def gate(b, s, c0, w, tag):
-            planes = kept([P, PACK, w], BF16, f"h_planes{b}{s}{c0}", tag)
-            h_planes[b, s, c0] = planes
-            for t in range(PACK):
-                bank = take_bank(w)
-                for a in (1, 0):
-                    nc.tensor.matmul_mx(
-                        out=bank[:],
-                        lhsT=wg_w[b, a][:, P * t : P * (t + 1)].bitcast(FP8X4),
-                        lhsT_scale=wg_sc[b, a][:, P * t : P * (t + 1)],
-                        rhs=v_w[a, s][:, c0 : c0 + w].bitcast(FP8X4),
-                        rhs_scale=v_plane(a, slice(s * HALF + c0, s * HALF + c0 + w)),
-                        start=(a == 1),
-                        stop=(a == 0),
-                    )
-                sig = work.tile([P, w], F32, name="sig", bufs=8)
+        def gate(b, c0, w, passes=(1, 0), first_tag=None):
+            s, per = c0 // HALF, HALF // w
+            for t0 in range(0, PACK, per):
+                bank = take_bank(HALF)
+                for t in range(t0, t0 + per):
+                    for a in passes:
+                        nc.tensor.matmul_mx(
+                            out=bank[:, (t - t0) * w : (t - t0 + 1) * w],
+                            lhsT=wg_w[b, a][:, P * t : P * (t + 1)].bitcast(FP8X4),
+                            lhsT_scale=wg_sc[b, a][:, P * t : P * (t + 1)],
+                            rhs=v_w[a, s][:, c0 % HALF : c0 % HALF + w].bitcast(FP8X4),
+                            rhs_scale=v_plane(a, slice(c0, c0 + w)),
+                            start=(a == passes[0]),
+                            stop=(a == passes[1]),
+                        )
+                if first_tag and t0 == 0:
+                    sig = kept([P, HALF], F32, "sig_first", first_tag)
+                else:
+                    sig = work.tile([P, HALF], F32, name="sig", bufs=SIG_BUFS)
                 nc.scalar.activation(sig[:], bank[:], ACT.Sigmoid)
+                for t in range(t0, t0 + per):
+                    sig_g[b, c0, t] = sig[:, (t - t0) * w : (t - t0 + 1) * w]
+
+        def product(b, c0, w, tiles=range(PACK), tag=""):
+            if tag:
+                h_planes[b, c0] = kept([P, PACK, w], BF16, "h_planes_first", tag)
+            if (b, c0) not in h_planes:
+                h_planes[b, c0] = work.tile([P, PACK, w], BF16, name="h_planes")
+            planes = h_planes[b, c0]
+            for t in tiles:
                 nc.vector.scalar_tensor_tensor(
-                    planes[:, t, :], tanh_f[b, s, t][:, c0 : c0 + w], gain_sb[:, b, t : t + 1], sig[:], MULT, MULT
+                    planes[:, t, :],
+                    tanh_f[b, c0 // HALF, t][:, c0 % HALF : c0 % HALF + w],
+                    gain_sb[:, b, t : t + 1],
+                    sig_g[b, c0, t],
+                    MULT,
+                    MULT,
                 )
 
         h_il = {}
 
-        def interleave_h(b, s, c0, w):
-            h_il[b, s, c0] = work.tile([P, PACK * w], BF16, name="h_il", align_bytes=AL)
+        def interleave_h(b, c0, w):
+            h_il[b, c0] = work.tile([P, PACK * w], BF16, name="h_il", align_bytes=AL)
             nc.vector.tensor_copy(
-                h_il[b, s, c0][:].rearrange("p (c i t) -> p c t i", t=PACK, i=4),
-                h_planes[b, s, c0][:].rearrange("p t (c i) -> p c t i", i=4),
+                h_il[b, c0][:].rearrange("p (c i t) -> p c t i", t=PACK, i=4),
+                h_planes[b, c0][:].rearrange("p t (c i) -> p c t i", i=4),
             )
 
-        def quant_h(b, s, c0, w):
+        def quant_h(b, c0, w):
             nc.vector.quantize_mx(
-                out=h_w[b, s][:, c0 : c0 + w].bitcast(FP8X4), scales=h_sc[b, s][:, c0 : c0 + w], in_=h_il[b, s, c0][:]
+                out=h_w[b][:, c0 : c0 + w].bitcast(FP8X4), scales=h_sc[b][:, c0 : c0 + w], in_=h_il[b, c0][:]
             )
 
-        def mm_y(bank, s, c0, w, i, b):
-            nc.tensor.matmul_mx(
-                out=bank[:],
-                lhsT=wo_w[:, b, P * i : P * (i + 1)].bitcast(FP8X4),
-                lhsT_scale=wo_sc[:, b, :].bitcast(U8)[:, P * i : P * (i + 1)],
-                rhs=h_w[b, s][:, c0 : c0 + w].bitcast(FP8X4),
-                rhs_scale=h_sc[b, s][:, c0 : c0 + w],
-                start=(b == 0),
-                stop=(b == 1),
-            )
-
-        def store_y(bank, s, c0, w, i, on_vector):
-            y = work.tile([P, w], F32, name="y_sb", bufs=12)
-            if on_vector:
-                nc.vector.tensor_scalar(y[:], bank[:], bo_sb[:, i : i + 1], None, ADD)
-            else:
-                nc.scalar.activation(y[:], bank[:], ACT.Identity, bias=bo_sb[:, i : i + 1])
-            nc.sync.dma_start(out[P * i : P * (i + 1), s * HALF + c0 : s * HALF + c0 + w], y[:])
-
-        def project(s, c0, w, tiles=range(N // P), on_vector=()):
-            for i in tiles:
-                bank = take_bank(w)
-                for b in range(2):
-                    mm_y(bank, s, c0, w, i, b)
-                store_y(bank, s, c0, w, i, i in on_vector)
+        def project(c0, w, on_vector=()):
+            for i0 in range(0, N // P, 2):
+                bank = take_bank(2 * w)
+                for i in (i0, i0 + 1):
+                    for b in range(2):
+                        nc.tensor.matmul_mx(
+                            out=bank[:, (i - i0) * w : (i - i0 + 1) * w],
+                            lhsT=wo_w[:, b, P * i : P * (i + 1)].bitcast(FP8X4),
+                            lhsT_scale=wo_sc[:, b, :].bitcast(U8)[:, P * i : P * (i + 1)],
+                            rhs=h_w[b][:, c0 : c0 + w].bitcast(FP8X4),
+                            rhs_scale=h_sc[b][:, c0 : c0 + w],
+                            start=(b == 0),
+                            stop=(b == 1),
+                        )
+                y = work.tile([P, 2, w], F32, name="y_sb", bufs=8)
+                for i in (i0, i0 + 1):
+                    src = bank[:, (i - i0) * w : (i - i0 + 1) * w]
+                    if i0 in on_vector:
+                        nc.vector.tensor_scalar(y[:, i - i0, :], src, bo_sb[:, i : i + 1], None, ADD)
+                    else:
+                        nc.scalar.activation(y[:, i - i0, :], src, ACT.Identity, bias=bo_sb[:, i : i + 1])
+                dst = out[P * i0 : P * (i0 + 2), c0 : c0 + w].rearrange("(i p) c -> p i c", p=P)
+                nc.sync.dma_start(dst, y[:])
 
         Q = HALF // 2
         gather_scales()
-        wg_b0 = kept([P, 2, PACK, KP], F32, "wg_b0", "slot_a")
-        load_wg(0, 0, wg_b0[:, 0, :, :])
+        load_wg(0, 0, tag="tab_sc")
+        load_wg(0, 1, 0, Q)
+        load_wg(0, 1, Q, Q)
+        gain_sb = kept([P, 2, PACK], F32, "gain_sb")
+        nc.sync.dma_start(gain_sb[:], gain.rearrange("(b p t) -> p b t", b=2, t=PACK))
+        load_wg(1, 0)
         load_wf(1, kept([P, 2, KP // 2], I32, "wf_raw1")[:])
-        load_wg(0, 1, wg_b0[:, 1, :, :])
+        load_wg(1, 1)
+        wo_w = kept([P, 2, N], I32, "wo_w")
+        nc.sync.dma_start(wo_w[:], wo_words.rearrange("a p n i -> p a (n i)").bitcast(I32))
+        load_plane(wo_sc, wo_scales, nc.sync)
+        bo_sb = kept([P, N // P], F32, "bo_sb")
+        with nc.allow_non_contiguous_dma(reason="one bias value a partition"):
+            nc.sync.dma_start(bo_sb[:], bo.rearrange("(i p) -> p i", p=P))
         permute_wf_scales(0)
         gather_words(0, 0)
         permute_wf(0)
-        permute_wf_scales(1, "slot_f")
+        permute_wf_scales(1)
+        gather_words(0, 1)
         gather_words(1, 0)
         filt(0, 0)
         gather_words(1, 1)
-        gather_words(0, 1)
-        for a in range(2):
-            load_wg(1, a, kept([P, PACK, KP], F32, f"wg_b1{a}")[:])
+        cast_wg(0, 0, True)
         filt(0, 1)
-        cast_wg(0, 0, "bf0", True)
-        permute_wf(1)
-        cast_wg(0, 1, "bf1", True)
-        wo_w = kept([P, 2, N], I32, "wo_w", "slot_a")
-        nc.sync.dma_start(wo_w[:], wo_words.rearrange("a p n i -> p a (n i)").bitcast(I32))
-        load_plane(wo_sc, wo_scales)
+        cast_wg(0, 1, True, 0, Q)
         quant_wg(0, 0)
-        quant_wg(0, 1)
-        bo_sb = kept([P, N // P], F32, "bo_sb", "wf_raw1")
-        with nc.allow_non_contiguous_dma(reason="one bias value a partition"):
-            nc.sync.dma_start(bo_sb[:], bo.rearrange("(i p) -> p i", p=P))
-        filt(1, 0, (0,))
-        cast_wg(1, 0, "bf0", True)
-        gate(0, 0, 0, HALF, "hp0")
-        cast_wg(1, 1, "bf1", False)
+        cast_wg(0, 1, True, Q, Q)
+        quant_wg(0, 1, 0, Q)
+        quant_wg(0, 1, Q, Q)
+        cast_wg(1, 0, True)
+        gate(0, 0, HALF)
+        permute_wf(1)
+        product(0, 0, HALF, tag="wg_raw100")
+        gate(0, HALF, HALF)
+        cast_wg(1, 1, False)
         quant_wg(1, 0)
-        interleave_h(0, 0, 0, HALF)
-        gate(0, 1, 0, HALF, "hp1")
-        quant_h(0, 0, 0, HALF)
+        interleave_h(0, 0, HALF)
+        filt(1, 0)
+        quant_h(0, 0, HALF)
+        product(0, HALF, HALF)
         quant_wg(1, 1)
-        filt(1, 0, (1, 2, 3))
-        interleave_h(0, 1, 0, HALF)
-        gate(1, 0, 0, HALF, "hp0")
-        quant_h(0, 1, 0, HALF)
-        filt(1, 1, range(PACK))
-        interleave_h(1, 0, 0, HALF)
-        quant_h(1, 0, 0, HALF)
-        gate(1, 1, 0, Q, "hp1")
-        interleave_h(1, 1, 0, Q)
-        gate(1, 1, Q, Q, "hp0")
-        project(0, 0, HALF)
-        quant_h(1, 1, 0, Q)
-        interleave_h(1, 1, Q, Q)
-        project(1, 0, Q)
-        last = [take_bank(Q) for i in range(N // P)]
-        for i in range(N // P):
-            mm_y(last[i], 1, Q, Q, i, 0)
-        quant_h(1, 1, Q, Q)
-        for i in range(N // P):
-            mm_y(last[i], 1, Q, Q, i, 1)
-            store_y(last[i], 1, Q, Q, i, i % 2 == 0)
+        gate(1, 0, 256)
+        interleave_h(0, HALF, HALF)
+        product(1, 0, 256, (0,))
+        quant_h(0, HALF, HALF)
+        gate(1, 256, 256)
+        filt(1, 1, range(0, 2))
+        product(1, 0, 256, (1, 2, 3))
+        interleave_h(1, 0, 256)
+        product(1, 256, 256, (0,))
+        quant_h(1, 0, 256)
+        gate(1, 512, 256)
+        filt(1, 1, range(2, 4))
+        product(1, 256, 256, (1, 2, 3))
+        project(0, 256)
+        interleave_h(1, 256, 256)
+        product(1, 512, 256, (0,))
+        quant_h(1, 256, 256)
+        gate(1, 768, 128)
+        product(1, 512, 256, (1, 2, 3))
+        project(256, 256)
+        interleave_h(1, 512, 256)
+        product(1, 768, 128, (0,))
+        quant_h(1, 512, 256)
+        gate(1, 896, 128)
+        product(1, 768, 128, (1, 2, 3))
+        project(512, 256)
+        interleave_h(1, 768, 128)
+        product(1, 896, 128, (0,))
+        quant_h(1, 768, 128)
+        product(1, 896, 128, (1, 2, 3))
+        project(768, 128, ())
+        interleave_h(1, 896, 128)
+        quant_h(1, 896, 128)
+        project(896, 128, (0,))

@@ -78,13 +78,13 @@ def tile_list_unit_vocoder_gate_kernel(
             src = wg[a * KP : (a + 1) * KP, b * KP + c0 : b * KP + c0 + w]
             nc.sync.dma_start(wg_raw[b, a, c0][:], src.rearrange("(p j) c -> p j c", j=PACK))
 
-        def load_plane(plane, scales, queue):
-            for q in range(4):
-                src = scales.bitcast(I32)[:, 4 * q : 4 * q + 4, :].rearrange("a r c -> r a c")
-                queue.dma_start(plane[32 * q : 32 * q + 4, :, :], src)
+        def load_plane(plane, scales):
+            for r in range(4):
+                src = scales.bitcast(I32)[:, r:16:4, :].rearrange("a q c -> q a c")
+                nc.sync.dma_start(plane[r:P:32, :, :], src)
 
         load_tab(0)
-        load_plane(wf_sc_raw, wf_scales, nc.sync)
+        load_plane(wf_sc_raw, wf_scales)
         nc.scalar.activation(warm_out[:], warm[:], ACT.Sigmoid)
         load_wf(0, kept([P, 2, KP // 2], I32, "wf_raw0", "slot_f")[:])
         load_tab(1)
@@ -257,7 +257,7 @@ def tile_list_unit_vocoder_gate_kernel(
         load_wg(1, 1)
         wo_w = kept([P, 2, N], I32, "wo_w")
         nc.sync.dma_start(wo_w[:], wo_words.rearrange("a p n i -> p a (n i)").bitcast(I32))
-        load_plane(wo_sc, wo_scales, nc.sync)
+        load_plane(wo_sc, wo_scales)
         bo_sb = kept([P, N // P], F32, "bo_sb")
         with nc.allow_non_contiguous_dma(reason="one bias value a partition"):
             nc.sync.dma_start(bo_sb[:], bo.rearrange("(i p) -> p i", p=P))

@@ -105,7 +105,7 @@ def tile_list_unit_vocoder_gate_kernel(
 
         def gather_scales():
             nc.vector.tensor_copy(v_sc[:], tab_sc[:].bitcast(U8).indirect(offsets[:]))
-            for q in range(4):
+            for q in (0, 2, 1, 3):
                 nc.sync.dma_start(v_pl[32 * q : 32 * q + 4, :, :], v_sc[:].bitcast(I32)[8 * q : 8 * q + 8, :])
 
         def v_plane(a, cols):
@@ -130,8 +130,8 @@ def tile_list_unit_vocoder_gate_kernel(
         def cast_wg(b, a, on_vector, c0=0, w=KP):
             if (b, a) not in wg_bf:
                 wg_bf[b, a] = kept([P, PACK * KP], BF16, f"wg_bf{b}{a}")
-            dst = wg_bf[b, a][:].rearrange("p (t m j) -> p m t j", t=PACK, j=PACK)[:, c0 // PACK : (c0 + w) // PACK]
-            src = wg_raw[b, a, c0][:].rearrange("p j (m t) -> p m t j", t=PACK)
+            dst = wg_bf[b, a][:].rearrange("p (t m j) -> p m j t", t=PACK, j=PACK)[:, c0 // PACK : (c0 + w) // PACK]
+            src = wg_raw[b, a, c0][:].rearrange("p j (m t) -> p m j t", t=PACK)
             if on_vector:
                 nc.vector.tensor_copy(dst, src)
             else:
@@ -221,38 +221,53 @@ def tile_list_unit_vocoder_gate_kernel(
                 out=h_w[b][:, c0 : c0 + w].bitcast(FP8X4), scales=h_sc[b][:, c0 : c0 + w], in_=h_il[b, c0][:]
             )
 
+        def mm_y(dst, i, b, c0, w):
+            nc.tensor.matmul_mx(
+                out=dst,
+                lhsT=wo_w[:, b, P * i : P * (i + 1)].bitcast(FP8X4),
+                lhsT_scale=wo_sc[:, b, :].bitcast(U8)[:, P * i : P * (i + 1)],
+                rhs=h_w[b][:, c0 : c0 + w].bitcast(FP8X4),
+                rhs_scale=h_sc[b][:, c0 : c0 + w],
+                start=(b == 0),
+                stop=(b == 1),
+            )
+
+        def store_pair(sums, i0, c0, w, on_vector):
+            y = work.tile([P, 2, w], F32, name="y_sb", bufs=8)
+            for i in (i0, i0 + 1):
+                if on_vector:
+                    nc.vector.tensor_scalar(y[:, i - i0, :], sums[i], bo_sb[:, i : i + 1], None, ADD)
+                else:
+                    nc.scalar.activation(y[:, i - i0, :], sums[i], ACT.Identity, bias=bo_sb[:, i : i + 1])
+            dst = out[P * i0 : P * (i0 + 2), c0 : c0 + w].rearrange("(i p) c -> p i c", p=P)
+            nc.sync.dma_start(dst, y[:])
+
         def project(c0, w, on_vector=()):
             for i0 in range(0, N // P, 2):
                 bank = take_bank(2 * w)
+                sums = {i: bank[:, (i - i0) * w : (i - i0 + 1) * w] for i in (i0, i0 + 1)}
                 for i in (i0, i0 + 1):
                     for b in range(2):
-                        nc.tensor.matmul_mx(
-                            out=bank[:, (i - i0) * w : (i - i0 + 1) * w],
-                            lhsT=wo_w[:, b, P * i : P * (i + 1)].bitcast(FP8X4),
-                            lhsT_scale=wo_sc[:, b, :].bitcast(U8)[:, P * i : P * (i + 1)],
-                            rhs=h_w[b][:, c0 : c0 + w].bitcast(FP8X4),
-                            rhs_scale=h_sc[b][:, c0 : c0 + w],
-                            start=(b == 0),
-                            stop=(b == 1),
-                        )
-                y = work.tile([P, 2, w], F32, name="y_sb", bufs=8)
-                for i in (i0, i0 + 1):
-                    src = bank[:, (i - i0) * w : (i - i0 + 1) * w]
-                    if i0 in on_vector:
-                        nc.vector.tensor_scalar(y[:, i - i0, :], src, bo_sb[:, i : i + 1], None, ADD)
-                    else:
-                        nc.scalar.activation(y[:, i - i0, :], src, ACT.Identity, bias=bo_sb[:, i : i + 1])
-                dst = out[P * i0 : P * (i0 + 2), c0 : c0 + w].rearrange("(i p) c -> p i c", p=P)
-                nc.sync.dma_start(dst, y[:])
+                        mm_y(sums[i], i, b, c0, w)
+                store_pair(sums, i0, c0, w, i0 in on_vector)
+
+        def finish(c0, w):
+            sums = {i: take_bank(w)[:] for i in range(N // P)}
+            for i in range(N // P):
+                mm_y(sums[i], i, 0, c0, w)
+            quant_h(1, c0, w)
+            for i in range(N // P):
+                mm_y(sums[i], i, 1, c0, w)
+            store_pair(sums, 0, c0, w, True)
+            store_pair(sums, 2, c0, w, False)
 
         Q = HALF // 2
         gather_scales()
         load_wg(0, 0, tag="tab_sc")
-        load_wg(0, 1, 0, Q)
-        load_wg(0, 1, Q, Q)
+        load_wg(0, 1)
+        load_wg(1, 0)
         gain_sb = kept([P, 2, PACK], F32, "gain_sb")
         nc.sync.dma_start(gain_sb[:], gain.rearrange("(b p t) -> p b t", b=2, t=PACK))
-        load_wg(1, 0)
         load_wf(1, kept([P, 2, KP // 2], I32, "wf_raw1")[:])
         load_wg(1, 1)
         wo_w = kept([P, 2, N], I32, "wo_w")
@@ -271,9 +286,8 @@ def tile_list_unit_vocoder_gate_kernel(
         gather_words(1, 1)
         cast_wg(0, 0, True)
         filt(0, 1)
-        cast_wg(0, 1, True, 0, Q)
         quant_wg(0, 0)
-        cast_wg(0, 1, True, Q, Q)
+        cast_wg(0, 1, True)
         quant_wg(0, 1, 0, Q)
         quant_wg(0, 1, Q, Q)
         cast_wg(1, 0, True)
@@ -284,7 +298,7 @@ def tile_list_unit_vocoder_gate_kernel(
         cast_wg(1, 1, False)
         quant_wg(1, 0)
         interleave_h(0, 0, HALF)
-        filt(1, 0)
+        filt(1, 0, range(0, 4))
         quant_h(0, 0, HALF)
         product(0, HALF, HALF)
         quant_wg(1, 1)
@@ -318,7 +332,6 @@ def tile_list_unit_vocoder_gate_kernel(
         product(1, 896, 128, (0,))
         quant_h(1, 768, 128)
         product(1, 896, 128, (1, 2, 3))
-        project(768, 128, ())
+        project(768, 128, (0,))
         interleave_h(1, 896, 128)
-        quant_h(1, 896, 128)
-        project(896, 128, (0,))
+        finish(896, 128)

@@ -127,11 +127,11 @@ def tile_list_unit_vocoder_gate_kernel(
 
         wg_bf = {}
 
-        def cast_wg(b, a, on_vector, c0=0, w=KP):
+        def cast_wg(b, a, on_vector, m0=0, m1=P):
             if (b, a) not in wg_bf:
                 wg_bf[b, a] = kept([P, PACK * KP], BF16, f"wg_bf{b}{a}")
-            dst = wg_bf[b, a][:].rearrange("p (t m j) -> p m j t", t=PACK, j=PACK)[:, c0 // PACK : (c0 + w) // PACK]
-            src = wg_raw[b, a, c0][:].rearrange("p j (m t) -> p m j t", t=PACK)
+            dst = wg_bf[b, a][:].rearrange("p (t m j) -> p m j t", t=PACK, j=PACK)[:, m0:m1]
+            src = wg_raw[b, a, 0][:].rearrange("p j (m t) -> p m j t", t=PACK)[:, m0:m1]
             if on_vector:
                 nc.vector.tensor_copy(dst, src)
             else:
@@ -165,8 +165,40 @@ def tile_list_unit_vocoder_gate_kernel(
                 tanh_f[b, s, t] = work.tile([P, HALF], F32, name="tanh_f", bufs=16)
                 nc.scalar.activation(tanh_f[b, s, t][:], bank[:], ACT.Tanh)
 
+        def filt_first():
+            banks = [take_bank(HALF) for t in range(PACK)]
+            for a, t in ((0, 0), (0, 1), (1, 0), (1, 1), (0, 2), (1, 2), (0, 3), (1, 3)):
+                mm_f(banks[t], 0, 0, t, a, True)
+                if a == 1:
+                    tanh_f[0, 0, t] = work.tile([P, HALF], F32, name="tanh_f", bufs=16)
+                    nc.scalar.activation(tanh_f[0, 0, t][:], banks[t][:], ACT.Tanh)
+
         h_planes = {}
         sig_g = {}
+
+        def mm_g(dst, b, t, a, c0, w, start, stop):
+            nc.tensor.matmul_mx(
+                out=dst,
+                lhsT=wg_w[b, a][:, P * t : P * (t + 1)].bitcast(FP8X4),
+                lhsT_scale=wg_sc[b, a][:, P * t : P * (t + 1)],
+                rhs=v_w[a, c0 // HALF][:, c0 % HALF : c0 % HALF + w].bitcast(FP8X4),
+                rhs_scale=v_plane(a, slice(c0, c0 + w)),
+                start=start,
+                stop=stop,
+            )
+
+        def gate_open():
+            banks = [take_bank(HALF) for t in range(PACK)]
+            for t in range(PACK):
+                mm_g(banks[t][:], 0, t, 0, 0, HALF, True, False)
+            return banks
+
+        def gate_close(banks):
+            for t in range(PACK):
+                mm_g(banks[t][:], 0, t, 1, 0, HALF, False, True)
+                sig = work.tile([P, HALF], F32, name="sig", bufs=SIG_BUFS)
+                nc.scalar.activation(sig[:], banks[t][:], ACT.Sigmoid)
+                sig_g[0, 0, t] = sig[:]
 
         def gate(b, c0, w, passes=(1, 0), first_tag=None):
             s, per = c0 // HALF, HALF // w
@@ -209,9 +241,9 @@ def tile_list_unit_vocoder_gate_kernel(
 
         h_il = {}
 
-        def interleave_h(b, c0, w):
+        def interleave_h(b, c0, w, copy=nc.vector.tensor_copy):
             h_il[b, c0] = work.tile([P, PACK * w], BF16, name="h_il", align_bytes=AL)
-            nc.vector.tensor_copy(
+            copy(
                 h_il[b, c0][:].rearrange("p (c i t) -> p c t i", t=PACK, i=4),
                 h_planes[b, c0][:].rearrange("p t (c i) -> p c t i", i=4),
             )
@@ -251,15 +283,17 @@ def tile_list_unit_vocoder_gate_kernel(
                         mm_y(sums[i], i, b, c0, w)
                 store_pair(sums, i0, c0, w, i0 in on_vector)
 
-        def finish(c0, w):
+        def open_sums(c0, w):
             sums = {i: take_bank(w)[:] for i in range(N // P)}
             for i in range(N // P):
                 mm_y(sums[i], i, 0, c0, w)
-            quant_h(1, c0, w)
-            for i in range(N // P):
-                mm_y(sums[i], i, 1, c0, w)
-            store_pair(sums, 0, c0, w, True)
-            store_pair(sums, 2, c0, w, False)
+            return sums
+
+        def close_sums(sums, c0, w, on_vector=()):
+            for i0 in range(0, N // P, 2):
+                for i in (i0, i0 + 1):
+                    mm_y(sums[i], i, 1, c0, w)
+                store_pair(sums, i0, c0, w, i0 in on_vector)
 
         Q = HALF // 2
         gather_scales()
@@ -268,8 +302,8 @@ def tile_list_unit_vocoder_gate_kernel(
         load_wg(1, 0)
         gain_sb = kept([P, 2, PACK], F32, "gain_sb")
         nc.sync.dma_start(gain_sb[:], gain.rearrange("(b p t) -> p b t", b=2, t=PACK))
-        load_wf(1, kept([P, 2, KP // 2], I32, "wf_raw1")[:])
         load_wg(1, 1)
+        load_wf(1, kept([P, 2, KP // 2], I32, "wf_raw1")[:])
         wo_w = kept([P, 2, N], I32, "wo_w")
         nc.sync.dma_start(wo_w[:], wo_words.rearrange("a p n i -> p a (n i)").bitcast(I32))
         load_plane(wo_sc, wo_scales)
@@ -282,7 +316,7 @@ def tile_list_unit_vocoder_gate_kernel(
         permute_wf_scales(1)
         gather_words(0, 1)
         gather_words(1, 0)
-        filt(0, 0)
+        filt_first()
         gather_words(1, 1)
         cast_wg(0, 0, True)
         filt(0, 1)
@@ -292,28 +326,29 @@ def tile_list_unit_vocoder_gate_kernel(
         quant_wg(0, 1, Q, Q)
         cast_wg(1, 0, True)
         gate(0, 0, HALF)
-        permute_wf(1)
-        product(0, 0, HALF, tag="wg_raw100")
-        gate(0, HALF, HALF)
-        cast_wg(1, 1, False)
         quant_wg(1, 0)
+        product(0, 0, HALF)
+        cast_wg(1, 1, False)
+        gate(0, HALF, HALF)
+        permute_wf(1)
         interleave_h(0, 0, HALF)
         filt(1, 0, range(0, 4))
-        quant_h(0, 0, HALF)
-        product(0, HALF, HALF)
+        product(0, HALF, HALF, (0,))
         quant_wg(1, 1)
+        product(0, HALF, HALF, (1, 2, 3))
+        quant_h(0, 0, HALF)
         gate(1, 0, 256)
+        filt(1, 1, range(0, 2))
         interleave_h(0, HALF, HALF)
         product(1, 0, 256, (0,))
         quant_h(0, HALF, HALF)
         gate(1, 256, 256)
-        filt(1, 1, range(0, 2))
+        filt(1, 1, range(2, 4))
         product(1, 0, 256, (1, 2, 3))
         interleave_h(1, 0, 256)
         product(1, 256, 256, (0,))
         quant_h(1, 0, 256)
         gate(1, 512, 256)
-        filt(1, 1, range(2, 4))
         product(1, 256, 256, (1, 2, 3))
         project(0, 256)
         interleave_h(1, 256, 256)
@@ -322,16 +357,19 @@ def tile_list_unit_vocoder_gate_kernel(
         gate(1, 768, 128)
         product(1, 512, 256, (1, 2, 3))
         project(256, 256)
+        gate(1, 896, 128)
         interleave_h(1, 512, 256)
         product(1, 768, 128, (0,))
+        sums = open_sums(512, 256)
         quant_h(1, 512, 256)
-        gate(1, 896, 128)
         product(1, 768, 128, (1, 2, 3))
-        project(512, 256)
+        close_sums(sums, 512, 256, ())
         interleave_h(1, 768, 128)
         product(1, 896, 128, (0,))
         quant_h(1, 768, 128)
         product(1, 896, 128, (1, 2, 3))
-        project(768, 128, (0,))
+        project(768, 128, ())
         interleave_h(1, 896, 128)
-        finish(896, 128)
+        sums = open_sums(896, 128)
+        quant_h(1, 896, 128)
+        close_sums(sums, 896, 128, (0,))

@@ -131,7 +131,8 @@ def tile_list_unit_vocoder_gate_kernel(
             if (b, a) not in wg_bf:
                 wg_bf[b, a] = kept([P, PACK * KP], BF16, f"wg_bf{b}{a}")
             dst = wg_bf[b, a][:].rearrange("p (t m j) -> p m j t", t=PACK, j=PACK)[:, m0:m1]
-            src = wg_raw[b, a, 0][:].rearrange("p j (m t) -> p m j t", t=PACK)[:, m0:m1]
+            c0 = max(c for (bb, aa, c) in wg_raw if (bb, aa) == (b, a) and c <= PACK * m0)
+            src = wg_raw[b, a, c0][:].rearrange("p j (m t) -> p m j t", t=PACK)[:, m0 - c0 // PACK : m1 - c0 // PACK]
             if on_vector:
                 nc.vector.tensor_copy(dst, src)
             else:
@@ -298,8 +299,10 @@ def tile_list_unit_vocoder_gate_kernel(
         Q = HALF // 2
         gather_scales()
         load_wg(0, 0, tag="tab_sc")
-        load_wg(0, 1)
-        load_wg(1, 0)
+        load_wg(0, 1, 0, 256)
+        load_wg(0, 1, 256, 256)
+        load_wg(1, 0, 0, 256)
+        load_wg(1, 0, 256, 256)
         gain_sb = kept([P, 2, PACK], F32, "gain_sb")
         nc.sync.dma_start(gain_sb[:], gain.rearrange("(b p t) -> p b t", b=2, t=PACK))
         load_wg(1, 1)
@@ -321,10 +324,13 @@ def tile_list_unit_vocoder_gate_kernel(
         cast_wg(0, 0, True)
         filt(0, 1)
         quant_wg(0, 0)
-        cast_wg(0, 1, True)
-        quant_wg(0, 1, 0, Q)
+        cast_wg(0, 1, True, 0, 64)
+        cast_wg(0, 1, True, 64, P)
+        quant_wg(0, 1, 0, P)
+        quant_wg(0, 1, P, P)
         quant_wg(0, 1, Q, Q)
-        cast_wg(1, 0, True)
+        cast_wg(1, 0, True, 0, 64)
+        cast_wg(1, 0, True, 64, P)
         gate(0, 0, HALF)
         quant_wg(1, 0)
         product(0, 0, HALF)

@@ -190,13 +190,15 @@ def tile_list_unit_vocoder_gate_kernel(
 
         def gate_open():
             banks = [take_bank(HALF) for t in range(PACK)]
-            for t in range(PACK):
+            for t in range(1):
                 mm_g(banks[t][:], 0, t, 0, 0, HALF, True, False)
             return banks
 
         def gate_close(banks):
             for t in range(PACK):
-                mm_g(banks[t][:], 0, t, 1, 0, HALF, False, True)
+                mm_g(banks[t][:], 0, t, 1, 0, HALF, t >= 1, t < 1)
+                if t >= 1:
+                    mm_g(banks[t][:], 0, t, 0, 0, HALF, False, True)
                 sig = work.tile([P, HALF], F32, name="sig", bufs=SIG_BUFS)
                 nc.scalar.activation(sig[:], banks[t][:], ACT.Sigmoid)
                 sig_g[0, 0, t] = sig[:]
@@ -243,10 +245,11 @@ def tile_list_unit_vocoder_gate_kernel(
         h_il = {}
 
         def interleave_h(b, c0, w, copy=nc.vector.tensor_copy):
+            p0 = max(c for (bb, c) in h_planes if bb == b and c <= c0)
             h_il[b, c0] = work.tile([P, PACK * w], BF16, name="h_il", align_bytes=AL)
             copy(
                 h_il[b, c0][:].rearrange("p (c i t) -> p c t i", t=PACK, i=4),
-                h_planes[b, c0][:].rearrange("p t (c i) -> p c t i", i=4),
+                h_planes[b, p0][:, :, c0 - p0 : c0 - p0 + w].rearrange("p t (c i) -> p c t i", i=4),
             )
 
         def quant_h(b, c0, w):
@@ -266,7 +269,7 @@ def tile_list_unit_vocoder_gate_kernel(
             )
 
         def store_pair(sums, i0, c0, w, on_vector):
-            y = work.tile([P, 2, w], F32, name="y_sb", bufs=8)
+            y = work.tile([P, 2, w], F32, name="y_sb", bufs=12)
             for i in (i0, i0 + 1):
                 if on_vector:
                     nc.vector.tensor_scalar(y[:, i - i0, :], sums[i], bo_sb[:, i : i + 1], None, ADD)
@@ -305,8 +308,8 @@ def tile_list_unit_vocoder_gate_kernel(
         load_wg(1, 0, 256, 256)
         gain_sb = kept([P, 2, PACK], F32, "gain_sb")
         nc.sync.dma_start(gain_sb[:], gain.rearrange("(b p t) -> p b t", b=2, t=PACK))
-        load_wg(1, 1)
         load_wf(1, kept([P, 2, KP // 2], I32, "wf_raw1")[:])
+        load_wg(1, 1)
         wo_w = kept([P, 2, N], I32, "wo_w")
         nc.sync.dma_start(wo_w[:], wo_words.rearrange("a p n i -> p a (n i)").bitcast(I32))
         load_plane(wo_sc, wo_scales)
@@ -324,6 +327,7 @@ def tile_list_unit_vocoder_gate_kernel(
         cast_wg(0, 0, True)
         filt(0, 1)
         quant_wg(0, 0)
+        first_gate = gate_open()
         cast_wg(0, 1, True, 0, 64)
         cast_wg(0, 1, True, 64, P)
         quant_wg(0, 1, 0, P)
@@ -331,14 +335,15 @@ def tile_list_unit_vocoder_gate_kernel(
         quant_wg(0, 1, Q, Q)
         cast_wg(1, 0, True, 0, 64)
         cast_wg(1, 0, True, 64, P)
-        gate(0, 0, HALF)
+        gate_close(first_gate)
         quant_wg(1, 0)
         product(0, 0, HALF)
-        cast_wg(1, 1, False)
+        cast_wg(1, 1, False, 24, P)
         gate(0, HALF, HALF)
         permute_wf(1)
         interleave_h(0, 0, HALF)
         filt(1, 0, range(0, 4))
+        cast_wg(1, 1, True, 0, 24)
         product(0, HALF, HALF, (0,))
         quant_wg(1, 1)
         product(0, HALF, HALF, (1, 2, 3))
@@ -364,16 +369,21 @@ def tile_list_unit_vocoder_gate_kernel(
         product(1, 512, 256, (1, 2, 3))
         project(256, 256)
         gate(1, 896, 128)
-        interleave_h(1, 512, 256)
+        interleave_h(1, 512, 128)
         product(1, 768, 128, (0,))
-        sums = open_sums(512, 256)
-        quant_h(1, 512, 256)
-        product(1, 768, 128, (1, 2, 3))
-        close_sums(sums, 512, 256, ())
-        interleave_h(1, 768, 128)
+        sums = open_sums(512, 128)
+        quant_h(1, 512, 128)
+        interleave_h(1, 640, 128)
+        close_sums(sums, 512, 128)
+        product(1, 768, 128, (1,))
+        quant_h(1, 640, 128)
+        product(1, 768, 128, (2, 3))
+        project(640, 128)
         product(1, 896, 128, (0,))
+        interleave_h(1, 768, 128)
+        product(1, 896, 128, (1,))
         quant_h(1, 768, 128)
-        product(1, 896, 128, (1, 2, 3))
+        product(1, 896, 128, (2, 3))
         project(768, 128, ())
         interleave_h(1, 896, 128)
         sums = open_sums(896, 128)

@@ -83,10 +83,10 @@ def tile_list_unit_vocoder_gate_kernel(
                 src = scales.bitcast(I32)[:, r:16:4, :].rearrange("a q c -> q a c")
                 nc.sync.dma_start(plane[r:P:32, :, :], src)
 
+        load_wf(0, kept([P, 2, KP // 2], I32, "wf_raw0", "slot_f")[:])
         load_tab(0)
         load_plane(wf_sc_raw, wf_scales)
         nc.scalar.activation(warm_out[:], warm[:], ACT.Sigmoid)
-        load_wf(0, kept([P, 2, KP // 2], I32, "wf_raw0", "slot_f")[:])
         load_tab(1)
 
         v_w = {}

@@ -20,9 +20,21 @@ ADD = mybir.AluOpType.add
 P = 128
 PACK = 4
 KP = P * PACK
-HALF = 512
-AL = 64
-SIG_BUFS = 4
+HALF = S // 2
+QUARTER = S // 4
+EIGHTH = S // 8
+BANKS = 8
+GROUP = 32
+ROWS = 4
+WORD = 4
+LIST_ROWS = 16
+ALIGN = 64
+RUN = 2
+WF_RUN = 8
+VECTOR_GROUPS = 48
+SIG_BUFS = 5
+H_BUFS = 3
+OUT_BUFS = 12
 
 
 def tile_list_unit_vocoder_gate_kernel(
@@ -35,27 +47,30 @@ def tile_list_unit_vocoder_gate_kernel(
         psum = ctx.enter_context(tc.psum_pool(name="psum", bufs=1))
 
         def kept(shape, dtype, name, tag=""):
-            return keep.tile(shape, dtype, name=name, tag=tag or name, align_bytes=AL)
+            return keep.tile(shape, dtype, name=name, tag=tag or name, align_bytes=ALIGN)
 
         banks_taken = []
 
         def take_bank(w):
-            banks_taken.append(psum.tile([P, w], F32, name=f"bank{len(banks_taken) % 8}"))
+            banks_taken.append(psum.tile([P, w], F32, name=f"bank{len(banks_taken) % BANKS}"))
             return banks_taken[-1]
 
-        offsets = keep.tile([P, S // 16], U16, name="offsets")
+        def retake_bank(back):
+            return psum.tile([P, HALF], F32, name=f"bank{(len(banks_taken) - back) % BANKS}")
+
+        offsets = keep.tile([P, S // LIST_ROWS], U16, name="offsets")
         nc.sync.dma_start(offsets[:], offs)
 
-        tab_sc = kept([P, T // 4], I32, "tab_sc")
-        nc.sync.dma_start(tab_sc[0:32, :], tab_scales.bitcast(I32).rearrange("a q c -> q a c"))
-        wf_sc_raw = kept([P, 2, H // 4], I32, "wf_sc_raw", "slot_s")
+        tab_sc = kept([P, T // WORD], I32, "tab_sc")
+        nc.sync.dma_start(tab_sc[0:GROUP, :], tab_scales.bitcast(I32).rearrange("a q c -> q a c"))
+        wf_sc_raw = kept([P, 2, H // WORD], I32, "wf_sc_raw")
         nc.vector.memset(wf_sc_raw[:], 0)
-        nc.vector.memset(tab_sc[32:64, :], 0)
-        nc.vector.memset(tab_sc[64:128, :], 0)
-        v_pl = kept([P, 2, S // 4], I32, "v_pl")
-        nc.gpsimd.memset(v_pl[:], 0)
+        nc.vector.memset(tab_sc[GROUP : 2 * GROUP, :], 0)
+        nc.vector.memset(tab_sc[2 * GROUP : P, :], 0)
+        v_planes = kept([P, 2, S // WORD], I32, "v_planes")
+        nc.gpsimd.memset(v_planes[:], 0)
 
-        wo_sc = kept([P, 2, N // 4], I32, "wo_sc")
+        wo_sc = kept([P, 2, N // WORD], I32, "wo_sc")
         warm = kept([P, 1], F32, "warm")
         warm_out = kept([P, 1], F32, "warm_out")
         nc.gpsimd.memset(warm[:], 0.0)
@@ -68,24 +83,24 @@ def tile_list_unit_vocoder_gate_kernel(
         def load_tab(a):
             nc.sync.dma_start(tab[a][:], tab_words[a].rearrange("p n i -> p (n i)").bitcast(I32))
 
-        def load_wf(b, dst):
-            wf_raw[b] = dst
+        def load_wf(b):
+            wf_raw[b] = kept([P, 2, KP // 2], I32, f"wf_raw{b}")
             src = wf_words.bitcast(I32).rearrange("a p c -> p a c")
-            nc.sync.dma_start(dst, src[:, :, b * (KP // 2) : (b + 1) * (KP // 2)])
+            nc.sync.dma_start(wf_raw[b][:], src[:, :, b * (KP // 2) : (b + 1) * (KP // 2)])
 
         def load_wg(b, a, c0=0, w=KP, tag=""):
             wg_raw[b, a, c0] = kept([P, PACK, w], F32, f"wg_raw{b}{a}{c0}", tag)
             src = wg[a * KP : (a + 1) * KP, b * KP + c0 : b * KP + c0 + w]
             nc.sync.dma_start(wg_raw[b, a, c0][:], src.rearrange("(p j) c -> p j c", j=PACK))
 
-        def load_plane(plane, scales):
-            for r in range(4):
-                src = scales.bitcast(I32)[:, r:16:4, :].rearrange("a q c -> q a c")
-                nc.sync.dma_start(plane[r:P:32, :, :], src)
+        def load_planes(planes, scales):
+            for r in range(ROWS):
+                src = scales.bitcast(I32)[:, r : ROWS * ROWS : ROWS, :].rearrange("a q c -> q a c")
+                nc.sync.dma_start(planes[r:P:GROUP, :, :], src)
 
-        load_wf(0, kept([P, 2, KP // 2], I32, "wf_raw0", "slot_f")[:])
+        load_wf(0)
         load_tab(0)
-        load_plane(wf_sc_raw, wf_scales)
+        load_planes(wf_sc_raw, wf_scales)
         nc.scalar.activation(warm_out[:], warm[:], ACT.Sigmoid)
         load_tab(1)
 
@@ -98,27 +113,28 @@ def tile_list_unit_vocoder_gate_kernel(
         h_w = [kept([P, S], U32, f"h_w{b}") for b in range(2)]
         h_sc = [kept([P, S], U8, f"h_sc{b}") for b in range(2)]
 
-        def gather_words(a, s, tag=""):
-            v_w[a, s] = kept([P, HALF], U32, f"v_w{a}{s}", tag)
-            cols = slice(s * HALF // 16, (s + 1) * HALF // 16)
+        def gather_words(a, s):
+            v_w[a, s] = kept([P, HALF], U32, f"v_w{a}{s}")
+            cols = slice(s * HALF // LIST_ROWS, (s + 1) * HALF // LIST_ROWS)
             nc.vector.tensor_copy(v_w[a, s][:], tab[a][:].bitcast(U32).indirect(offsets[:, cols]))
 
         def gather_scales():
             nc.vector.tensor_copy(v_sc[:], tab_sc[:].bitcast(U8).indirect(offsets[:]))
-            for q in (0, 2, 1, 3):
-                nc.sync.dma_start(v_pl[32 * q : 32 * q + 4, :, :], v_sc[:].bitcast(I32)[8 * q : 8 * q + 8, :])
+            for g in (0, 2, 1, 3):
+                flat = v_sc[:].bitcast(I32)[2 * ROWS * g : 2 * ROWS * (g + 1), :]
+                nc.sync.dma_start(v_planes[GROUP * g : GROUP * g + ROWS, :, :], flat)
 
-        def v_plane(a, cols):
-            return v_pl[:, a, :].bitcast(U8)[:, cols]
+        def v_plane(a, c0, w):
+            return v_planes[:, a, :].bitcast(U8)[:, c0 : c0 + w]
 
-        def permute_wf(b):
+        def reorder_wf(b):
             nc.vector.tensor_copy(
-                wf_w[b][:].bitcast(U16).rearrange("p a (t m i) -> p a m t i", t=PACK, i=8),
-                wf_raw[b].bitcast(U16).rearrange("p a (m i t) -> p a m t i", t=PACK, i=8),
+                wf_w[b][:].bitcast(U16).rearrange("p a (t m i) -> p a m t i", t=PACK, i=WF_RUN),
+                wf_raw[b][:].bitcast(U16).rearrange("p a (m i t) -> p a m t i", t=PACK, i=WF_RUN),
             )
 
-        def permute_wf_scales(b, tag=""):
-            wf_sc[b] = kept([P, 2, KP], U8, f"wf_sc{b}", tag)
+        def reorder_wf_scales(b):
+            wf_sc[b] = kept([P, 2, KP], U8, f"wf_sc{b}")
             src = wf_sc_raw[:].bitcast(U8)[:, :, b * KP : (b + 1) * KP]
             nc.gpsimd.tensor_copy(
                 wf_sc[b][:].rearrange("p a (t m) -> p a t m", t=PACK),
@@ -127,265 +143,257 @@ def tile_list_unit_vocoder_gate_kernel(
 
         wg_bf = {}
 
-        def cast_wg(b, a, on_vector, m0=0, m1=P):
+        def round_wg(b, a, copy, m0=0, m1=P):
             if (b, a) not in wg_bf:
                 wg_bf[b, a] = kept([P, PACK * KP], BF16, f"wg_bf{b}{a}")
             dst = wg_bf[b, a][:].rearrange("p (t m j) -> p m j t", t=PACK, j=PACK)[:, m0:m1]
             c0 = max(c for (bb, aa, c) in wg_raw if (bb, aa) == (b, a) and c <= PACK * m0)
             src = wg_raw[b, a, c0][:].rearrange("p j (m t) -> p m j t", t=PACK)[:, m0 - c0 // PACK : m1 - c0 // PACK]
-            if on_vector:
-                nc.vector.tensor_copy(dst, src)
-            else:
-                nc.scalar.copy(dst, src)
+            copy(dst, src)
 
-        def quant_wg(b, a, c0=0, w=KP):
+        def quantise_wg(b, a, c0=0, w=KP):
             nc.vector.quantize_mx(
                 out=wg_w[b, a][:, c0 : c0 + w].bitcast(FP8X4),
                 scales=wg_sc[b, a][:, c0 : c0 + w],
                 in_=wg_bf[b, a][:, PACK * c0 : PACK * (c0 + w)],
             )
 
-        tanh_f = {}
+        tanh_f = {(b, s): kept([P, PACK, HALF], F32, f"tanh_f{b}{s}") for b in range(2) for s in range(2)}
+        gained = {(b, s): kept([P, PACK, HALF], F32, f"gained{b}{s}") for b in range(2) for s in range(2)}
 
-        def mm_f(bank, b, s, t, a, up):
+        def apply_gain(b, s, tiles=range(PACK)):
+            for t in tiles:
+                nc.vector.tensor_scalar(gained[b, s][:, t, :], tanh_f[b, s][:, t, :], gain_sb[:, b, t : t + 1], None, MULT)
+
+        def filter_pass(bank, b, s, t, a, start):
             nc.tensor.matmul_mx(
                 out=bank[:],
                 lhsT=wf_w[b][:, a, 2 * P * t : 2 * P * (t + 1)].bitcast(FP4X4),
                 lhsT_scale=wf_sc[b][:, a, P * t : P * (t + 1)],
                 rhs=v_w[a, s][:].bitcast(FP8X4),
-                rhs_scale=v_plane(a, slice(s * HALF, (s + 1) * HALF)),
-                start=(a == 0) == up,
-                stop=(a == 1) == up,
+                rhs_scale=v_plane(a, s * HALF, HALF),
+                start=start,
+                stop=not start,
             )
 
-        def filt(b, s, tiles=range(PACK)):
-            for t in tiles:
-                bank = take_bank(HALF)
-                for a in ((0, 1) if (b, s) == (0, 0) else (1, 0)):
-                    mm_f(bank, b, s, t, a, (b, s) == (0, 0))
-                tanh_f[b, s, t] = work.tile([P, HALF], F32, name="tanh_f", bufs=16)
-                nc.scalar.activation(tanh_f[b, s, t][:], bank[:], ACT.Tanh)
-
-        def filt_first():
+        def filter_first():
             banks = [take_bank(HALF) for t in range(PACK)]
             for a, t in ((0, 0), (0, 1), (1, 0), (1, 1), (0, 2), (1, 2), (0, 3), (1, 3)):
-                mm_f(banks[t], 0, 0, t, a, True)
+                filter_pass(banks[t], 0, 0, t, a, a == 0)
                 if a == 1:
-                    tanh_f[0, 0, t] = work.tile([P, HALF], F32, name="tanh_f", bufs=16)
-                    nc.scalar.activation(tanh_f[0, 0, t][:], banks[t][:], ACT.Tanh)
+                    nc.scalar.activation(tanh_f[0, 0][:, t, :], banks[t][:], ACT.Tanh)
 
-        h_planes = {}
+        def filter_tiles(b, s, tiles=range(PACK), back=0):
+            for t in tiles:
+                bank = retake_bank(back + tiles[0] - t) if back else take_bank(HALF)
+                for a in (1, 0):
+                    filter_pass(bank, b, s, t, a, a == 1)
+                nc.scalar.activation(tanh_f[b, s][:, t, :], bank[:], ACT.Tanh)
+
         sig_g = {}
 
-        def mm_g(dst, b, t, a, c0, w, start, stop):
+        def gate_pass(dst, b, t, a, c0, w, start):
             nc.tensor.matmul_mx(
                 out=dst,
                 lhsT=wg_w[b, a][:, P * t : P * (t + 1)].bitcast(FP8X4),
                 lhsT_scale=wg_sc[b, a][:, P * t : P * (t + 1)],
                 rhs=v_w[a, c0 // HALF][:, c0 % HALF : c0 % HALF + w].bitcast(FP8X4),
-                rhs_scale=v_plane(a, slice(c0, c0 + w)),
+                rhs_scale=v_plane(a, c0, w),
                 start=start,
-                stop=stop,
+                stop=not start,
             )
 
         def gate_open():
-            banks = [take_bank(HALF) for t in range(PACK)]
-            for t in range(1):
-                mm_g(banks[t][:], 0, t, 0, 0, HALF, True, False)
-            return banks
+            bank = take_bank(HALF)
+            gate_pass(bank[:, 0:QUARTER], 0, 0, 0, 0, QUARTER, True)
+            return bank
 
-        def gate_close(banks):
-            for t in range(PACK):
-                mm_g(banks[t][:], 0, t, 1, 0, HALF, t >= 1, t < 1)
-                if t >= 1:
-                    mm_g(banks[t][:], 0, t, 0, 0, HALF, False, True)
-                sig = work.tile([P, HALF], F32, name="sig", bufs=SIG_BUFS)
-                nc.scalar.activation(sig[:], banks[t][:], ACT.Sigmoid)
-                sig_g[0, 0, t] = sig[:]
+        def gate(b, c0, w, opened=None):
+            per_bank = HALF // w
+            sig_g[b, c0] = work.tile([P, PACK, w], F32, name="sig", bufs=SIG_BUFS)
+            for t0 in range(0, PACK, per_bank):
+                bank = opened if opened is not None and t0 == 0 else take_bank(HALF)
+                for t in range(t0, t0 + per_bank):
+                    dst = bank[:, (t - t0) * w : (t - t0 + 1) * w]
+                    if opened is not None and t == 0:
+                        gate_pass(dst, b, t, 1, c0, w, False)
+                    else:
+                        gate_pass(dst, b, t, 1, c0, w, True)
+                        gate_pass(dst, b, t, 0, c0, w, False)
+                dst_sig = sig_g[b, c0][:, t0 : t0 + per_bank, :].rearrange("p t c -> p (t c)")
+                nc.scalar.activation(dst_sig, bank[:], ACT.Sigmoid)
 
-        def gate(b, c0, w, passes=(1, 0), first_tag=None):
-            s, per = c0 // HALF, HALF // w
-            for t0 in range(0, PACK, per):
-                bank = take_bank(HALF)
-                for t in range(t0, t0 + per):
-                    for a in passes:
-                        nc.tensor.matmul_mx(
-                            out=bank[:, (t - t0) * w : (t - t0 + 1) * w],
-                            lhsT=wg_w[b, a][:, P * t : P * (t + 1)].bitcast(FP8X4),
-                            lhsT_scale=wg_sc[b, a][:, P * t : P * (t + 1)],
-                            rhs=v_w[a, s][:, c0 % HALF : c0 % HALF + w].bitcast(FP8X4),
-                            rhs_scale=v_plane(a, slice(c0, c0 + w)),
-                            start=(a == passes[0]),
-                            stop=(a == passes[1]),
-                        )
-                if first_tag and t0 == 0:
-                    sig = kept([P, HALF], F32, "sig_first", first_tag)
-                else:
-                    sig = work.tile([P, HALF], F32, name="sig", bufs=SIG_BUFS)
-                nc.scalar.activation(sig[:], bank[:], ACT.Sigmoid)
-                for t in range(t0, t0 + per):
-                    sig_g[b, c0, t] = sig[:, (t - t0) * w : (t - t0 + 1) * w]
+        h_bf = {}
 
-        def product(b, c0, w, tiles=range(PACK), tag=""):
+        def product(b, c0, w, tag=""):
+            g0 = max(c for (bb, c) in sig_g if bb == b and c <= c0)
+            q0 = c0 - c0 % QUARTER
             if tag:
-                h_planes[b, c0] = kept([P, PACK, w], BF16, "h_planes_first", tag)
-            if (b, c0) not in h_planes:
-                h_planes[b, c0] = work.tile([P, PACK, w], BF16, name="h_planes")
-            planes = h_planes[b, c0]
-            for t in tiles:
-                nc.vector.scalar_tensor_tensor(
-                    planes[:, t, :],
-                    tanh_f[b, c0 // HALF, t][:, c0 % HALF : c0 % HALF + w],
-                    gain_sb[:, b, t : t + 1],
-                    sig_g[b, c0, t],
-                    MULT,
-                    MULT,
-                )
-
-        h_il = {}
-
-        def interleave_h(b, c0, w, copy=nc.vector.tensor_copy):
-            p0 = max(c for (bb, c) in h_planes if bb == b and c <= c0)
-            h_il[b, c0] = work.tile([P, PACK * w], BF16, name="h_il", align_bytes=AL)
-            copy(
-                h_il[b, c0][:].rearrange("p (c i t) -> p c t i", t=PACK, i=4),
-                h_planes[b, p0][:, :, c0 - p0 : c0 - p0 + w].rearrange("p t (c i) -> p c t i", i=4),
+                h_bf[b, q0] = kept([P, PACK * QUARTER], BF16, f"h_bf{b}{q0}", tag)
+            elif (b, q0) not in h_bf:
+                h_bf[b, q0] = work.tile([P, PACK * QUARTER], BF16, name="h_bf", bufs=H_BUFS, align_bytes=ALIGN)
+            nc.vector.tensor_tensor(
+                h_bf[b, q0][:, PACK * (c0 - q0) : PACK * (c0 - q0 + w)].rearrange("p (c i t) -> p c t i", t=PACK, i=RUN),
+                gained[b, c0 // HALF][:, :, c0 % HALF : c0 % HALF + w].rearrange("p t (c i) -> p c t i", i=RUN),
+                sig_g[b, g0][:, :, c0 - g0 : c0 - g0 + w].rearrange("p t (c i) -> p c t i", i=RUN),
+                MULT,
             )
 
-        def quant_h(b, c0, w):
+        def quantise_h(b, c0, w):
+            q0 = c0 - c0 % QUARTER
             nc.vector.quantize_mx(
-                out=h_w[b][:, c0 : c0 + w].bitcast(FP8X4), scales=h_sc[b][:, c0 : c0 + w], in_=h_il[b, c0][:]
+                out=h_w[b][:, c0 : c0 + w].bitcast(FP8X4),
+                scales=h_sc[b][:, c0 : c0 + w],
+                in_=h_bf[b, q0][:, PACK * (c0 - q0) : PACK * (c0 - q0 + w)],
             )
 
-        def mm_y(dst, i, b, c0, w):
+        pairs = range(0, N // P, 2)
+
+        def out_pass(bank, i, b, c0, w, start, stop):
             nc.tensor.matmul_mx(
-                out=dst,
+                out=bank[:, (i % 2) * w : (i % 2 + 1) * w],
                 lhsT=wo_w[:, b, P * i : P * (i + 1)].bitcast(FP8X4),
                 lhsT_scale=wo_sc[:, b, :].bitcast(U8)[:, P * i : P * (i + 1)],
                 rhs=h_w[b][:, c0 : c0 + w].bitcast(FP8X4),
                 rhs_scale=h_sc[b][:, c0 : c0 + w],
-                start=(b == 0),
-                stop=(b == 1),
+                start=start,
+                stop=stop,
             )
 
-        def store_pair(sums, i0, c0, w, on_vector):
-            y = work.tile([P, 2, w], F32, name="y_sb", bufs=12)
+        def store_pair(bank, i0, c0, w, on_vector):
+            y = work.tile([P, 2, w], F32, name="y", bufs=OUT_BUFS)
             for i in (i0, i0 + 1):
+                sums = bank[:, (i - i0) * w : (i - i0 + 1) * w]
                 if on_vector:
-                    nc.vector.tensor_scalar(y[:, i - i0, :], sums[i], bo_sb[:, i : i + 1], None, ADD)
+                    nc.vector.tensor_scalar(y[:, i - i0, :], sums, bo_sb[:, i : i + 1], None, ADD)
                 else:
-                    nc.scalar.activation(y[:, i - i0, :], sums[i], ACT.Identity, bias=bo_sb[:, i : i + 1])
+                    nc.scalar.activation(y[:, i - i0, :], sums, ACT.Identity, bias=bo_sb[:, i : i + 1])
             dst = out[P * i0 : P * (i0 + 2), c0 : c0 + w].rearrange("(i p) c -> p i c", p=P)
             nc.sync.dma_start(dst, y[:])
 
-        def project(c0, w, on_vector=()):
-            for i0 in range(0, N // P, 2):
-                bank = take_bank(2 * w)
-                sums = {i: bank[:, (i - i0) * w : (i - i0 + 1) * w] for i in (i0, i0 + 1)}
+        def project(c0):
+            for i0 in pairs:
+                bank = take_bank(2 * QUARTER)
                 for i in (i0, i0 + 1):
                     for b in range(2):
-                        mm_y(sums[i], i, b, c0, w)
-                store_pair(sums, i0, c0, w, i0 in on_vector)
+                        out_pass(bank, i, b, c0, QUARTER, b == 0, b == 1)
+                store_pair(bank, i0, c0, QUARTER, False)
 
-        def open_sums(c0, w):
-            sums = {i: take_bank(w)[:] for i in range(N // P)}
+        out_banks = {}
+
+        def project_open(c0):
+            out_banks[c0] = {i0: take_bank(2 * EIGHTH) for i0 in pairs}
             for i in range(N // P):
-                mm_y(sums[i], i, 0, c0, w)
-            return sums
+                out_pass(out_banks[c0][i - i % 2], i, 0, c0, EIGHTH, i % 2 == 0, False)
 
-        def close_sums(sums, c0, w, on_vector=()):
-            for i0 in range(0, N // P, 2):
-                for i in (i0, i0 + 1):
-                    mm_y(sums[i], i, 1, c0, w)
-                store_pair(sums, i0, c0, w, i0 in on_vector)
+        def project_close(c0):
+            for i in range(N // P):
+                out_pass(out_banks[c0][i - i % 2], i, 1, c0, EIGHTH, False, i % 2 == 1)
 
-        Q = HALF // 2
+        def store_eighth(c0, i0, on_vector):
+            store_pair(out_banks[c0][i0], i0, c0, EIGHTH, on_vector)
+
+        vector_copy, scalar_copy = nc.vector.tensor_copy, nc.scalar.copy
+        half_cols, half_groups = KP // 2, P // 2
+
         gather_scales()
         load_wg(0, 0, tag="tab_sc")
-        load_wg(0, 1, 0, 256)
-        load_wg(0, 1, 256, 256)
-        load_wg(1, 0, 0, 256)
-        load_wg(1, 0, 256, 256)
+        load_wg(0, 1, 0, half_cols)
+        load_wg(0, 1, half_cols, half_cols)
         gain_sb = kept([P, 2, PACK], F32, "gain_sb")
         nc.sync.dma_start(gain_sb[:], gain.rearrange("(b p t) -> p b t", b=2, t=PACK))
-        load_wf(1, kept([P, 2, KP // 2], I32, "wf_raw1")[:])
+        load_wg(1, 0, 0, half_cols)
+        load_wg(1, 0, half_cols, half_cols)
+        load_wf(1)
         load_wg(1, 1)
         wo_w = kept([P, 2, N], I32, "wo_w")
         nc.sync.dma_start(wo_w[:], wo_words.rearrange("a p n i -> p a (n i)").bitcast(I32))
-        load_plane(wo_sc, wo_scales)
+        load_planes(wo_sc, wo_scales)
         bo_sb = kept([P, N // P], F32, "bo_sb")
         with nc.allow_non_contiguous_dma(reason="one bias value a partition"):
             nc.sync.dma_start(bo_sb[:], bo.rearrange("(i p) -> p i", p=P))
-        permute_wf_scales(0)
+
+        reorder_wf_scales(0)
         gather_words(0, 0)
-        permute_wf(0)
-        permute_wf_scales(1)
+        reorder_wf(0)
+        reorder_wf_scales(1)
         gather_words(0, 1)
         gather_words(1, 0)
-        filt_first()
+        filter_first()
         gather_words(1, 1)
-        cast_wg(0, 0, True)
-        filt(0, 1)
-        quant_wg(0, 0)
+        round_wg(0, 0, vector_copy)
+        filter_tiles(0, 1)
+
+        quantise_wg(0, 0)
         first_gate = gate_open()
-        cast_wg(0, 1, True, 0, 64)
-        cast_wg(0, 1, True, 64, P)
-        quant_wg(0, 1, 0, P)
-        quant_wg(0, 1, P, P)
-        quant_wg(0, 1, Q, Q)
-        cast_wg(1, 0, True, 0, 64)
-        cast_wg(1, 0, True, 64, P)
-        gate_close(first_gate)
-        quant_wg(1, 0)
-        product(0, 0, HALF)
-        cast_wg(1, 1, False, 24, P)
-        gate(0, HALF, HALF)
-        permute_wf(1)
-        interleave_h(0, 0, HALF)
-        filt(1, 0, range(0, 4))
-        cast_wg(1, 1, True, 0, 24)
-        product(0, HALF, HALF, (0,))
-        quant_wg(1, 1)
-        product(0, HALF, HALF, (1, 2, 3))
-        quant_h(0, 0, HALF)
-        gate(1, 0, 256)
-        filt(1, 1, range(0, 2))
-        interleave_h(0, HALF, HALF)
-        product(1, 0, 256, (0,))
-        quant_h(0, HALF, HALF)
-        gate(1, 256, 256)
-        filt(1, 1, range(2, 4))
-        product(1, 0, 256, (1, 2, 3))
-        interleave_h(1, 0, 256)
-        product(1, 256, 256, (0,))
-        quant_h(1, 0, 256)
-        gate(1, 512, 256)
-        product(1, 256, 256, (1, 2, 3))
-        project(0, 256)
-        interleave_h(1, 256, 256)
-        product(1, 512, 256, (0,))
-        quant_h(1, 256, 256)
-        gate(1, 768, 128)
-        product(1, 512, 256, (1, 2, 3))
-        project(256, 256)
-        gate(1, 896, 128)
-        interleave_h(1, 512, 128)
-        product(1, 768, 128, (0,))
-        sums = open_sums(512, 128)
-        quant_h(1, 512, 128)
-        interleave_h(1, 640, 128)
-        close_sums(sums, 512, 128)
-        product(1, 768, 128, (1,))
-        quant_h(1, 640, 128)
-        product(1, 768, 128, (2, 3))
-        project(640, 128)
-        product(1, 896, 128, (0,))
-        interleave_h(1, 768, 128)
-        product(1, 896, 128, (1,))
-        quant_h(1, 768, 128)
-        product(1, 896, 128, (2, 3))
-        project(768, 128, ())
-        interleave_h(1, 896, 128)
-        sums = open_sums(896, 128)
-        quant_h(1, 896, 128)
-        close_sums(sums, 896, 128, (0,))
+        round_wg(0, 1, vector_copy, 0, half_groups)
+        round_wg(0, 1, vector_copy, half_groups, P)
+        quantise_wg(0, 1, 0, 2 * P)
+        quantise_wg(0, 1, 2 * P, 2 * P)
+        apply_gain(0, 0)
+        round_wg(1, 0, vector_copy, 0, half_groups)
+        round_wg(1, 0, vector_copy, half_groups, P)
+
+        gate(0, 0, QUARTER, first_gate)
+        gate(0, QUARTER, QUARTER)
+        product(0, 0, QUARTER)
+        reorder_wf(1)
+        product(0, QUARTER, QUARTER)
+        round_wg(1, 1, scalar_copy, VECTOR_GROUPS, P)
+        gate(0, 2 * QUARTER, QUARTER)
+        gate(0, 3 * QUARTER, QUARTER)
+        quantise_wg(1, 0)
+        round_wg(1, 1, vector_copy, 0, VECTOR_GROUPS)
+        filter_tiles(1, 0)
+        apply_gain(0, 1)
+        quantise_h(0, 0, QUARTER)
+        quantise_wg(1, 1)
+
+        filter_tiles(1, 1, range(0, 1))
+        gate(1, 0, QUARTER)
+        gate(1, QUARTER, QUARTER)
+        filter_tiles(1, 1, range(1, PACK), back=PACK)
+        quantise_h(0, QUARTER, QUARTER)
+        product(0, 2 * QUARTER, QUARTER, tag="wg_bf11")
+        apply_gain(1, 0)
+        quantise_h(0, 2 * QUARTER, QUARTER)
+        product(1, 0, EIGHTH)
+        product(1, EIGHTH, EIGHTH)
+        product(1, 2 * EIGHTH, EIGHTH)
+        quantise_h(1, 0, QUARTER)
+        product(1, 3 * EIGHTH, EIGHTH)
+        project(0)
+        gate(1, 2 * QUARTER, QUARTER)
+        apply_gain(1, 1, range(0, 1))
+        quantise_h(1, QUARTER, QUARTER)
+        product(0, 3 * QUARTER, QUARTER, tag="gained10")
+        gate(1, 6 * EIGHTH, EIGHTH)
+        gate(1, 7 * EIGHTH, EIGHTH)
+        project(QUARTER)
+        apply_gain(1, 1, range(1, PACK))
+        quantise_h(0, 3 * QUARTER, QUARTER)
+
+        product(1, 4 * EIGHTH, EIGHTH)
+        product(1, 5 * EIGHTH, EIGHTH)
+        project_open(4 * EIGHTH)
+        project_open(5 * EIGHTH)
+        quantise_h(1, 4 * EIGHTH, EIGHTH)
+        project_close(4 * EIGHTH)
+        for i0 in pairs:
+            store_eighth(4 * EIGHTH, i0, False)
+        product(1, 6 * EIGHTH, EIGHTH)
+        project_open(6 * EIGHTH)
+        quantise_h(1, 5 * EIGHTH, EIGHTH)
+        project_close(5 * EIGHTH)
+        for i0 in pairs:
+            store_eighth(5 * EIGHTH, i0, False)
+        product(1, 7 * EIGHTH, EIGHTH)
+        quantise_h(1, 6 * EIGHTH, EIGHTH)
+        project_close(6 * EIGHTH)
+        project_open(7 * EIGHTH)
+        store_eighth(6 * EIGHTH, pairs[0], False)
+        quantise_h(1, 7 * EIGHTH, EIGHTH)
+        project_close(7 * EIGHTH)
+        store_eighth(6 * EIGHTH, pairs[1], True)
+        store_eighth(7 * EIGHTH, pairs[0], True)
+        store_eighth(7 * EIGHTH, pairs[1], False)

@@ -31,8 +31,8 @@ LIST_ROWS = 16
 ALIGN = 64
 RUN = 2
 WF_RUN = 8
-VECTOR_GROUPS = 48
-SIG_BUFS = 5
+SCALAR_GAINS = 3
+SIG_BUFS = {"sig_a": 2, "sig_b": 3}
 H_BUFS = 3
 OUT_BUFS = 12
 
@@ -49,14 +49,8 @@ def tile_list_unit_vocoder_gate_kernel(
         def kept(shape, dtype, name, tag=""):
             return keep.tile(shape, dtype, name=name, tag=tag or name, align_bytes=ALIGN)
 
-        banks_taken = []
-
-        def take_bank(w):
-            banks_taken.append(psum.tile([P, w], F32, name=f"bank{len(banks_taken) % BANKS}"))
-            return banks_taken[-1]
-
-        def retake_bank(back):
-            return psum.tile([P, HALF], F32, name=f"bank{(len(banks_taken) - back) % BANKS}")
+        def bank_tile(n, w=HALF):
+            return psum.tile([P, w], F32, name=f"bank{n}")
 
         offsets = keep.tile([P, S // LIST_ROWS], U16, name="offsets")
         nc.sync.dma_start(offsets[:], offs)
@@ -143,13 +137,12 @@ def tile_list_unit_vocoder_gate_kernel(
 
         wg_bf = {}
 
-        def round_wg(b, a, copy, m0=0, m1=P):
+        def round_wg(b, a, t0):
             if (b, a) not in wg_bf:
                 wg_bf[b, a] = kept([P, PACK * KP], BF16, f"wg_bf{b}{a}")
-            dst = wg_bf[b, a][:].rearrange("p (t m j) -> p m j t", t=PACK, j=PACK)[:, m0:m1]
-            c0 = max(c for (bb, aa, c) in wg_raw if (bb, aa) == (b, a) and c <= PACK * m0)
-            src = wg_raw[b, a, c0][:].rearrange("p j (m t) -> p m j t", t=PACK)[:, m0 - c0 // PACK : m1 - c0 // PACK]
-            copy(dst, src)
+            dst = wg_bf[b, a][:].rearrange("p (t m j) -> p m j t", t=PACK, j=PACK)[:, :, :, t0 : t0 + 2]
+            src = wg_raw[b, a, 0][:].rearrange("p j (m t) -> p m j t", t=PACK)[:, :, :, t0 : t0 + 2]
+            nc.vector.tensor_copy(dst, src)
 
         def quantise_wg(b, a, c0=0, w=KP):
             nc.vector.quantize_mx(
@@ -159,11 +152,21 @@ def tile_list_unit_vocoder_gate_kernel(
             )
 
         tanh_f = {(b, s): kept([P, PACK, HALF], F32, f"tanh_f{b}{s}") for b in range(2) for s in range(2)}
-        gained = {(b, s): kept([P, PACK, HALF], F32, f"gained{b}{s}") for b in range(2) for s in range(2)}
+        gained = {}
 
-        def apply_gain(b, s, tiles=range(PACK)):
-            for t in tiles:
+        def apply_gain(b, s, t, tag="", on_scalar=False):
+            if (b, s) not in gained:
+                gained[b, s] = kept([P, PACK, HALF], F32, f"gained{b}{s}", tag)
+            if on_scalar:
+                nc.scalar.activation(gained[b, s][:, t, :], tanh_f[b, s][:, t, :], ACT.Copy, scale=gain_sb[:, b, t : t + 1])
+            else:
                 nc.vector.tensor_scalar(gained[b, s][:, t, :], tanh_f[b, s][:, t, :], gain_sb[:, b, t : t + 1], None, MULT)
+
+        def prepare_wg(b, a):
+            for t0 in (0, 2):
+                round_wg(b, a, t0)
+            for t0 in (0, 2):
+                quantise_wg(b, a, P * t0, 2 * P)
 
         def filter_pass(bank, b, s, t, a, start):
             nc.tensor.matmul_mx(
@@ -177,18 +180,17 @@ def tile_list_unit_vocoder_gate_kernel(
             )
 
         def filter_first():
-            banks = [take_bank(HALF) for t in range(PACK)]
+            banks = [bank_tile(t) for t in range(PACK)]
             for a, t in ((0, 0), (0, 1), (1, 0), (1, 1), (0, 2), (1, 2), (0, 3), (1, 3)):
                 filter_pass(banks[t], 0, 0, t, a, a == 0)
                 if a == 1:
                     nc.scalar.activation(tanh_f[0, 0][:, t, :], banks[t][:], ACT.Tanh)
 
-        def filter_tiles(b, s, tiles=range(PACK), back=0):
-            for t in tiles:
-                bank = retake_bank(back + tiles[0] - t) if back else take_bank(HALF)
-                for a in (1, 0):
-                    filter_pass(bank, b, s, t, a, a == 1)
-                nc.scalar.activation(tanh_f[b, s][:, t, :], bank[:], ACT.Tanh)
+        def filter_tile(b, s, t):
+            bank = bank_tile(PACK * s + t)
+            for a in (1, 0):
+                filter_pass(bank, b, s, t, a, a == 1)
+            nc.scalar.activation(tanh_f[b, s][:, t, :], bank[:], ACT.Tanh)
 
         sig_g = {}
 
@@ -203,24 +205,15 @@ def tile_list_unit_vocoder_gate_kernel(
                 stop=not start,
             )
 
-        def gate_open():
-            bank = take_bank(HALF)
-            gate_pass(bank[:, 0:QUARTER], 0, 0, 0, 0, QUARTER, True)
-            return bank
-
-        def gate(b, c0, w, opened=None):
-            per_bank = HALF // w
-            sig_g[b, c0] = work.tile([P, PACK, w], F32, name="sig", bufs=SIG_BUFS)
-            for t0 in range(0, PACK, per_bank):
-                bank = opened if opened is not None and t0 == 0 else take_bank(HALF)
-                for t in range(t0, t0 + per_bank):
-                    dst = bank[:, (t - t0) * w : (t - t0 + 1) * w]
-                    if opened is not None and t == 0:
-                        gate_pass(dst, b, t, 1, c0, w, False)
-                    else:
-                        gate_pass(dst, b, t, 1, c0, w, True)
-                        gate_pass(dst, b, t, 0, c0, w, False)
-                dst_sig = sig_g[b, c0][:, t0 : t0 + per_bank, :].rearrange("p t c -> p (t c)")
+        def gate(b, c0, bank0, ring):
+            sig_g[b, c0] = work.tile([P, PACK, QUARTER], F32, name=f"sig{b}{c0}", tag=ring, bufs=SIG_BUFS[ring])
+            for t0 in (0, 2):
+                bank = bank_tile(bank0 + t0 // 2)
+                for t in (t0, t0 + 1):
+                    dst = bank[:, (t - t0) * QUARTER : (t - t0 + 1) * QUARTER]
+                    gate_pass(dst, b, t, 1, c0, QUARTER, True)
+                    gate_pass(dst, b, t, 0, c0, QUARTER, False)
+                dst_sig = sig_g[b, c0][:, t0 : t0 + 2, :].rearrange("p t c -> p (t c)")
                 nc.scalar.activation(dst_sig, bank[:], ACT.Sigmoid)
 
         h_bf = {}
@@ -271,40 +264,28 @@ def tile_list_unit_vocoder_gate_kernel(
             dst = out[P * i0 : P * (i0 + 2), c0 : c0 + w].rearrange("(i p) c -> p i c", p=P)
             nc.sync.dma_start(dst, y[:])
 
-        def project(c0):
-            for i0 in pairs:
-                bank = take_bank(2 * QUARTER)
-                for i in (i0, i0 + 1):
-                    for b in range(2):
-                        out_pass(bank, i, b, c0, QUARTER, b == 0, b == 1)
-                store_pair(bank, i0, c0, QUARTER, False)
-
         out_banks = {}
 
-        def project_open(c0):
-            out_banks[c0] = {i0: take_bank(2 * EIGHTH) for i0 in pairs}
+        def project_open(c0, w, bank0):
+            out_banks[c0] = {i0: bank_tile(bank0 + i0 // 2, 2 * w) for i0 in pairs}
             for i in range(N // P):
-                out_pass(out_banks[c0][i - i % 2], i, 0, c0, EIGHTH, i % 2 == 0, False)
+                out_pass(out_banks[c0][i - i % 2], i, 0, c0, w, i % 2 == 0, False)
 
-        def project_close(c0):
+        def project_close(c0, w):
             for i in range(N // P):
-                out_pass(out_banks[c0][i - i % 2], i, 1, c0, EIGHTH, False, i % 2 == 1)
+                out_pass(out_banks[c0][i - i % 2], i, 1, c0, w, False, i % 2 == 1)
 
-        def store_eighth(c0, i0, on_vector):
-            store_pair(out_banks[c0][i0], i0, c0, EIGHTH, on_vector)
-
-        vector_copy, scalar_copy = nc.vector.tensor_copy, nc.scalar.copy
-        half_cols, half_groups = KP // 2, P // 2
+        def store(c0, w, on_vector=()):
+            for i0 in pairs:
+                store_pair(out_banks[c0][i0], i0, c0, w, i0 in on_vector)
 
         gather_scales()
-        load_wg(0, 0, tag="tab_sc")
-        load_wg(0, 1, 0, half_cols)
-        load_wg(0, 1, half_cols, half_cols)
         gain_sb = kept([P, 2, PACK], F32, "gain_sb")
-        nc.sync.dma_start(gain_sb[:], gain.rearrange("(b p t) -> p b t", b=2, t=PACK))
-        load_wg(1, 0, 0, half_cols)
-        load_wg(1, 0, half_cols, half_cols)
+        load_wg(0, 0, tag="tab_sc")
         load_wf(1)
+        nc.sync.dma_start(gain_sb[:], gain.rearrange("(b p t) -> p b t", b=2, t=PACK))
+        load_wg(0, 1)
+        load_wg(1, 0)
         load_wg(1, 1)
         wo_w = kept([P, 2, N], I32, "wo_w")
         nc.sync.dma_start(wo_w[:], wo_words.rearrange("a p n i -> p a (n i)").bitcast(I32))
@@ -321,79 +302,69 @@ def tile_list_unit_vocoder_gate_kernel(
         gather_words(1, 0)
         filter_first()
         gather_words(1, 1)
-        round_wg(0, 0, vector_copy)
-        filter_tiles(0, 1)
+        for t in range(PACK):
+            filter_tile(0, 1, t)
 
-        quantise_wg(0, 0)
-        first_gate = gate_open()
-        round_wg(0, 1, vector_copy, 0, half_groups)
-        round_wg(0, 1, vector_copy, half_groups, P)
-        quantise_wg(0, 1, 0, 2 * P)
-        quantise_wg(0, 1, 2 * P, 2 * P)
-        apply_gain(0, 0)
-        round_wg(1, 0, vector_copy, 0, half_groups)
-        round_wg(1, 0, vector_copy, half_groups, P)
-
-        gate(0, 0, QUARTER, first_gate)
-        gate(0, QUARTER, QUARTER)
-        product(0, 0, QUARTER)
+        prepare_wg(0, 0)
         reorder_wf(1)
+        for t in range(PACK):
+            apply_gain(0, 0, t, "tab_sc")
+            filter_tile(1, 0, t)
+        prepare_wg(0, 1)
+        for t in range(PACK):
+            apply_gain(0, 1, t, "wg_raw010")
+        prepare_wg(1, 0)
+        for t in range(PACK):
+            filter_tile(1, 1, t)
+        prepare_wg(1, 1)
+        for t in range(PACK):
+            apply_gain(1, 0, t, "wg_raw110")
+
+        gate(0, 0, 0, "sig_a")
+        gate(0, QUARTER, 2, "sig_a")
+        gate(1, 0, 4, "sig_b")
+        gate(1, QUARTER, 6, "sig_b")
+        product(0, 0, QUARTER, tag="wg_bf11")
         product(0, QUARTER, QUARTER)
-        round_wg(1, 1, scalar_copy, VECTOR_GROUPS, P)
-        gate(0, 2 * QUARTER, QUARTER)
-        gate(0, 3 * QUARTER, QUARTER)
-        quantise_wg(1, 0)
-        round_wg(1, 1, vector_copy, 0, VECTOR_GROUPS)
-        filter_tiles(1, 0)
-        apply_gain(0, 1)
         quantise_h(0, 0, QUARTER)
-        quantise_wg(1, 1)
-
-        filter_tiles(1, 1, range(0, 1))
-        gate(1, 0, QUARTER)
-        gate(1, QUARTER, QUARTER)
-        filter_tiles(1, 1, range(1, PACK), back=PACK)
+        gate(1, 2 * QUARTER, 0, "sig_b")
+        gate(0, 2 * QUARTER, 4, "sig_a")
+        product(1, 0, QUARTER)
         quantise_h(0, QUARTER, QUARTER)
-        product(0, 2 * QUARTER, QUARTER, tag="wg_bf11")
-        apply_gain(1, 0)
-        quantise_h(0, 2 * QUARTER, QUARTER)
-        product(1, 0, EIGHTH)
-        product(1, EIGHTH, EIGHTH)
-        product(1, 2 * EIGHTH, EIGHTH)
+        project_open(0, QUARTER, 2)
+        for t in range(PACK):
+            apply_gain(1, 1, t, "tab_sc", on_scalar=t >= PACK - SCALAR_GAINS)
+        product(1, QUARTER, QUARTER)
+        gate(0, 3 * QUARTER, 6, "sig_a")
+        project_open(QUARTER, QUARTER, 0)
         quantise_h(1, 0, QUARTER)
-        product(1, 3 * EIGHTH, EIGHTH)
-        project(0)
-        gate(1, 2 * QUARTER, QUARTER)
-        apply_gain(1, 1, range(0, 1))
+        project_close(0, QUARTER)
+        store(0, QUARTER)
+        product(0, 2 * QUARTER, QUARTER)
+        gate(1, 3 * QUARTER, 6, "sig_b")
         quantise_h(1, QUARTER, QUARTER)
-        product(0, 3 * QUARTER, QUARTER, tag="gained10")
-        gate(1, 6 * EIGHTH, EIGHTH)
-        gate(1, 7 * EIGHTH, EIGHTH)
-        project(QUARTER)
-        apply_gain(1, 1, range(1, PACK))
-        quantise_h(0, 3 * QUARTER, QUARTER)
-
+        project_close(QUARTER, QUARTER)
+        store(QUARTER, QUARTER)
         product(1, 4 * EIGHTH, EIGHTH)
+        quantise_h(0, 2 * QUARTER, QUARTER)
         product(1, 5 * EIGHTH, EIGHTH)
-        project_open(4 * EIGHTH)
-        project_open(5 * EIGHTH)
+        project_open(4 * EIGHTH, EIGHTH, 4)
         quantise_h(1, 4 * EIGHTH, EIGHTH)
-        project_close(4 * EIGHTH)
-        for i0 in pairs:
-            store_eighth(4 * EIGHTH, i0, False)
-        product(1, 6 * EIGHTH, EIGHTH)
-        project_open(6 * EIGHTH)
+        project_close(4 * EIGHTH, EIGHTH)
+        store(4 * EIGHTH, EIGHTH)
+        product(0, 3 * QUARTER, QUARTER)
+        project_open(5 * EIGHTH, EIGHTH, 2)
         quantise_h(1, 5 * EIGHTH, EIGHTH)
-        project_close(5 * EIGHTH)
-        for i0 in pairs:
-            store_eighth(5 * EIGHTH, i0, False)
-        product(1, 7 * EIGHTH, EIGHTH)
+        project_close(5 * EIGHTH, EIGHTH)
+        store(5 * EIGHTH, EIGHTH)
+        product(1, 6 * EIGHTH, EIGHTH)
+        quantise_h(0, 3 * QUARTER, QUARTER)
+        project_open(6 * EIGHTH, EIGHTH, 0)
+        project_open(7 * EIGHTH, EIGHTH, 6)
         quantise_h(1, 6 * EIGHTH, EIGHTH)
-        project_close(6 * EIGHTH)
-        project_open(7 * EIGHTH)
-        store_eighth(6 * EIGHTH, pairs[0], False)
+        project_close(6 * EIGHTH, EIGHTH)
+        store(6 * EIGHTH, EIGHTH)
+        product(1, 7 * EIGHTH, EIGHTH)
         quantise_h(1, 7 * EIGHTH, EIGHTH)
-        project_close(7 * EIGHTH)
-        store_eighth(6 * EIGHTH, pairs[1], True)
-        store_eighth(7 * EIGHTH, pairs[0], True)
-        store_eighth(7 * EIGHTH, pairs[1], False)
+        project_close(7 * EIGHTH, EIGHTH)
+        store(7 * EIGHTH, EIGHTH, pairs[:1])

@@ -34,6 +34,7 @@ WF_RUN = 8
 SCALAR_GAINS = 3
 SIG_BUFS = {"sig_a": 2, "sig_b": 3}
 H_BUFS = 3
+WARM_PASSES = 4
 OUT_BUFS = 12
 
 
@@ -144,6 +145,12 @@ def tile_list_unit_vocoder_gate_kernel(
             src = wg_raw[b, a, 0][:].rearrange("p j (m t) -> p m j t", t=PACK)[:, :, :, t0 : t0 + 2]
             nc.vector.tensor_copy(dst, src)
 
+        def round_wg_half(b, a, u):
+            if (b, a) not in wg_bf:
+                wg_bf[b, a] = kept([P, PACK * KP], BF16, f"wg_bf{b}{a}")
+            dst = wg_bf[b, a][:].rearrange("p (t m j) -> p m j t", t=PACK, j=PACK)[:, u * P // 2 : (u + 1) * P // 2]
+            nc.vector.tensor_copy(dst, wg_raw[b, a, u * KP // 2][:].rearrange("p j (m t) -> p m j t", t=PACK))
+
         def quantise_wg(b, a, c0=0, w=KP):
             nc.vector.quantize_mx(
                 out=wg_w[b, a][:, c0 : c0 + w].bitcast(FP8X4),
@@ -179,6 +186,19 @@ def tile_list_unit_vocoder_gate_kernel(
                 stop=not start,
             )
 
+        def warm_tensor():
+            bank = bank_tile(BANKS - 1)
+            for a in range(WARM_PASSES):
+                nc.tensor.matmul_mx(
+                    out=bank[:],
+                    lhsT=wf_raw[0][:, 0, :].bitcast(U8)[:, 0 : 2 * P].bitcast(FP4X4),
+                    lhsT_scale=wf_sc_raw[:, 0, :].bitcast(U8)[:, 0:P],
+                    rhs=tab[0][:, 0:HALF].bitcast(FP8X4),
+                    rhs_scale=wf_sc_raw[:, 0, :].bitcast(U8)[:, 0:HALF],
+                    start=True,
+                    stop=True,
+                )
+
         def filter_first():
             banks = [bank_tile(t) for t in range(PACK)]
             for a, t in ((0, 0), (0, 1), (1, 0), (1, 1), (0, 2), (1, 2), (0, 3), (1, 3)):
@@ -205,15 +225,16 @@ def tile_list_unit_vocoder_gate_kernel(
                 stop=not start,
             )
 
-        def gate(b, c0, bank0, ring):
-            sig_g[b, c0] = work.tile([P, PACK, QUARTER], F32, name=f"sig{b}{c0}", tag=ring, bufs=SIG_BUFS[ring])
-            for t0 in (0, 2):
-                bank = bank_tile(bank0 + t0 // 2)
-                for t in (t0, t0 + 1):
-                    dst = bank[:, (t - t0) * QUARTER : (t - t0 + 1) * QUARTER]
-                    gate_pass(dst, b, t, 1, c0, QUARTER, True)
-                    gate_pass(dst, b, t, 0, c0, QUARTER, False)
-                dst_sig = sig_g[b, c0][:, t0 : t0 + 2, :].rearrange("p t c -> p (t c)")
+        def gate(b, c0, w, banks, ring):
+            per_bank = HALF // w
+            sig_g[b, c0] = work.tile([P, PACK, w], F32, name=f"sig{b}{c0}", tag=ring, bufs=SIG_BUFS[ring])
+            for t0 in range(0, PACK, per_bank):
+                bank = bank_tile(banks[t0 // per_bank])
+                for t in range(t0, t0 + per_bank):
+                    dst = bank[:, (t - t0) * w : (t - t0 + 1) * w]
+                    gate_pass(dst, b, t, 1, c0, w, True)
+                    gate_pass(dst, b, t, 0, c0, w, False)
+                dst_sig = sig_g[b, c0][:, t0 : t0 + per_bank, :].rearrange("p t c -> p (t c)")
                 nc.scalar.activation(dst_sig, bank[:], ACT.Sigmoid)
 
         h_bf = {}
@@ -240,11 +261,12 @@ def tile_list_unit_vocoder_gate_kernel(
                 in_=h_bf[b, q0][:, PACK * (c0 - q0) : PACK * (c0 - q0 + w)],
             )
 
-        pairs = range(0, N // P, 2)
+        out_tiles = range(N // P)
+        out_sums = {}
 
-        def out_pass(bank, i, b, c0, w, start, stop):
+        def out_pass(i, b, c0, w, start, stop):
             nc.tensor.matmul_mx(
-                out=bank[:, (i % 2) * w : (i % 2 + 1) * w],
+                out=out_sums[c0, i],
                 lhsT=wo_w[:, b, P * i : P * (i + 1)].bitcast(FP8X4),
                 lhsT_scale=wo_sc[:, b, :].bitcast(U8)[:, P * i : P * (i + 1)],
                 rhs=h_w[b][:, c0 : c0 + w].bitcast(FP8X4),
@@ -253,35 +275,36 @@ def tile_list_unit_vocoder_gate_kernel(
                 stop=stop,
             )
 
-        def store_pair(bank, i0, c0, w, on_vector):
-            y = work.tile([P, 2, w], F32, name="y", bufs=OUT_BUFS)
-            for i in (i0, i0 + 1):
-                sums = bank[:, (i - i0) * w : (i - i0 + 1) * w]
+        def project_open(c0, w, banks):
+            per_bank = len(out_tiles) // len(banks)
+            for i in out_tiles:
+                if i % per_bank == 0:
+                    bank = bank_tile(banks[i // per_bank], per_bank * w)
+                out_sums[c0, i] = bank[:, (i % per_bank) * w : (i % per_bank + 1) * w]
+                out_pass(i, 0, c0, w, i % per_bank == 0, False)
+
+        def project_close(c0, w, per_bank=2):
+            for i in out_tiles:
+                out_pass(i, 1, c0, w, False, i % per_bank == per_bank - 1)
+
+        def store(c0, w, tiles, on_vector=False, tag=""):
+            if tag:
+                y = kept([P, len(out_tiles[tiles]), w], F32, f"y{c0}", tag)
+            else:
+                y = work.tile([P, len(out_tiles[tiles]), w], F32, name="y", bufs=OUT_BUFS)
+            for n, i in enumerate(out_tiles[tiles]):
                 if on_vector:
-                    nc.vector.tensor_scalar(y[:, i - i0, :], sums, bo_sb[:, i : i + 1], None, ADD)
+                    nc.vector.tensor_scalar(y[:, n, :], out_sums[c0, i], bo_sb[:, i : i + 1], None, ADD)
                 else:
-                    nc.scalar.activation(y[:, i - i0, :], sums, ACT.Identity, bias=bo_sb[:, i : i + 1])
-            dst = out[P * i0 : P * (i0 + 2), c0 : c0 + w].rearrange("(i p) c -> p i c", p=P)
-            nc.sync.dma_start(dst, y[:])
+                    nc.scalar.activation(y[:, n, :], out_sums[c0, i], ACT.Identity, bias=bo_sb[:, i : i + 1])
+            nc.sync.dma_start(out[:, c0 : c0 + w].rearrange("(i p) c -> p i c", p=P)[:, tiles, :], y[:])
 
-        out_banks = {}
-
-        def project_open(c0, w, bank0):
-            out_banks[c0] = {i0: bank_tile(bank0 + i0 // 2, 2 * w) for i0 in pairs}
-            for i in range(N // P):
-                out_pass(out_banks[c0][i - i % 2], i, 0, c0, w, i % 2 == 0, False)
-
-        def project_close(c0, w):
-            for i in range(N // P):
-                out_pass(out_banks[c0][i - i % 2], i, 1, c0, w, False, i % 2 == 1)
-
-        def store(c0, w, on_vector=()):
-            for i0 in pairs:
-                store_pair(out_banks[c0][i0], i0, c0, w, i0 in on_vector)
+        low, high, even, odd = slice(0, 2), slice(2, 4), slice(0, 4, 2), slice(1, 4, 2)
 
         gather_scales()
         gain_sb = kept([P, 2, PACK], F32, "gain_sb")
-        load_wg(0, 0, tag="tab_sc")
+        load_wg(0, 0, 0, KP // 2, tag="tab_sc")
+        load_wg(0, 0, KP // 2, KP // 2)
         load_wf(1)
         nc.sync.dma_start(gain_sb[:], gain.rearrange("(b p t) -> p b t", b=2, t=PACK))
         load_wg(0, 1)
@@ -297,6 +320,7 @@ def tile_list_unit_vocoder_gate_kernel(
         reorder_wf_scales(0)
         gather_words(0, 0)
         reorder_wf(0)
+        warm_tensor()
         reorder_wf_scales(1)
         gather_words(0, 1)
         gather_words(1, 0)
@@ -305,10 +329,12 @@ def tile_list_unit_vocoder_gate_kernel(
         for t in range(PACK):
             filter_tile(0, 1, t)
 
-        prepare_wg(0, 0)
+        round_wg_half(0, 0, 0)
+        round_wg_half(0, 0, 1)
         reorder_wf(1)
+        quantise_wg(0, 0)
         for t in range(PACK):
-            apply_gain(0, 0, t, "tab_sc")
+            apply_gain(0, 0, t, "wg_raw00256")
             filter_tile(1, 0, t)
         prepare_wg(0, 1)
         for t in range(PACK):
@@ -320,51 +346,52 @@ def tile_list_unit_vocoder_gate_kernel(
         for t in range(PACK):
             apply_gain(1, 0, t, "wg_raw110")
 
-        gate(0, 0, 0, "sig_a")
-        gate(0, QUARTER, 2, "sig_a")
-        gate(1, 0, 4, "sig_b")
-        gate(1, QUARTER, 6, "sig_b")
+        gate(0, 0, QUARTER, (0, 1), "sig_a")
+        gate(0, QUARTER, QUARTER, (2, 3), "sig_a")
+        gate(1, 0, QUARTER, (4, 5), "sig_b")
+        gate(1, QUARTER, QUARTER, (6, 7), "sig_b")
         product(0, 0, QUARTER, tag="wg_bf11")
         product(0, QUARTER, QUARTER)
         quantise_h(0, 0, QUARTER)
-        gate(1, 2 * QUARTER, 0, "sig_b")
-        gate(0, 2 * QUARTER, 4, "sig_a")
+        gate(1, 2 * QUARTER, QUARTER, (0, 1), "sig_b")
+        gate(0, 2 * QUARTER, QUARTER, (4, 5), "sig_a")
         product(1, 0, QUARTER)
         quantise_h(0, QUARTER, QUARTER)
-        project_open(0, QUARTER, 2)
-        for t in range(PACK):
-            apply_gain(1, 1, t, "tab_sc", on_scalar=t >= PACK - SCALAR_GAINS)
-        product(1, QUARTER, QUARTER)
-        gate(0, 3 * QUARTER, 6, "sig_a")
-        project_open(QUARTER, QUARTER, 0)
+        project_open(0, QUARTER, (2, 3))
         quantise_h(1, 0, QUARTER)
         project_close(0, QUARTER)
-        store(0, QUARTER)
-        product(0, 2 * QUARTER, QUARTER)
-        gate(1, 3 * QUARTER, 6, "sig_b")
+        product(1, QUARTER, QUARTER)
+        for t in range(PACK):
+            apply_gain(1, 1, t, "wg_raw00256", on_scalar=t >= PACK - SCALAR_GAINS)
+        store(0, QUARTER, low)
+        store(0, QUARTER, high)
+        gate(0, 3 * QUARTER, QUARTER, (6, 7), "sig_a")
+        project_open(QUARTER, QUARTER, (0, 1))
         quantise_h(1, QUARTER, QUARTER)
         project_close(QUARTER, QUARTER)
-        store(QUARTER, QUARTER)
-        product(1, 4 * EIGHTH, EIGHTH)
+        store(QUARTER, QUARTER, low)
+        gate(1, 6 * EIGHTH, EIGHTH, (2,), "sig_b")
+        store(QUARTER, QUARTER, high)
+        gate(1, 7 * EIGHTH, EIGHTH, (3,), "sig_b")
+        product(0, 2 * QUARTER, QUARTER)
+        product(1, 2 * QUARTER, QUARTER)
         quantise_h(0, 2 * QUARTER, QUARTER)
-        product(1, 5 * EIGHTH, EIGHTH)
-        project_open(4 * EIGHTH, EIGHTH, 4)
-        quantise_h(1, 4 * EIGHTH, EIGHTH)
-        project_close(4 * EIGHTH, EIGHTH)
-        store(4 * EIGHTH, EIGHTH)
+        project_open(2 * QUARTER, QUARTER, (4, 5))
+        quantise_h(1, 2 * QUARTER, QUARTER)
+        project_close(2 * QUARTER, QUARTER)
+        for i in out_tiles:
+            store(2 * QUARTER, QUARTER, slice(i, i + 1))
         product(0, 3 * QUARTER, QUARTER)
-        project_open(5 * EIGHTH, EIGHTH, 2)
-        quantise_h(1, 5 * EIGHTH, EIGHTH)
-        project_close(5 * EIGHTH, EIGHTH)
-        store(5 * EIGHTH, EIGHTH)
-        product(1, 6 * EIGHTH, EIGHTH)
+        product(1, 6 * EIGHTH, EIGHTH, tag="h_last")
         quantise_h(0, 3 * QUARTER, QUARTER)
-        project_open(6 * EIGHTH, EIGHTH, 0)
-        project_open(7 * EIGHTH, EIGHTH, 6)
+        project_open(6 * EIGHTH, EIGHTH, (6, 7))
         quantise_h(1, 6 * EIGHTH, EIGHTH)
         project_close(6 * EIGHTH, EIGHTH)
-        store(6 * EIGHTH, EIGHTH)
+        project_open(7 * EIGHTH, EIGHTH, (0, 1, 2, 3))
+        store(6 * EIGHTH, EIGHTH, low)
         product(1, 7 * EIGHTH, EIGHTH)
         quantise_h(1, 7 * EIGHTH, EIGHTH)
-        project_close(7 * EIGHTH, EIGHTH)
-        store(7 * EIGHTH, EIGHTH, pairs[:1])
+        project_close(7 * EIGHTH, EIGHTH, 1)
+        store(6 * EIGHTH, EIGHTH, high, True, "h_last")
+        store(7 * EIGHTH, EIGHTH, even)
+        store(7 * EIGHTH, EIGHTH, odd, True)

@@ -161,13 +161,15 @@ def tile_list_unit_vocoder_gate_kernel(
         tanh_f = {(b, s): kept([P, PACK, HALF], F32, f"tanh_f{b}{s}") for b in range(2) for s in range(2)}
         gained = {}
 
-        def apply_gain(b, s, t, tag="", on_scalar=False):
+        def apply_gain(b, s, t, tag="", on_scalar=False, factor=None):
             if (b, s) not in gained:
                 gained[b, s] = kept([P, PACK, HALF], F32, f"gained{b}{s}", tag)
+            if factor is None:
+                factor = gain_sb[:, b, t : t + 1]
             if on_scalar:
-                nc.scalar.activation(gained[b, s][:, t, :], tanh_f[b, s][:, t, :], ACT.Copy, scale=gain_sb[:, b, t : t + 1])
+                nc.scalar.activation(gained[b, s][:, t, :], tanh_f[b, s][:, t, :], ACT.Copy, scale=factor)
             else:
-                nc.vector.tensor_scalar(gained[b, s][:, t, :], tanh_f[b, s][:, t, :], gain_sb[:, b, t : t + 1], None, MULT)
+                nc.vector.tensor_scalar(gained[b, s][:, t, :], tanh_f[b, s][:, t, :], factor, None, MULT)
 
         def prepare_wg(b, a):
             for t0 in (0, 2):
@@ -304,6 +306,9 @@ def tile_list_unit_vocoder_gate_kernel(
         gather_scales()
         gain_sb = kept([P, 2, PACK], F32, "gain_sb")
         load_wg(0, 0, 0, KP // 2, tag="tab_sc")
+        gain_first = kept([P, 1], F32, "gain_first")
+        with nc.allow_non_contiguous_dma(reason="one gain value a partition"):
+            nc.sync.dma_start(gain_first[:], gain.rearrange("(b p t) -> p b t", b=2, t=PACK)[:, 0, 0:1])
         load_wg(0, 0, KP // 2, KP // 2)
         load_wf(1)
         nc.sync.dma_start(gain_sb[:], gain.rearrange("(b p t) -> p b t", b=2, t=PACK))
@@ -330,11 +335,13 @@ def tile_list_unit_vocoder_gate_kernel(
             filter_tile(0, 1, t)
 
         round_wg_half(0, 0, 0)
+        apply_gain(0, 0, 0, factor=gain_first[:])
         round_wg_half(0, 0, 1)
         reorder_wf(1)
         quantise_wg(0, 0)
+        for t in range(1, PACK):
+            apply_gain(0, 0, t)
         for t in range(PACK):
-            apply_gain(0, 0, t, "wg_raw00256")
             filter_tile(1, 0, t)
         prepare_wg(0, 1)
         for t in range(PACK):
@@ -342,41 +349,43 @@ def tile_list_unit_vocoder_gate_kernel(
         prepare_wg(1, 0)
         for t in range(PACK):
             filter_tile(1, 1, t)
+        for t in range(PACK - SCALAR_GAINS):
+            apply_gain(1, 1, t, "wg_raw100")
         prepare_wg(1, 1)
         for t in range(PACK):
             apply_gain(1, 0, t, "wg_raw110")
 
         gate(0, 0, QUARTER, (0, 1), "sig_a")
         gate(0, QUARTER, QUARTER, (2, 3), "sig_a")
-        gate(1, 0, QUARTER, (4, 5), "sig_b")
-        gate(1, QUARTER, QUARTER, (6, 7), "sig_b")
+        for t in range(PACK - SCALAR_GAINS, PACK):
+            apply_gain(1, 1, t, on_scalar=True)
+        gate(1, 0, QUARTER, (6, 7), "sig_b")
+        gate(1, QUARTER, QUARTER, (0, 1), "sig_b")
         product(0, 0, QUARTER, tag="wg_bf11")
         product(0, QUARTER, QUARTER)
         quantise_h(0, 0, QUARTER)
-        gate(1, 2 * QUARTER, QUARTER, (0, 1), "sig_b")
         gate(0, 2 * QUARTER, QUARTER, (4, 5), "sig_a")
+        gate(1, 2 * QUARTER, QUARTER, (2, 3), "sig_b")
         product(1, 0, QUARTER)
         quantise_h(0, QUARTER, QUARTER)
-        project_open(0, QUARTER, (2, 3))
+        project_open(0, QUARTER, (0, 1))
         quantise_h(1, 0, QUARTER)
         project_close(0, QUARTER)
         product(1, QUARTER, QUARTER)
-        for t in range(PACK):
-            apply_gain(1, 1, t, "wg_raw00256", on_scalar=t >= PACK - SCALAR_GAINS)
+        gate(0, 3 * QUARTER, QUARTER, (6, 7), "sig_a")
         store(0, QUARTER, low)
         store(0, QUARTER, high)
-        gate(0, 3 * QUARTER, QUARTER, (6, 7), "sig_a")
-        project_open(QUARTER, QUARTER, (0, 1))
+        project_open(QUARTER, QUARTER, (2, 3))
+        product(0, 2 * QUARTER, QUARTER)
         quantise_h(1, QUARTER, QUARTER)
         project_close(QUARTER, QUARTER)
         store(QUARTER, QUARTER, low)
-        gate(1, 6 * EIGHTH, EIGHTH, (2,), "sig_b")
+        gate(1, 6 * EIGHTH, EIGHTH, (4,), "sig_b")
         store(QUARTER, QUARTER, high)
-        gate(1, 7 * EIGHTH, EIGHTH, (3,), "sig_b")
-        product(0, 2 * QUARTER, QUARTER)
+        gate(1, 7 * EIGHTH, EIGHTH, (5,), "sig_b")
         product(1, 2 * QUARTER, QUARTER)
         quantise_h(0, 2 * QUARTER, QUARTER)
-        project_open(2 * QUARTER, QUARTER, (4, 5))
+        project_open(2 * QUARTER, QUARTER, (6, 7))
         quantise_h(1, 2 * QUARTER, QUARTER)
         project_close(2 * QUARTER, QUARTER)
         for i in out_tiles:
@@ -384,10 +393,10 @@ def tile_list_unit_vocoder_gate_kernel(
         product(0, 3 * QUARTER, QUARTER)
         product(1, 6 * EIGHTH, EIGHTH, tag="h_last")
         quantise_h(0, 3 * QUARTER, QUARTER)
-        project_open(6 * EIGHTH, EIGHTH, (6, 7))
+        project_open(6 * EIGHTH, EIGHTH, (0, 1))
         quantise_h(1, 6 * EIGHTH, EIGHTH)
         project_close(6 * EIGHTH, EIGHTH)
-        project_open(7 * EIGHTH, EIGHTH, (0, 1, 2, 3))
+        project_open(7 * EIGHTH, EIGHTH, (2, 3, 4, 5))
         store(6 * EIGHTH, EIGHTH, low)
         product(1, 7 * EIGHTH, EIGHTH)
         quantise_h(1, 7 * EIGHTH, EIGHTH)

@@ -34,7 +34,7 @@ WF_RUN = 8
 SCALAR_GAINS = 3
 SIG_BUFS = {"sig_a": 2, "sig_b": 3}
 H_BUFS = 3
-WARM_PASSES = 4
+WARM_PASSES = (4, 2)
 OUT_BUFS = 12
 
 
@@ -87,6 +87,12 @@ def tile_list_unit_vocoder_gate_kernel(
             wg_raw[b, a, c0] = kept([P, PACK, w], F32, f"wg_raw{b}{a}{c0}", tag)
             src = wg[a * KP : (a + 1) * KP, b * KP + c0 : b * KP + c0 + w]
             nc.sync.dma_start(wg_raw[b, a, c0][:], src.rearrange("(p j) c -> p j c", j=PACK))
+
+        gain_sb = {}
+
+        def load_gain(b):
+            gain_sb[b] = kept([P, PACK], F32, f"gain_sb{b}")
+            nc.sync.dma_start(gain_sb[b][:], gain[b * KP : (b + 1) * KP].rearrange("(p t) -> p t", t=PACK))
 
         def load_planes(planes, scales):
             for r in range(ROWS):
@@ -161,15 +167,13 @@ def tile_list_unit_vocoder_gate_kernel(
         tanh_f = {(b, s): kept([P, PACK, HALF], F32, f"tanh_f{b}{s}") for b in range(2) for s in range(2)}
         gained = {}
 
-        def apply_gain(b, s, t, tag="", on_scalar=False, factor=None):
+        def apply_gain(b, s, t, tag="", on_scalar=False):
             if (b, s) not in gained:
                 gained[b, s] = kept([P, PACK, HALF], F32, f"gained{b}{s}", tag)
-            if factor is None:
-                factor = gain_sb[:, b, t : t + 1]
             if on_scalar:
-                nc.scalar.activation(gained[b, s][:, t, :], tanh_f[b, s][:, t, :], ACT.Copy, scale=factor)
+                nc.scalar.activation(gained[b, s][:, t, :], tanh_f[b, s][:, t, :], ACT.Copy, scale=gain_sb[b][:, t : t + 1])
             else:
-                nc.vector.tensor_scalar(gained[b, s][:, t, :], tanh_f[b, s][:, t, :], factor, None, MULT)
+                nc.vector.tensor_scalar(gained[b, s][:, t, :], tanh_f[b, s][:, t, :], gain_sb[b][:, t : t + 1], None, MULT)
 
         def prepare_wg(b, a):
             for t0 in (0, 2):
@@ -188,14 +192,14 @@ def tile_list_unit_vocoder_gate_kernel(
                 stop=not start,
             )
 
-        def warm_tensor():
+        def warm_tensor(words, passes):
             bank = bank_tile(BANKS - 1)
-            for a in range(WARM_PASSES):
+            for n in range(passes):
                 nc.tensor.matmul_mx(
                     out=bank[:],
                     lhsT=wf_raw[0][:, 0, :].bitcast(U8)[:, 0 : 2 * P].bitcast(FP4X4),
                     lhsT_scale=wf_sc_raw[:, 0, :].bitcast(U8)[:, 0:P],
-                    rhs=tab[0][:, 0:HALF].bitcast(FP8X4),
+                    rhs=words.bitcast(FP8X4),
                     rhs_scale=wf_sc_raw[:, 0, :].bitcast(U8)[:, 0:HALF],
                     start=True,
                     stop=True,
@@ -285,6 +289,15 @@ def tile_list_unit_vocoder_gate_kernel(
                 out_sums[c0, i] = bank[:, (i % per_bank) * w : (i % per_bank + 1) * w]
                 out_pass(i, 0, c0, w, i % per_bank == 0, False)
 
+        def project(c0, w, banks):
+            per_bank = len(out_tiles) // len(banks)
+            for i in out_tiles:
+                if i % per_bank == 0:
+                    bank = bank_tile(banks[i // per_bank], per_bank * w)
+                out_sums[c0, i] = bank[:, (i % per_bank) * w : (i % per_bank + 1) * w]
+                out_pass(i, 1, c0, w, True, False)
+                out_pass(i, 0, c0, w, False, True)
+
         def project_close(c0, w, per_bank=2):
             for i in out_tiles:
                 out_pass(i, 1, c0, w, False, i % per_bank == per_bank - 1)
@@ -304,15 +317,12 @@ def tile_list_unit_vocoder_gate_kernel(
         low, high, even, odd = slice(0, 2), slice(2, 4), slice(0, 4, 2), slice(1, 4, 2)
 
         gather_scales()
-        gain_sb = kept([P, 2, PACK], F32, "gain_sb")
         load_wg(0, 0, 0, KP // 2, tag="tab_sc")
-        gain_first = kept([P, 1], F32, "gain_first")
-        with nc.allow_non_contiguous_dma(reason="one gain value a partition"):
-            nc.sync.dma_start(gain_first[:], gain.rearrange("(b p t) -> p b t", b=2, t=PACK)[:, 0, 0:1])
         load_wg(0, 0, KP // 2, KP // 2)
         load_wf(1)
-        nc.sync.dma_start(gain_sb[:], gain.rearrange("(b p t) -> p b t", b=2, t=PACK))
+        load_gain(0)
         load_wg(0, 1)
+        load_gain(1)
         load_wg(1, 0)
         load_wg(1, 1)
         wo_w = kept([P, 2, N], I32, "wo_w")
@@ -325,9 +335,10 @@ def tile_list_unit_vocoder_gate_kernel(
         reorder_wf_scales(0)
         gather_words(0, 0)
         reorder_wf(0)
-        warm_tensor()
+        warm_tensor(tab[0][:, 0:HALF], WARM_PASSES[0])
         reorder_wf_scales(1)
         gather_words(0, 1)
+        warm_tensor(v_w[0, 1][:], WARM_PASSES[1])
         gather_words(1, 0)
         filter_first()
         gather_words(1, 1)
@@ -335,30 +346,28 @@ def tile_list_unit_vocoder_gate_kernel(
             filter_tile(0, 1, t)
 
         round_wg_half(0, 0, 0)
-        apply_gain(0, 0, 0, factor=gain_first[:])
         round_wg_half(0, 0, 1)
         reorder_wf(1)
         quantise_wg(0, 0)
-        for t in range(1, PACK):
-            apply_gain(0, 0, t)
         for t in range(PACK):
-            filter_tile(1, 0, t)
+            apply_gain(0, 0, t, "wg_raw00256")
+        for t in range(PACK):
+            apply_gain(0, 1, t)
         prepare_wg(0, 1)
         for t in range(PACK):
-            apply_gain(0, 1, t, "wg_raw010")
+            filter_tile(1, 0, t)
+            if t < PACK - 1:
+                apply_gain(1, 0, t, on_scalar=t > 0)
         prepare_wg(1, 0)
         for t in range(PACK):
             filter_tile(1, 1, t)
-        for t in range(PACK - SCALAR_GAINS):
-            apply_gain(1, 1, t, "wg_raw100")
         prepare_wg(1, 1)
         for t in range(PACK):
-            apply_gain(1, 0, t, "wg_raw110")
+            apply_gain(1, 1, t, "wg_raw110")
 
         gate(0, 0, QUARTER, (0, 1), "sig_a")
         gate(0, QUARTER, QUARTER, (2, 3), "sig_a")
-        for t in range(PACK - SCALAR_GAINS, PACK):
-            apply_gain(1, 1, t, on_scalar=True)
+        apply_gain(1, 0, PACK - 1, on_scalar=True)
         gate(1, 0, QUARTER, (6, 7), "sig_b")
         gate(1, QUARTER, QUARTER, (0, 1), "sig_b")
         product(0, 0, QUARTER, tag="wg_bf11")
@@ -375,17 +384,16 @@ def tile_list_unit_vocoder_gate_kernel(
         gate(0, 3 * QUARTER, QUARTER, (6, 7), "sig_a")
         store(0, QUARTER, low)
         store(0, QUARTER, high)
-        project_open(QUARTER, QUARTER, (2, 3))
         product(0, 2 * QUARTER, QUARTER)
         quantise_h(1, QUARTER, QUARTER)
-        project_close(QUARTER, QUARTER)
+        project(QUARTER, QUARTER, (2, 3))
         store(QUARTER, QUARTER, low)
         gate(1, 6 * EIGHTH, EIGHTH, (4,), "sig_b")
         store(QUARTER, QUARTER, high)
-        gate(1, 7 * EIGHTH, EIGHTH, (5,), "sig_b")
+        gate(1, 7 * EIGHTH, EIGHTH, (6,), "sig_b")
         product(1, 2 * QUARTER, QUARTER)
         quantise_h(0, 2 * QUARTER, QUARTER)
-        project_open(2 * QUARTER, QUARTER, (6, 7))
+        project_open(2 * QUARTER, QUARTER, (5, 7))
         quantise_h(1, 2 * QUARTER, QUARTER)
         project_close(2 * QUARTER, QUARTER)
         for i in out_tiles:
@@ -396,7 +404,7 @@ def tile_list_unit_vocoder_gate_kernel(
         project_open(6 * EIGHTH, EIGHTH, (0, 1))
         quantise_h(1, 6 * EIGHTH, EIGHTH)
         project_close(6 * EIGHTH, EIGHTH)
-        project_open(7 * EIGHTH, EIGHTH, (2, 3, 4, 5))
+        project_open(7 * EIGHTH, EIGHTH, (2, 3, 4, 6))
         store(6 * EIGHTH, EIGHTH, low)
         product(1, 7 * EIGHTH, EIGHTH)
         quantise_h(1, 7 * EIGHTH, EIGHTH)

@@ -23,7 +23,6 @@ KP = P * PACK
 HALF = S // 2
 QUARTER = S // 4
 EIGHTH = S // 8
-BANKS = 8
 GROUP = 32
 ROWS = 4
 WORD = 4
@@ -31,10 +30,10 @@ LIST_ROWS = 16
 ALIGN = 64
 RUN = 2
 WF_RUN = 8
-SCALAR_GAINS = 3
-SIG_BUFS = {"sig_a": 2, "sig_b": 3}
+SIG_BUFS = (2, 3)
 H_BUFS = 3
-WARM_PASSES = (4, 2)
+WARM_BANK = 7
+WARM_FIRST, WARM_SECOND = 4, 2
 OUT_BUFS = 12
 
 
@@ -144,18 +143,19 @@ def tile_list_unit_vocoder_gate_kernel(
 
         wg_bf = {}
 
-        def round_wg(b, a, t0):
+        def rounded(b, a):
             if (b, a) not in wg_bf:
                 wg_bf[b, a] = kept([P, PACK * KP], BF16, f"wg_bf{b}{a}")
-            dst = wg_bf[b, a][:].rearrange("p (t m j) -> p m j t", t=PACK, j=PACK)[:, :, :, t0 : t0 + 2]
-            src = wg_raw[b, a, 0][:].rearrange("p j (m t) -> p m j t", t=PACK)[:, :, :, t0 : t0 + 2]
-            nc.vector.tensor_copy(dst, src)
+            return wg_bf[b, a][:].rearrange("p (t m j) -> p m j t", t=PACK, j=PACK)
 
-        def round_wg_half(b, a, u):
-            if (b, a) not in wg_bf:
-                wg_bf[b, a] = kept([P, PACK * KP], BF16, f"wg_bf{b}{a}")
-            dst = wg_bf[b, a][:].rearrange("p (t m j) -> p m j t", t=PACK, j=PACK)[:, u * P // 2 : (u + 1) * P // 2]
-            nc.vector.tensor_copy(dst, wg_raw[b, a, u * KP // 2][:].rearrange("p j (m t) -> p m j t", t=PACK))
+        def loaded(b, a, c0):
+            return wg_raw[b, a, c0][:].rearrange("p j (m t) -> p m j t", t=PACK)
+
+        def round_tiles(b, a, t0):
+            nc.vector.tensor_copy(rounded(b, a)[:, :, :, t0 : t0 + 2], loaded(b, a, 0)[:, :, :, t0 : t0 + 2])
+
+        def round_columns(b, a, c0):
+            nc.vector.tensor_copy(rounded(b, a)[:, c0 // PACK : c0 // PACK + P // 2], loaded(b, a, c0))
 
         def quantise_wg(b, a, c0=0, w=KP):
             nc.vector.quantize_mx(
@@ -167,17 +167,20 @@ def tile_list_unit_vocoder_gate_kernel(
         tanh_f = {(b, s): kept([P, PACK, HALF], F32, f"tanh_f{b}{s}") for b in range(2) for s in range(2)}
         gained = {}
 
-        def apply_gain(b, s, t, tag="", on_scalar=False):
+        def gain_operands(b, s, t, tag=""):
             if (b, s) not in gained:
                 gained[b, s] = kept([P, PACK, HALF], F32, f"gained{b}{s}", tag)
-            if on_scalar:
-                nc.scalar.activation(gained[b, s][:, t, :], tanh_f[b, s][:, t, :], ACT.Copy, scale=gain_sb[b][:, t : t + 1])
-            else:
-                nc.vector.tensor_scalar(gained[b, s][:, t, :], tanh_f[b, s][:, t, :], gain_sb[b][:, t : t + 1], None, MULT)
+            return gained[b, s][:, t, :], tanh_f[b, s][:, t, :]
+
+        def gain_on_vector(b, s, t, gains, tag=""):
+            nc.vector.tensor_scalar(*gain_operands(b, s, t, tag), gains[:, t : t + 1], None, MULT)
+
+        def gain_on_scalar(b, s, t):
+            nc.scalar.activation(*gain_operands(b, s, t), ACT.Copy, scale=gain_sb[b][:, t : t + 1])
 
         def prepare_wg(b, a):
             for t0 in (0, 2):
-                round_wg(b, a, t0)
+                round_tiles(b, a, t0)
             for t0 in (0, 2):
                 quantise_wg(b, a, P * t0, 2 * P)
 
@@ -193,7 +196,7 @@ def tile_list_unit_vocoder_gate_kernel(
             )
 
         def warm_tensor(words, passes):
-            bank = bank_tile(BANKS - 1)
+            bank = bank_tile(WARM_BANK)
             for n in range(passes):
                 nc.tensor.matmul_mx(
                     out=bank[:],
@@ -231,9 +234,9 @@ def tile_list_unit_vocoder_gate_kernel(
                 stop=not start,
             )
 
-        def gate(b, c0, w, banks, ring):
+        def gate(b, c0, w, banks):
             per_bank = HALF // w
-            sig_g[b, c0] = work.tile([P, PACK, w], F32, name=f"sig{b}{c0}", tag=ring, bufs=SIG_BUFS[ring])
+            sig_g[b, c0] = work.tile([P, PACK, w], F32, name=f"sig{b}", bufs=SIG_BUFS[b])
             for t0 in range(0, PACK, per_bank):
                 bank = bank_tile(banks[t0 // per_bank])
                 for t in range(t0, t0 + per_bank):
@@ -246,14 +249,15 @@ def tile_list_unit_vocoder_gate_kernel(
         h_bf = {}
 
         def product(b, c0, w, tag=""):
-            g0 = max(c for (bb, c) in sig_g if bb == b and c <= c0)
+            g0 = max(c for (half, c) in sig_g if half == b and c <= c0)
             q0 = c0 - c0 % QUARTER
             if tag:
                 h_bf[b, q0] = kept([P, PACK * QUARTER], BF16, f"h_bf{b}{q0}", tag)
             elif (b, q0) not in h_bf:
                 h_bf[b, q0] = work.tile([P, PACK * QUARTER], BF16, name="h_bf", bufs=H_BUFS, align_bytes=ALIGN)
+            dst = h_bf[b, q0][:, PACK * (c0 - q0) : PACK * (c0 - q0 + w)]
             nc.vector.tensor_tensor(
-                h_bf[b, q0][:, PACK * (c0 - q0) : PACK * (c0 - q0 + w)].rearrange("p (c i t) -> p c t i", t=PACK, i=RUN),
+                dst.rearrange("p (c i t) -> p c t i", t=PACK, i=RUN),
                 gained[b, c0 // HALF][:, :, c0 % HALF : c0 % HALF + w].rearrange("p t (c i) -> p c t i", i=RUN),
                 sig_g[b, g0][:, :, c0 - g0 : c0 - g0 + w].rearrange("p t (c i) -> p c t i", i=RUN),
                 MULT,
@@ -268,6 +272,7 @@ def tile_list_unit_vocoder_gate_kernel(
             )
 
         out_tiles = range(N // P)
+        out_bank = {}
         out_sums = {}
 
         def out_pass(i, b, c0, w, start, stop):
@@ -281,32 +286,30 @@ def tile_list_unit_vocoder_gate_kernel(
                 stop=stop,
             )
 
-        def project_open(c0, w, banks):
+        def take_banks(c0, w, banks, i):
             per_bank = len(out_tiles) // len(banks)
-            for i in out_tiles:
-                if i % per_bank == 0:
-                    bank = bank_tile(banks[i // per_bank], per_bank * w)
-                out_sums[c0, i] = bank[:, (i % per_bank) * w : (i % per_bank + 1) * w]
-                out_pass(i, 0, c0, w, i % per_bank == 0, False)
+            if i % per_bank == 0:
+                out_bank[c0] = bank_tile(banks[i // per_bank], per_bank * w)
+            out_sums[c0, i] = out_bank[c0][:, (i % per_bank) * w : (i % per_bank + 1) * w]
+            return per_bank
 
-        def project(c0, w, banks):
-            per_bank = len(out_tiles) // len(banks)
+        def project_open(c0, w, banks):
             for i in out_tiles:
-                if i % per_bank == 0:
-                    bank = bank_tile(banks[i // per_bank], per_bank * w)
-                out_sums[c0, i] = bank[:, (i % per_bank) * w : (i % per_bank + 1) * w]
-                out_pass(i, 1, c0, w, True, False)
-                out_pass(i, 0, c0, w, False, True)
+                per_bank = take_banks(c0, w, banks, i)
+                out_pass(i, 0, c0, w, i % per_bank == 0, False)
 
         def project_close(c0, w, per_bank=2):
             for i in out_tiles:
                 out_pass(i, 1, c0, w, False, i % per_bank == per_bank - 1)
 
-        def store(c0, w, tiles, on_vector=False, tag=""):
-            if tag:
-                y = kept([P, len(out_tiles[tiles]), w], F32, f"y{c0}", tag)
-            else:
-                y = work.tile([P, len(out_tiles[tiles]), w], F32, name="y", bufs=OUT_BUFS)
+        def project_whole(c0, w, banks):
+            for i in out_tiles:
+                take_banks(c0, w, banks, i)
+                out_pass(i, 1, c0, w, True, False)
+                out_pass(i, 0, c0, w, False, True)
+
+        def store(c0, w, tiles, on_vector=False):
+            y = work.tile([P, len(out_tiles[tiles]), w], F32, name="y", bufs=OUT_BUFS)
             for n, i in enumerate(out_tiles[tiles]):
                 if on_vector:
                     nc.vector.tensor_scalar(y[:, n, :], out_sums[c0, i], bo_sb[:, i : i + 1], None, ADD)
@@ -318,6 +321,9 @@ def tile_list_unit_vocoder_gate_kernel(
 
         gather_scales()
         load_wg(0, 0, 0, KP // 2, tag="tab_sc")
+        gain_first = kept([P, 1], F32, "gain_first")
+        with nc.allow_non_contiguous_dma(reason="one gain value a partition"):
+            nc.sync.dma_start(gain_first[:], gain[0:KP].rearrange("(p t) -> p t", t=PACK)[:, 0:1])
         load_wg(0, 0, KP // 2, KP // 2)
         load_wf(1)
         load_gain(0)
@@ -335,62 +341,67 @@ def tile_list_unit_vocoder_gate_kernel(
         reorder_wf_scales(0)
         gather_words(0, 0)
         reorder_wf(0)
-        warm_tensor(tab[0][:, 0:HALF], WARM_PASSES[0])
+        warm_tensor(tab[0][:, 0:HALF], WARM_FIRST)
         reorder_wf_scales(1)
         gather_words(0, 1)
-        warm_tensor(v_w[0, 1][:], WARM_PASSES[1])
+        warm_tensor(v_w[0, 1][:], WARM_SECOND)
         gather_words(1, 0)
         filter_first()
         gather_words(1, 1)
         for t in range(PACK):
             filter_tile(0, 1, t)
 
-        round_wg_half(0, 0, 0)
-        round_wg_half(0, 0, 1)
+        round_columns(0, 0, 0)
+        gain_on_vector(0, 0, 0, gain_first)
+        round_columns(0, 0, KP // 2)
         reorder_wf(1)
         quantise_wg(0, 0)
+        for t in range(1, PACK):
+            gain_on_vector(0, 0, t, gain_sb[0])
         for t in range(PACK):
-            apply_gain(0, 0, t, "wg_raw00256")
-        for t in range(PACK):
-            apply_gain(0, 1, t)
+            gain_on_vector(0, 1, t, gain_sb[0])
         prepare_wg(0, 1)
-        for t in range(PACK):
+        filter_tile(1, 0, 0)
+        gain_on_vector(1, 0, 0, gain_sb[1])
+        for t in (1, 2):
             filter_tile(1, 0, t)
-            if t < PACK - 1:
-                apply_gain(1, 0, t, on_scalar=t > 0)
+            gain_on_scalar(1, 0, t)
+        filter_tile(1, 0, 3)
         prepare_wg(1, 0)
         for t in range(PACK):
             filter_tile(1, 1, t)
         prepare_wg(1, 1)
         for t in range(PACK):
-            apply_gain(1, 1, t, "wg_raw110")
+            gain_on_vector(1, 1, t, gain_sb[1], "wg_raw110")
 
-        gate(0, 0, QUARTER, (0, 1), "sig_a")
-        gate(0, QUARTER, QUARTER, (2, 3), "sig_a")
-        apply_gain(1, 0, PACK - 1, on_scalar=True)
-        gate(1, 0, QUARTER, (6, 7), "sig_b")
-        gate(1, QUARTER, QUARTER, (0, 1), "sig_b")
+        gate(0, 0, QUARTER, (0, 1))
+        gate(0, QUARTER, QUARTER, (2, 3))
+        gain_on_scalar(1, 0, 3)
+        gate(1, 0, QUARTER, (6, 7))
+        gate(1, QUARTER, QUARTER, (0, 1))
         product(0, 0, QUARTER, tag="wg_bf11")
         product(0, QUARTER, QUARTER)
         quantise_h(0, 0, QUARTER)
-        gate(0, 2 * QUARTER, QUARTER, (4, 5), "sig_a")
-        gate(1, 2 * QUARTER, QUARTER, (2, 3), "sig_b")
+        gate(0, 2 * QUARTER, QUARTER, (4, 5))
+        gate(1, 2 * QUARTER, QUARTER, (2, 3))
         product(1, 0, QUARTER)
         quantise_h(0, QUARTER, QUARTER)
         project_open(0, QUARTER, (0, 1))
         quantise_h(1, 0, QUARTER)
         project_close(0, QUARTER)
         product(1, QUARTER, QUARTER)
-        gate(0, 3 * QUARTER, QUARTER, (6, 7), "sig_a")
+        gate(0, 3 * QUARTER, QUARTER, (6, 7))
         store(0, QUARTER, low)
         store(0, QUARTER, high)
+
         product(0, 2 * QUARTER, QUARTER)
         quantise_h(1, QUARTER, QUARTER)
-        project(QUARTER, QUARTER, (2, 3))
+        project_whole(QUARTER, QUARTER, (2, 3))
         store(QUARTER, QUARTER, low)
-        gate(1, 6 * EIGHTH, EIGHTH, (4,), "sig_b")
+        gate(1, 6 * EIGHTH, EIGHTH, (4,))
         store(QUARTER, QUARTER, high)
-        gate(1, 7 * EIGHTH, EIGHTH, (6,), "sig_b")
+        gate(1, 7 * EIGHTH, EIGHTH, (6,))
+
         product(1, 2 * QUARTER, QUARTER)
         quantise_h(0, 2 * QUARTER, QUARTER)
         project_open(2 * QUARTER, QUARTER, (5, 7))
@@ -398,17 +409,21 @@ def tile_list_unit_vocoder_gate_kernel(
         project_close(2 * QUARTER, QUARTER)
         for i in out_tiles:
             store(2 * QUARTER, QUARTER, slice(i, i + 1))
-        product(0, 3 * QUARTER, QUARTER)
-        product(1, 6 * EIGHTH, EIGHTH, tag="h_last")
-        quantise_h(0, 3 * QUARTER, QUARTER)
+
+        product(0, 6 * EIGHTH, EIGHTH)
+        product(1, 6 * EIGHTH, EIGHTH)
+        quantise_h(0, 6 * EIGHTH, EIGHTH)
         project_open(6 * EIGHTH, EIGHTH, (0, 1))
         quantise_h(1, 6 * EIGHTH, EIGHTH)
         project_close(6 * EIGHTH, EIGHTH)
-        project_open(7 * EIGHTH, EIGHTH, (2, 3, 4, 6))
         store(6 * EIGHTH, EIGHTH, low)
+        store(6 * EIGHTH, EIGHTH, high)
+
+        product(0, 7 * EIGHTH, EIGHTH)
         product(1, 7 * EIGHTH, EIGHTH)
+        quantise_h(0, 7 * EIGHTH, EIGHTH)
+        project_open(7 * EIGHTH, EIGHTH, (2, 3, 4, 6))
         quantise_h(1, 7 * EIGHTH, EIGHTH)
-        project_close(7 * EIGHTH, EIGHTH, 1)
-        store(6 * EIGHTH, EIGHTH, high, True, "h_last")
+        project_close(7 * EIGHTH, EIGHTH, per_bank=1)
         store(7 * EIGHTH, EIGHTH, even)
-        store(7 * EIGHTH, EIGHTH, odd, True)
+        store(7 * EIGHTH, EIGHTH, odd, on_vector=True)

@@ -344,7 +344,7 @@ def tile_list_unit_vocoder_gate_kernel(
         warm_tensor(tab[0][:, 0:HALF], WARM_FIRST)
         reorder_wf_scales(1)
         gather_words(0, 1)
-        warm_tensor(v_w[0, 1][:], WARM_SECOND)
+        warm_tensor(tab[1][:, 0:HALF], WARM_SECOND)
         gather_words(1, 0)
         filter_first()
         gather_words(1, 1)

from contextlib import ExitStack

import concourse.mybir as mybir

K, H, N, T, S = 1024, 1024, 512, 2048, 1024
FLOPS = 2 * S * (2 * K * H + H * N)

F32 = mybir.dt.float32
BF16 = mybir.dt.bfloat16
I32 = mybir.dt.int32
U32 = mybir.dt.uint32
U16 = mybir.dt.uint16
U8 = mybir.dt.uint8
FP8X4 = mybir.dt.float8_e4m3fn_x4
FP4X4 = mybir.dt.float4_e2m1fn_x4
ACT = mybir.ActivationFunctionType
MULT = mybir.AluOpType.mult
ADD = mybir.AluOpType.add

P = 128
PACK = 4
KP = P * PACK
HALF = S // 2
QUARTER = S // 4
EIGHTH = S // 8
GROUP = 32
ROWS = 4
WORD = 4
LIST_ROWS = 16
ALIGN = 64
RUN = 2
WF_RUN = 8
SIG_BUFS = (2, 3)
H_BUFS = 3
WARM_BANK = 7
WARM_FIRST, WARM_SECOND = 4, 2
OUT_BUFS = 12


def tile_list_unit_vocoder_gate_kernel(
    tc, tab_words, tab_scales, offs, wf_words, wf_scales, wg, gain, wo_words, wo_scales, bo, out
):
    nc = tc.nc
    with ExitStack() as ctx:
        keep = ctx.enter_context(tc.tile_pool(name="keep", bufs=1))
        work = ctx.enter_context(tc.tile_pool(name="work", bufs=2))
        psum = ctx.enter_context(tc.psum_pool(name="psum", bufs=1))

        def kept(shape, dtype, name, tag=""):
            return keep.tile(shape, dtype, name=name, tag=tag or name, align_bytes=ALIGN)

        def bank_tile(n, w=HALF):
            return psum.tile([P, w], F32, name=f"bank{n}")

        offsets = keep.tile([P, S // LIST_ROWS], U16, name="offsets")
        nc.sync.dma_start(offsets[:], offs)

        tab_sc = kept([P, T // WORD], I32, "tab_sc")
        nc.sync.dma_start(tab_sc[0:GROUP, :], tab_scales.bitcast(I32).rearrange("a q c -> q a c"))
        wf_sc_raw = kept([P, 2, H // WORD], I32, "wf_sc_raw")
        nc.vector.memset(wf_sc_raw[:], 0)
        nc.vector.memset(tab_sc[GROUP : 2 * GROUP, :], 0)
        nc.vector.memset(tab_sc[2 * GROUP : P, :], 0)
        v_planes = kept([P, 2, S // WORD], I32, "v_planes")
        nc.gpsimd.memset(v_planes[:], 0)

        wo_sc = kept([P, 2, N // WORD], I32, "wo_sc")
        warm = kept([P, 1], F32, "warm")
        warm_out = kept([P, 1], F32, "warm_out")
        nc.gpsimd.memset(warm[:], 0.0)
        nc.gpsimd.memset(wo_sc[:], 0)

        tab = [kept([P, T], I32, f"tab{a}") for a in range(2)]
        wf_raw = {}
        wg_raw = {}

        def load_tab(a):
            nc.sync.dma_start(tab[a][:], tab_words[a].rearrange("p n i -> p (n i)").bitcast(I32))

        def load_wf(b):
            wf_raw[b] = kept([P, 2, KP // 2], I32, f"wf_raw{b}")
            src = wf_words.bitcast(I32).rearrange("a p c -> p a c")
            nc.sync.dma_start(wf_raw[b][:], src[:, :, b * (KP // 2) : (b + 1) * (KP // 2)])

        def load_wg(b, a, c0=0, w=KP, tag=""):
            wg_raw[b, a, c0] = kept([P, PACK, w], F32, f"wg_raw{b}{a}{c0}", tag)
            src = wg[a * KP : (a + 1) * KP, b * KP + c0 : b * KP + c0 + w]
            nc.sync.dma_start(wg_raw[b, a, c0][:], src.rearrange("(p j) c -> p j c", j=PACK))

        gain_sb = {}

        def load_gain(b):
            gain_sb[b] = kept([P, PACK], F32, f"gain_sb{b}")
            nc.sync.dma_start(gain_sb[b][:], gain[b * KP : (b + 1) * KP].rearrange("(p t) -> p t", t=PACK))

        def load_planes(planes, scales):
            for r in range(ROWS):
                src = scales.bitcast(I32)[:, r : ROWS * ROWS : ROWS, :].rearrange("a q c -> q a c")
                nc.sync.dma_start(planes[r:P:GROUP, :, :], src)

        load_wf(0)
        load_tab(0)
        load_planes(wf_sc_raw, wf_scales)
        nc.scalar.activation(warm_out[:], warm[:], ACT.Sigmoid)
        load_tab(1)

        v_w = {}
        v_sc = kept([P, S], U8, "v_sc")
        wf_w = [kept([P, 2, 2 * KP], U8, f"wf_w{b}") for b in range(2)]
        wf_sc = {}
        wg_w = {(b, a): kept([P, KP], U32, f"wg_w{b}{a}") for b in range(2) for a in range(2)}
        wg_sc = {(b, a): kept([P, KP], U8, f"wg_sc{b}{a}") for b in range(2) for a in range(2)}
        h_w = [kept([P, S], U32, f"h_w{b}") for b in range(2)]
        h_sc = [kept([P, S], U8, f"h_sc{b}") for b in range(2)]

        def gather_words(a, s):
            v_w[a, s] = kept([P, HALF], U32, f"v_w{a}{s}")
            cols = slice(s * HALF // LIST_ROWS, (s + 1) * HALF // LIST_ROWS)
            nc.vector.tensor_copy(v_w[a, s][:], tab[a][:].bitcast(U32).indirect(offsets[:, cols]))

        def gather_scales():
            nc.vector.tensor_copy(v_sc[:], tab_sc[:].bitcast(U8).indirect(offsets[:]))
            for g in (0, 2, 1, 3):
                flat = v_sc[:].bitcast(I32)[2 * ROWS * g : 2 * ROWS * (g + 1), :]
                nc.sync.dma_start(v_planes[GROUP * g : GROUP * g + ROWS, :, :], flat)

        def v_plane(a, c0, w):
            return v_planes[:, a, :].bitcast(U8)[:, c0 : c0 + w]

        def reorder_wf(b):
            nc.vector.tensor_copy(
                wf_w[b][:].bitcast(U16).rearrange("p a (t m i) -> p a m t i", t=PACK, i=WF_RUN),
                wf_raw[b][:].bitcast(U16).rearrange("p a (m i t) -> p a m t i", t=PACK, i=WF_RUN),
            )

        def reorder_wf_scales(b):
            wf_sc[b] = kept([P, 2, KP], U8, f"wf_sc{b}")
            src = wf_sc_raw[:].bitcast(U8)[:, :, b * KP : (b + 1) * KP]
            nc.gpsimd.tensor_copy(
                wf_sc[b][:].rearrange("p a (t m) -> p a t m", t=PACK),
                src.rearrange("p a (m t) -> p a t m", t=PACK),
            )

        wg_bf = {}

        def rounded(b, a):
            if (b, a) not in wg_bf:
                wg_bf[b, a] = kept([P, PACK * KP], BF16, f"wg_bf{b}{a}")
            return wg_bf[b, a][:].rearrange("p (t m j) -> p m j t", t=PACK, j=PACK)

        def loaded(b, a, c0):
            return wg_raw[b, a, c0][:].rearrange("p j (m t) -> p m j t", t=PACK)

        def round_tiles(b, a, t0):
            nc.vector.tensor_copy(rounded(b, a)[:, :, :, t0 : t0 + 2], loaded(b, a, 0)[:, :, :, t0 : t0 + 2])

        def round_columns(b, a, c0):
            nc.vector.tensor_copy(rounded(b, a)[:, c0 // PACK : c0 // PACK + P // 2], loaded(b, a, c0))

        def quantise_wg(b, a, c0=0, w=KP):
            nc.vector.quantize_mx(
                out=wg_w[b, a][:, c0 : c0 + w].bitcast(FP8X4),
                scales=wg_sc[b, a][:, c0 : c0 + w],
                in_=wg_bf[b, a][:, PACK * c0 : PACK * (c0 + w)],
            )

        tanh_f = {(b, s): kept([P, PACK, HALF], F32, f"tanh_f{b}{s}") for b in range(2) for s in range(2)}
        gained = {}

        def gain_operands(b, s, t, tag=""):
            if (b, s) not in gained:
                gained[b, s] = kept([P, PACK, HALF], F32, f"gained{b}{s}", tag)
            return gained[b, s][:, t, :], tanh_f[b, s][:, t, :]

        def gain_on_vector(b, s, t, gains, tag=""):
            nc.vector.tensor_scalar(*gain_operands(b, s, t, tag), gains[:, t : t + 1], None, MULT)

        def gain_on_scalar(b, s, t):
            nc.scalar.activation(*gain_operands(b, s, t), ACT.Copy, scale=gain_sb[b][:, t : t + 1])

        def prepare_wg(b, a):
            for t0 in (0, 2):
                round_tiles(b, a, t0)
            for t0 in (0, 2):
                quantise_wg(b, a, P * t0, 2 * P)

        def filter_pass(bank, b, s, t, a, start):
            nc.tensor.matmul_mx(
                out=bank[:],
                lhsT=wf_w[b][:, a, 2 * P * t : 2 * P * (t + 1)].bitcast(FP4X4),
                lhsT_scale=wf_sc[b][:, a, P * t : P * (t + 1)],
                rhs=v_w[a, s][:].bitcast(FP8X4),
                rhs_scale=v_plane(a, s * HALF, HALF),
                start=start,
                stop=not start,
            )

        def warm_tensor(words, passes):
            bank = bank_tile(WARM_BANK)
            for n in range(passes):
                nc.tensor.matmul_mx(
                    out=bank[:],
                    lhsT=wf_raw[0][:, 0, :].bitcast(U8)[:, 0 : 2 * P].bitcast(FP4X4),
                    lhsT_scale=wf_sc_raw[:, 0, :].bitcast(U8)[:, 0:P],
                    rhs=words.bitcast(FP8X4),
                    rhs_scale=wf_sc_raw[:, 0, :].bitcast(U8)[:, 0:HALF],
                    start=True,
                    stop=True,
                )

        def filter_first():
            banks = [bank_tile(t) for t in range(PACK)]
            for a, t in ((0, 0), (0, 1), (1, 0), (1, 1), (0, 2), (1, 2), (0, 3), (1, 3)):
                filter_pass(banks[t], 0, 0, t, a, a == 0)
                if a == 1:
                    nc.scalar.activation(tanh_f[0, 0][:, t, :], banks[t][:], ACT.Tanh)

        def filter_tile(b, s, t):
            bank = bank_tile(PACK * s + t)
            for a in (1, 0):
                filter_pass(bank, b, s, t, a, a == 1)
            nc.scalar.activation(tanh_f[b, s][:, t, :], bank[:], ACT.Tanh)

        sig_g = {}

        def gate_pass(dst, b, t, a, c0, w, start):
            nc.tensor.matmul_mx(
                out=dst,
                lhsT=wg_w[b, a][:, P * t : P * (t + 1)].bitcast(FP8X4),
                lhsT_scale=wg_sc[b, a][:, P * t : P * (t + 1)],
                rhs=v_w[a, c0 // HALF][:, c0 % HALF : c0 % HALF + w].bitcast(FP8X4),
                rhs_scale=v_plane(a, c0, w),
                start=start,
                stop=not start,
            )

        def gate(b, c0, w, banks):
            per_bank = HALF // w
            sig_g[b, c0] = work.tile([P, PACK, w], F32, name=f"sig{b}", bufs=SIG_BUFS[b])
            for t0 in range(0, PACK, per_bank):
                bank = bank_tile(banks[t0 // per_bank])
                for t in range(t0, t0 + per_bank):
                    dst = bank[:, (t - t0) * w : (t - t0 + 1) * w]
                    gate_pass(dst, b, t, 1, c0, w, True)
                    gate_pass(dst, b, t, 0, c0, w, False)
                dst_sig = sig_g[b, c0][:, t0 : t0 + per_bank, :].rearrange("p t c -> p (t c)")
                nc.scalar.activation(dst_sig, bank[:], ACT.Sigmoid)

        h_bf = {}

        def product(b, c0, w, tag=""):
            g0 = max(c for (half, c) in sig_g if half == b and c <= c0)
            q0 = c0 - c0 % QUARTER
            if tag:
                h_bf[b, q0] = kept([P, PACK * QUARTER], BF16, f"h_bf{b}{q0}", tag)
            elif (b, q0) not in h_bf:
                h_bf[b, q0] = work.tile([P, PACK * QUARTER], BF16, name="h_bf", bufs=H_BUFS, align_bytes=ALIGN)
            dst = h_bf[b, q0][:, PACK * (c0 - q0) : PACK * (c0 - q0 + w)]
            nc.vector.tensor_tensor(
                dst.rearrange("p (c i t) -> p c t i", t=PACK, i=RUN),
                gained[b, c0 // HALF][:, :, c0 % HALF : c0 % HALF + w].rearrange("p t (c i) -> p c t i", i=RUN),
                sig_g[b, g0][:, :, c0 - g0 : c0 - g0 + w].rearrange("p t (c i) -> p c t i", i=RUN),
                MULT,
            )

        def quantise_h(b, c0, w):
            q0 = c0 - c0 % QUARTER
            nc.vector.quantize_mx(
                out=h_w[b][:, c0 : c0 + w].bitcast(FP8X4),
                scales=h_sc[b][:, c0 : c0 + w],
                in_=h_bf[b, q0][:, PACK * (c0 - q0) : PACK * (c0 - q0 + w)],
            )

        out_tiles = range(N // P)
        out_bank = {}
        out_sums = {}

        def out_pass(i, b, c0, w, start, stop):
            nc.tensor.matmul_mx(
                out=out_sums[c0, i],
                lhsT=wo_w[:, b, P * i : P * (i + 1)].bitcast(FP8X4),
                lhsT_scale=wo_sc[:, b, :].bitcast(U8)[:, P * i : P * (i + 1)],
                rhs=h_w[b][:, c0 : c0 + w].bitcast(FP8X4),
                rhs_scale=h_sc[b][:, c0 : c0 + w],
                start=start,
                stop=stop,
            )

        def take_banks(c0, w, banks, i):
            per_bank = len(out_tiles) // len(banks)
            if i % per_bank == 0:
                out_bank[c0] = bank_tile(banks[i // per_bank], per_bank * w)
            out_sums[c0, i] = out_bank[c0][:, (i % per_bank) * w : (i % per_bank + 1) * w]
            return per_bank

        def project_open(c0, w, banks):
            for i in out_tiles:
                per_bank = take_banks(c0, w, banks, i)
                out_pass(i, 0, c0, w, i % per_bank == 0, False)

        def project_close(c0, w, per_bank=2):
            for i in out_tiles:
                out_pass(i, 1, c0, w, False, i % per_bank == per_bank - 1)

        def project_whole(c0, w, banks):
            for i in out_tiles:
                take_banks(c0, w, banks, i)
                out_pass(i, 1, c0, w, True, False)
                out_pass(i, 0, c0, w, False, True)

        def store(c0, w, tiles, on_vector=False):
            y = work.tile([P, len(out_tiles[tiles]), w], F32, name="y", bufs=OUT_BUFS)
            for n, i in enumerate(out_tiles[tiles]):
                if on_vector:
                    nc.vector.tensor_scalar(y[:, n, :], out_sums[c0, i], bo_sb[:, i : i + 1], None, ADD)
                else:
                    nc.scalar.activation(y[:, n, :], out_sums[c0, i], ACT.Identity, bias=bo_sb[:, i : i + 1])
            nc.sync.dma_start(out[:, c0 : c0 + w].rearrange("(i p) c -> p i c", p=P)[:, tiles, :], y[:])

        low, high, even, odd = slice(0, 2), slice(2, 4), slice(0, 4, 2), slice(1, 4, 2)

        gather_scales()
        load_wg(0, 0, 0, KP // 2, tag="tab_sc")
        gain_first = kept([P, 1], F32, "gain_first")
        with nc.allow_non_contiguous_dma(reason="one gain value a partition"):
            nc.sync.dma_start(gain_first[:], gain[0:KP].rearrange("(p t) -> p t", t=PACK)[:, 0:1])
        load_wg(0, 0, KP // 2, KP // 2)
        load_wf(1)
        load_gain(0)
        load_wg(0, 1)
        load_gain(1)
        load_wg(1, 0)
        load_wg(1, 1)
        wo_w = kept([P, 2, N], I32, "wo_w")
        nc.sync.dma_start(wo_w[:], wo_words.rearrange("a p n i -> p a (n i)").bitcast(I32))
        load_planes(wo_sc, wo_scales)
        bo_sb = kept([P, N // P], F32, "bo_sb")
        with nc.allow_non_contiguous_dma(reason="one bias value a partition"):
            nc.sync.dma_start(bo_sb[:], bo.rearrange("(i p) -> p i", p=P))

        reorder_wf_scales(0)
        gather_words(0, 0)
        reorder_wf(0)
        warm_tensor(tab[0][:, 0:HALF], WARM_FIRST)
        reorder_wf_scales(1)
        gather_words(0, 1)
        warm_tensor(tab[1][:, 0:HALF], WARM_SECOND)
        gather_words(1, 0)
        filter_first()
        gather_words(1, 1)
        for t in range(PACK):
            filter_tile(0, 1, t)

        round_columns(0, 0, 0)
        gain_on_vector(0, 0, 0, gain_first)
        round_columns(0, 0, KP // 2)
        reorder_wf(1)
        quantise_wg(0, 0)
        for t in range(1, PACK):
            gain_on_vector(0, 0, t, gain_sb[0])
        for t in range(PACK):
            gain_on_vector(0, 1, t, gain_sb[0])
        prepare_wg(0, 1)
        filter_tile(1, 0, 0)
        gain_on_vector(1, 0, 0, gain_sb[1])
        for t in (1, 2):
            filter_tile(1, 0, t)
            gain_on_scalar(1, 0, t)
        filter_tile(1, 0, 3)
        prepare_wg(1, 0)
        for t in range(PACK):
            filter_tile(1, 1, t)
        prepare_wg(1, 1)
        for t in range(PACK):
            gain_on_vector(1, 1, t, gain_sb[1], "wg_raw110")

        gate(0, 0, QUARTER, (0, 1))
        gate(0, QUARTER, QUARTER, (2, 3))
        gain_on_scalar(1, 0, 3)
        gate(1, 0, QUARTER, (6, 7))
        gate(1, QUARTER, QUARTER, (0, 1))
        product(0, 0, QUARTER, tag="wg_bf11")
        product(0, QUARTER, QUARTER)
        quantise_h(0, 0, QUARTER)
        gate(0, 2 * QUARTER, QUARTER, (4, 5))
        gate(1, 2 * QUARTER, QUARTER, (2, 3))
        product(1, 0, QUARTER)
        quantise_h(0, QUARTER, QUARTER)
        project_open(0, QUARTER, (0, 1))
        quantise_h(1, 0, QUARTER)
        project_close(0, QUARTER)
        product(1, QUARTER, QUARTER)
        gate(0, 3 * QUARTER, QUARTER, (6, 7))
        store(0, QUARTER, low)
        store(0, QUARTER, high)

        product(0, 2 * QUARTER, QUARTER)
        quantise_h(1, QUARTER, QUARTER)
        project_whole(QUARTER, QUARTER, (2, 3))
        store(QUARTER, QUARTER, low)
        gate(1, 6 * EIGHTH, EIGHTH, (4,))
        store(QUARTER, QUARTER, high)
        gate(1, 7 * EIGHTH, EIGHTH, (6,))

        product(1, 2 * QUARTER, QUARTER)
        quantise_h(0, 2 * QUARTER, QUARTER)
        project_open(2 * QUARTER, QUARTER, (5, 7))
        quantise_h(1, 2 * QUARTER, QUARTER)
        project_close(2 * QUARTER, QUARTER)
        for i in out_tiles:
            store(2 * QUARTER, QUARTER, slice(i, i + 1))

        product(0, 6 * EIGHTH, EIGHTH)
        product(1, 6 * EIGHTH, EIGHTH)
        quantise_h(0, 6 * EIGHTH, EIGHTH)
        project_open(6 * EIGHTH, EIGHTH, (0, 1))
        quantise_h(1, 6 * EIGHTH, EIGHTH)
        project_close(6 * EIGHTH, EIGHTH)
        store(6 * EIGHTH, EIGHTH, low)
        store(6 * EIGHTH, EIGHTH, high)

        product(0, 7 * EIGHTH, EIGHTH)
        product(1, 7 * EIGHTH, EIGHTH)
        quantise_h(0, 7 * EIGHTH, EIGHTH)
        project_open(7 * EIGHTH, EIGHTH, (2, 3, 4, 6))
        quantise_h(1, 7 * EIGHTH, EIGHTH)
        project_close(7 * EIGHTH, EIGHTH, per_bank=1)
        store(7 * EIGHTH, EIGHTH, even)
        store(7 * EIGHTH, EIGHTH, odd, on_vector=True)
